import numpy as np
import ml_dtypes


def mxq(x, axis, fmt="e4m3"):
    dtype, down = {"e4m3": (ml_dtypes.float8_e4m3fn, 7), "e5m2": (ml_dtypes.float8_e5m2, 14)}[fmt]
    v = np.moveaxis(np.asarray(x, np.float32).astype(ml_dtypes.bfloat16).astype(np.float64), axis, -1)
    blocks = v.reshape(v.shape[:-1] + (-1, 32))
    amax = np.abs(blocks).max(-1, keepdims=True)
    byte = np.maximum(np.where(amax > 0, np.frexp(amax)[1] - 1 + 127, 0) - down, 1)
    scale = np.exp2(byte - 127.0)
    codes = (blocks / scale).astype(np.float32).astype(dtype).astype(np.float64)
    return np.moveaxis((codes * scale).reshape(v.shape), -1, axis)


WIDE = False


def mx_kscale(k):
    if not WIDE:
        return np.ones(k)
    levels = np.array([10, -10, 5, -5, 0])
    if k % 512:
        return np.exp2(np.random.permutation(np.resize(levels, k // 32))).repeat(32)
    a = np.empty((k // 512, 16))
    for p in range(k // 512):
        a[p, :8] = np.random.permutation(np.resize(levels, 8))
        for g in range(8):
            far = levels[np.abs(levels - a[p, g]) >= 10]
            a[p, g + 8] = far[np.random.randint(len(far))]
    return np.exp2(a.ravel()).repeat(32)


def f64(x):
    return np.asarray(x).astype(np.float64)


def striped(idx):
    return np.tile(idx.reshape(-1, 16).T, (8, 1)).astype(np.uint16)


def unstriped(offs):
    return offs[:16].T.reshape(-1).astype(np.int64)


E2M1 = np.array([0.0, 0.5, 1.0, 1.5, 2.0, 3.0, 4.0, 6.0, -0.0, -0.5, -1.0, -1.5, -2.0, -3.0, -4.0, -6.0])


def pack_weight(w, fmt):
    k, n = w.shape
    w = f64(np.asarray(w, np.float32).astype(ml_dtypes.bfloat16)).reshape(k // 32, 32, n)
    amax = np.abs(w).max(1)
    if fmt == "e4m3":
        byte = np.frexp(amax)[1] - 1 + 127 - 7
    else:
        mant, ex = np.frexp(amax / 6.0)
        byte = np.where(mant > 0.5, ex, ex - 1) + 127
    byte = np.clip(np.where(amax > 0, byte, 1), 1, 254)
    scaled = (w * np.exp2(127.0 - byte)[:, None, :]).reshape(k, n).astype(np.float32)
    by_word = np.ascontiguousarray(scaled.reshape(k // 512, 128, 4, n).transpose(0, 1, 3, 2))
    if fmt == "e4m3":
        words = by_word.astype(ml_dtypes.float8_e4m3fn).view(np.uint8)
    else:
        c = by_word.astype(ml_dtypes.float4_e2m1fn).view(np.uint8) & 0xF
        words = (c[..., 0::2] | (c[..., 1::2] << 4)).reshape(k // 512, 128, 2 * n)
    return np.ascontiguousarray(words), np.ascontiguousarray(byte.astype(np.uint8).reshape(k // 512, 16, n))


def unpack_weight(words, scales, fmt):
    g, _, n = scales.shape
    words = np.ascontiguousarray(words).reshape(g, 128, n, -1)
    if fmt == "e4m3":
        vals = words.view(ml_dtypes.float8_e4m3fn).astype(np.float64)
    else:
        nib = np.empty((g, 128, n, 4), np.uint8)
        nib[..., 0::2] = words & 0xF
        nib[..., 1::2] = words >> 4
        vals = E2M1[nib]
    vals = vals * np.repeat(np.exp2(scales.astype(np.float64) - 127.0), 8, axis=1)[..., None]
    return vals.transpose(0, 1, 3, 2).reshape(g * 512, n)


def gelu(v):
    return 0.5 * v * (1.0 + np.tanh(np.sqrt(2.0 / np.pi) * (v + 0.044715 * v**3)))


K, T, S, H, P, N, P2 = 1024, 2048, 1024, 1024, 512, 768, 256

def setup_inputs():
    n = np.random.standard_normal
    s = mx_kscale(K)[:, None]
    u = mx_kscale(H)[:, None]
    tab_words, tab_scales = pack_weight(n((K, T)) * s, "e4m3")
    w1 = n((K, H)) / np.sqrt(K) / s * u.T
    wc_words, wc_scales = pack_weight(n((H, N)) / np.sqrt(H) / u, "e2m1")
    wf_words, wf_scales = pack_weight(n((H, N)) / np.sqrt(H) / u, "e4m3")
    leaves = np.random.permutation(S)
    phrases = np.random.permutation(P)
    return {
        "tab_words": tab_words, "tab_scales": tab_scales,
        "offs": striped(np.random.permutation(T)[:S]),
        "w1": w1.astype(np.float32),
        "pos1": striped(leaves[:P]), "pos2": striped(leaves[P:]),
        "wc_words": wc_words, "wc_scales": wc_scales,
        "wf_words": wf_words, "wf_scales": wf_scales,
        "mem": n((N, P)).astype(np.float32),
        "pos3": striped(phrases[:P2]), "pos4": striped(phrases[P2:]),
    }

def reference(tab_words, tab_scales, offs, w1, pos1, pos2, wc_words, wc_scales,
              wf_words, wf_scales, mem, pos3, pos4):
    v = unpack_weight(tab_words, tab_scales, "e4m3")[:, unstriped(offs)]
    h = mxq(f64(w1), 0, "e4m3").T @ v
    z = h[:, unstriped(pos1)] + h[:, unstriped(pos2)]
    zq = mxq(z, 0, "e4m3")
    wc = unpack_weight(wc_words, wc_scales, "e2m1")
    wf = unpack_weight(wf_words, wf_scales, "e4m3")
    content = np.tanh(wc.T @ zq)
    forget = 1.0 / (1.0 + np.exp(-(wf.T @ zq)))
    y = content + forget * f64(mem)
    return y[:, unstriped(pos3)] - y[:, unstriped(pos4)]

@@ -1,0 +1,336 @@
+from contextlib import ExitStack
+
+import concourse.mybir as mybir
+from concourse.masks import make_identity
+
+K, T, S, H, PH, N, CL = 1024, 2048, 1024, 1024, 512, 768, 256
+FLOPS = 2 * K * H * S + 2 * 2 * H * N * PH
+
+F32 = mybir.dt.float32
+BF16 = mybir.dt.bfloat16
+I32 = mybir.dt.int32
+U32 = mybir.dt.uint32
+U16 = mybir.dt.uint16
+U8 = mybir.dt.uint8
+FP8X4 = mybir.dt.float8_e4m3fn_x4
+FP4X4 = mybir.dt.float4_e2m1fn_x4
+ACT = mybir.ActivationFunctionType
+ALU = mybir.AluOpType
+
+P = 128
+BANK = 512
+PASSES = 2
+ROW_TILES = H // P
+OUT_TILES = N // P
+W1_LOADS = (128, 128, 256, 256, 256)
+EARLY = 384
+LATE = PH - EARLY
+RING = 4
+VECTOR_CASTS = (2, 5)
+
+
+def tile_list_phrase_tree_forget_kernel(
+    tc, tab_words, tab_scales, offs, w1, pos1, pos2, wc_words, wc_scales,
+    wf_words, wf_scales, mem, pos3, pos4, out,
+):
+    nc = tc.nc
+    with ExitStack() as ctx:
+        keep = ctx.enter_context(tc.tile_pool(name="keep", bufs=1))
+        psum = ctx.enter_context(tc.psum_pool(name="psum", bufs=1))
+
+        def sb(name, shape, dtype):
+            return keep.tile(shape, dtype, name=name, align_bytes=64)
+
+        banks = [psum.tile([P, BANK], F32, name="bank%d" % b) for b in range(8)]
+
+        offs_sb = sb("offs_sb", [P, S // 16], U16)
+        nc.sync.dma_start(offs_sb[:], offs)
+        tab_sc = sb("tab_sc", [P, T], U8)
+        nc.vector.memset(tab_sc[:].bitcast(I32), 0)
+        for q in range(4):
+            nc.scalar.dma_start(
+                tab_sc[32 * q : 32 * q + 8, :].bitcast(I32),
+                tab_scales[:, 4 * q : 4 * q + 4, :].bitcast(I32),
+            )
+        ident = sb("ident", [P, P], F32)
+        make_identity(nc, ident[:])
+        warm = sb("warm", [P, 1], F32)
+        nc.scalar.activation(warm[:], ident[:, 0:1], ACT.Sigmoid)
+
+        tab_w = [sb("tab_w%d" % a, [P, T], U32) for a in range(PASSES)]
+        w1_raw = [sb("w1_raw%d" % g, [P, PASSES, 4, w], F32) for g, w in enumerate(W1_LOADS)]
+        w1_start = [sum(W1_LOADS[:g]) for g in range(len(W1_LOADS))]
+
+        def load_tab(a):
+            nc.sync.dma_start(
+                tab_w[a][:].bitcast(I32),
+                tab_words[a].rearrange("p t i -> p (t i)").bitcast(I32),
+            )
+
+        def load_w1(g):
+            c0 = w1_start[g]
+            for a in range(PASSES):
+                nc.sync.dma_start(
+                    w1_raw[g][:, a, :, :],
+                    w1[512 * a : 512 * (a + 1), c0 : c0 + W1_LOADS[g]].rearrange("(p j) c -> p j c", j=4),
+                )
+
+        load_tab(0)
+        pos1_sb = sb("pos1_sb", [P, PH // 16], U16)
+        pos2_sb = sb("pos2_sb", [P, PH // 16], U16)
+        pos3_sb = sb("pos3_sb", [P, CL // 16], U16)
+        pos4_sb = sb("pos4_sb", [P, CL // 16], U16)
+        for dst, src in ((pos1_sb, pos1), (pos2_sb, pos2), (pos3_sb, pos3), (pos4_sb, pos4)):
+            nc.sync.dma_start(dst[:], src)
+        load_tab(1)
+        load_w1(0)
+        load_w1(1)
+        for g in range(2, len(W1_LOADS)):
+            load_w1(g)
+
+        w2_sc = sb("w2_sc", [P, PASSES, N], U8)
+        nc.gpsimd.memset(w2_sc[:].rearrange("p a c -> p (a c)").bitcast(I32), 0)
+        for q in range(4):
+            nc.sync.dma_start(
+                w2_sc[32 * q : 32 * q + 4, :, :].bitcast(I32),
+                wc_scales[:, 4 * q : 4 * q + 4, :].rearrange("a r c -> r a c").bitcast(I32),
+            )
+            nc.sync.dma_start(
+                w2_sc[32 * q + 4 : 32 * q + 8, :, :].bitcast(I32),
+                wf_scales[:, 4 * q : 4 * q + 4, :].rearrange("a r c -> r a c").bitcast(I32),
+            )
+        wc_sb = sb("wc_sb", [P, PASSES, 2 * N], U8)
+        nc.sync.dma_start(wc_sb[:].bitcast(I32), wc_words.rearrange("a p c -> p a c").bitcast(I32))
+        wf_sb = sb("wf_sb", [P, PASSES, N], U32)
+        nc.sync.dma_start(wf_sb[:].bitcast(I32), wf_words.rearrange("a p c i -> p a (c i)").bitcast(I32))
+        mem_sb = sb("mem_sb", [P, OUT_TILES, PH], F32)
+        nc.sync.dma_start(mem_sb[:], mem.rearrange("(n p) m -> p n m", p=P))
+
+        v_sc = [sb("v_sc%d" % hf, [P, BANK], U8) for hf in range(2)]
+        v_w = [[sb("v_w%d%d" % (a, hf), [P, BANK], U32) for hf in range(2)] for a in range(PASSES)]
+
+        def gather_tab(dst, window, hf):
+            nc.vector.tensor_copy(dst[:], window[:].indirect(offs_sb[:, 32 * hf : 32 * hf + 32]))
+
+        w1_bf = [sb("w1_bf%d" % r, [P, PASSES, P, 4], BF16) for r in range(3)]
+        w1_q = [sb("w1_q%d" % i, [P, PASSES * P], U32) for i in range(ROW_TILES)]
+        w1_sc = [sb("w1_sc%d" % i, [P, PASSES * P], U8) for i in range(ROW_TILES)]
+
+        def cast_w1(i):
+            g = max(x for x in range(len(W1_LOADS)) if w1_start[x] <= i * P)
+            c0 = i * P - w1_start[g]
+            (nc.vector.tensor_copy if i in VECTOR_CASTS else nc.scalar.copy)(
+                w1_bf[i % 3][:].rearrange("p a (c i) j -> p a c j i", i=4),
+                w1_raw[g][:, :, :, c0 : c0 + P].rearrange("p a j (c i) -> p a c j i", i=4),
+            )
+
+        def quant_w1(i):
+            nc.vector.quantize_mx(
+                out=w1_q[i][:].bitcast(FP8X4),
+                scales=w1_sc[i][:],
+                in_=w1_bf[i % 3][:].rearrange("p a c j -> p (a c j)"),
+            )
+
+        h_sb = [sb("h%d" % i, [P, S], F32) for i in range(ROW_TILES)]
+
+        def stage1(i):
+            for hf in range(2):
+                bank = banks[2 * (i % 3) + hf]
+                for a in range(PASSES):
+                    nc.tensor.matmul_mx(
+                        out=bank[:],
+                        lhsT=w1_q[i][:, a * P : (a + 1) * P].bitcast(FP8X4),
+                        lhsT_scale=w1_sc[i][:, a * P : (a + 1) * P],
+                        rhs=v_w[a][hf][:].bitcast(FP8X4),
+                        rhs_scale=v_sc[hf][4 * a : P, :],
+                        start=(a == 0),
+                        stop=(a == PASSES - 1),
+                    )
+                nc.scalar.copy(h_sb[i][:, hf * BANK : (hf + 1) * BANK], bank[:])
+
+        picked = [sb("picked%d" % r, [P, 2 * EARLY], F32) for r in range(RING)]
+
+        def gather_h(i, dst, m0, width):
+            for s, pos in enumerate((pos1_sb, pos2_sb)):
+                nc.vector.tensor_copy(
+                    dst[:, s * width : (s + 1) * width],
+                    h_sb[i][:].indirect(pos[:, m0 // 16 : (m0 + width) // 16]),
+                )
+
+        def add_turned(dst, src, width, c):
+            for s in range(2):
+                nc.tensor.matmul(
+                    dst, src[:, s * width + c * P : s * width + (c + 1) * P], ident[:],
+                    start=(s == 0), stop=(s == 1), is_transpose=True,
+                )
+
+        zt_e = [sb("zt_e%d" % a, [P, EARLY // P, 2, P, 2], BF16) for a in range(PASSES)]
+        zt_l = [sb("zt_l%d" % a, [P, 2, P, 2], BF16) for a in range(PASSES)]
+        z_bf = [sb("z_bf%d" % a, [P, PH * 2], F32) for a in range(PASSES)]
+        z_q = [sb("z_q%d" % a, [P, PH], U32) for a in range(PASSES)]
+        z_sc = [sb("z_sc%d" % a, [P, PH], U8) for a in range(PASSES)]
+
+        def turn_early(i):
+            bank = banks[2 * ((i + 2) % 3) if i != 6 else 3]
+            for c in range(EARLY // P):
+                add_turned(bank[:, c * P : (c + 1) * P], picked[i % RING], EARLY, c)
+            a, t = divmod(i, 4)
+            nc.scalar.copy(
+                zt_e[a][:, :, :, 32 * t : 32 * t + 32, :],
+                bank[:, 0:EARLY].rearrange("p (c q u e) -> p c u q e", q=32, u=2, e=2),
+            )
+
+        def turn_back(words, bank, a, c0, chunks):
+            for c in range(chunks):
+                for u in range(2):
+                    nc.tensor.transpose(bank[:, (2 * c + u) * P : (2 * c + u + 1) * P], words(c0 + c, u), ident[:])
+            nc.scalar.copy(
+                z_bf[a][:, c0 * 256 : (c0 + chunks) * 256].rearrange("p (c m u) -> p c m u", u=2, m=P),
+                bank[:, 0 : 2 * chunks * P].rearrange("p (c u m) -> p c m u", u=2, m=P),
+            )
+
+        def quant_z(a, c0, chunks):
+            nc.vector.quantize_mx(
+                out=z_q[a][:, c0 * P : (c0 + chunks) * P].bitcast(FP8X4),
+                scales=z_sc[a][:, c0 * P : (c0 + chunks) * P],
+                in_=z_bf[a][:, c0 * 256 : (c0 + chunks) * 256].bitcast(BF16),
+            )
+
+        def finish_early(a):
+            words = zt_e[a][:].rearrange("p c u q e -> p (c u q e)").bitcast(F32)
+            pick = lambda c, u: words[:, (2 * c + u) * P : (2 * c + u + 1) * P]
+            turn_back(pick, banks[6], a, 0, 2)
+            turn_back(pick, banks[7], a, 2, 1)
+            quant_z(a, 0, 2)
+            quant_z(a, 2, 1)
+
+        def late_slot(i):
+            if i >= 6:
+                return z_bf[1][:, (i - 5) * 2 * LATE : (i - 4) * 2 * LATE]
+            return picked[2 + i // 3][:, (i % 3) * 2 * LATE : (i % 3 + 1) * 2 * LATE]
+
+        def turn_late(a, bank1, bank2):
+            for t in range(4):
+                add_turned(bank1[:, t * P : (t + 1) * P], late_slot(4 * a + t), LATE, 0)
+            nc.scalar.copy(
+                zt_l[a][:],
+                bank1[:].rearrange("p (q u e) -> p u q e", u=2, e=2),
+            )
+            words = zt_l[a][:].rearrange("p u q e -> p (u q e)").bitcast(F32)
+            turn_back(lambda c, u: words[:, u * P : (u + 1) * P], bank2, a, 3, 1)
+            quant_z(a, 3, 1)
+
+        content = sb("content", [P, OUT_TILES, PH], F32)
+        gate = sb("gate", [P, OUT_TILES, PH], F32)
+        y_sb = [sb("y%d" % n, [P, PH], F32) for n in range(OUT_TILES)]
+
+        def content_mm(dst, n, m0):
+            for a in range(PASSES):
+                nc.tensor.matmul_mx(
+                    out=dst,
+                    lhsT=wc_sb[:, a, 2 * n * P : 2 * (n + 1) * P].bitcast(FP4X4),
+                    lhsT_scale=w2_sc[:, a, n * P : (n + 1) * P],
+                    rhs=z_q[a][:, m0 : m0 + P].bitcast(FP8X4),
+                    rhs_scale=z_sc[a][:, m0 : m0 + P],
+                    start=(a == 0), stop=(a == PASSES - 1),
+                )
+
+        def forget_mm(dst, n, m0, width):
+            for a in range(PASSES):
+                nc.tensor.matmul_mx(
+                    out=dst,
+                    lhsT=wf_sb[:, a, n * P : (n + 1) * P].bitcast(FP8X4),
+                    lhsT_scale=w2_sc[4:P, a, n * P : (n + 1) * P],
+                    rhs=z_q[a][:, m0 : m0 + width].bitcast(FP8X4),
+                    rhs_scale=z_sc[a][:, m0 : m0 + width],
+                    start=(a == 0), stop=(a == PASSES - 1),
+                )
+
+        def stage2_early(n, bank_f, bank_c):
+            forget_mm(bank_f[:, 0:256], n, 0, 256)
+            forget_mm(bank_f[:, 256:EARLY], n, 256, P)
+            nc.scalar.activation(gate[:, n, 0:EARLY], bank_f[:, 0:EARLY], ACT.Sigmoid)
+            for c in range(EARLY // P):
+                content_mm(bank_c[:, c * P : (c + 1) * P], n, c * P)
+            nc.scalar.activation(content[:, n, 0:EARLY], bank_c[:, 0:EARLY], ACT.Tanh)
+
+        def state_early(n):
+            nc.vector.tensor_tensor(gate[:, n, 0:EARLY], gate[:, n, 0:EARLY], mem_sb[:, n, 0:EARLY], ALU.mult)
+            nc.vector.tensor_tensor(y_sb[n][:, 0:EARLY], gate[:, n, 0:EARLY], content[:, n, 0:EARLY], ALU.add)
+
+        def stage2_late(n0, bank):
+            for d in range(2):
+                forget_mm(bank[:, d * P : (d + 1) * P], n0 + d, EARLY, P)
+            for d in range(2):
+                content_mm(bank[:, (2 + d) * P : (3 + d) * P], n0 + d, EARLY)
+            nc.scalar.activation(
+                gate[:, n0 : n0 + 2, EARLY:PH], bank[:, 0:256].rearrange("p (d m) -> p d m", d=2), ACT.Sigmoid)
+            nc.scalar.activation(
+                content[:, n0 : n0 + 2, EARLY:PH], bank[:, 256:512].rearrange("p (d m) -> p d m", d=2), ACT.Tanh)
+
+        def state_late(n0):
+            nc.vector.tensor_tensor(
+                gate[:, n0 : n0 + 2, EARLY:PH], gate[:, n0 : n0 + 2, EARLY:PH], mem_sb[:, n0 : n0 + 2, EARLY:PH], ALU.mult)
+            for n in (n0, n0 + 1):
+                nc.vector.tensor_tensor(y_sb[n][:, EARLY:PH], gate[:, n, EARLY:PH], content[:, n, EARLY:PH], ALU.add)
+
+        second = [sb("second%d" % n, [P, CL], F32) for n in range(OUT_TILES)]
+        result = [sb("result%d" % n, [P, CL], F32) for n in range(OUT_TILES)]
+
+        def clauses(n0):
+            for n in (n0, n0 + 1):
+                nc.vector.tensor_copy(second[n][:], y_sb[n][:].indirect(pos4_sb[:]))
+            for n in (n0, n0 + 1):
+                nc.vector.tensor_tensor(result[n][:], y_sb[n][:].indirect(pos3_sb[:]), second[n][:], ALU.subtract)
+                nc.sync.dma_start(out[n * P : (n + 1) * P, :], result[n][:])
+
+        gather_tab(v_w[0][0], tab_w[0], 0)
+        gather_tab(v_w[0][1], tab_w[0], 1)
+        gather_tab(v_sc[0], tab_sc, 0)
+        gather_tab(v_w[1][0], tab_w[1], 0)
+        cast_w1(0)
+        quant_w1(0)
+        gather_tab(v_sc[1], tab_sc, 1)
+        gather_tab(v_w[1][1], tab_w[1], 1)
+        cast_w1(1)
+        quant_w1(1)
+        cast_w1(2)
+        for i in range(ROW_TILES + 2):
+            if i < ROW_TILES:
+                stage1(i)
+            if i + 2 < ROW_TILES:
+                quant_w1(i + 2)
+            if i + 3 < ROW_TILES:
+                cast_w1(i + 3)
+            if i < ROW_TILES:
+                gather_h(i, picked[i % RING], 0, EARLY)
+            if i >= 2:
+                turn_early(i - 2)
+            if i - 2 == 3:
+                finish_early(0)
+        finish_early(1)
+        for i in range(ROW_TILES):
+            gather_h(i, late_slot(i), EARLY, LATE)
+        turn_late(0, banks[6], banks[5])
+        stage2_early(0, banks[2], banks[4])
+        turn_late(1, banks[7], banks[1])
+        stage2_early(1, banks[0], banks[3])
+        state_early(0)
+        stage2_early(2, banks[6], banks[5])
+        state_early(1)
+        stage2_late(0, banks[7])
+        stage2_early(3, banks[2], banks[4])
+        state_early(2)
+        state_late(0)
+        clauses(0)
+        stage2_late(2, banks[1])
+        stage2_early(4, banks[0], banks[3])
+        state_early(3)
+        state_late(2)
+        clauses(2)
+        stage2_early(5, banks[6], banks[5])
+        stage2_late(4, banks[7])
+        state_early(4)
+        state_early(5)
+        state_late(4)
+        clauses(4)

@@ -22,11 +22,15 @@ BANK = 512
 PASSES = 2
 ROW_TILES = H // P
 OUT_TILES = N // P
-W1_LOADS = (128, 128, 256, 256, 256)
+W1_LOADS = (256, 256, 256, 256)
 EARLY = 384
 LATE = PH - EARLY
 RING = 4
-VECTOR_CASTS = (2, 5)
+LAG = 3
+AHEAD = 2
+TURN_BANKS = (0, 2, 4, 0, 2, 3, 4, 0)
+EARLY_BANKS = ((1, 5), (2, 3), (4, 0))
+VECTOR_CASTS = (3, 7)
 
 
 def tile_list_phrase_tree_forget_kernel(
@@ -38,8 +42,8 @@ def tile_list_phrase_tree_forget_kernel(
         keep = ctx.enter_context(tc.tile_pool(name="keep", bufs=1))
         psum = ctx.enter_context(tc.psum_pool(name="psum", bufs=1))
 
-        def sb(name, shape, dtype):
-            return keep.tile(shape, dtype, name=name, align_bytes=64)
+        def sb(name, shape, dtype, tag=None):
+            return keep.tile(shape, dtype, name=name, tag=tag or name, align_bytes=64)
 
         banks = [psum.tile([P, BANK], F32, name="bank%d" % b) for b in range(8)]
 
@@ -48,7 +52,7 @@ def tile_list_phrase_tree_forget_kernel(
         tab_sc = sb("tab_sc", [P, T], U8)
         nc.vector.memset(tab_sc[:].bitcast(I32), 0)
         for q in range(4):
-            nc.scalar.dma_start(
+            nc.sync.dma_start(
                 tab_sc[32 * q : 32 * q + 8, :].bitcast(I32),
                 tab_scales[:, 4 * q : 4 * q + 4, :].bitcast(I32),
             )
@@ -58,7 +62,8 @@ def tile_list_phrase_tree_forget_kernel(
         nc.scalar.activation(warm[:], ident[:, 0:1], ACT.Sigmoid)
 
         tab_w = [sb("tab_w%d" % a, [P, T], U32) for a in range(PASSES)]
-        w1_raw = [sb("w1_raw%d" % g, [P, PASSES, 4, w], F32) for g, w in enumerate(W1_LOADS)]
+        w1_raw = [sb("w1_raw%d" % g, [P, PASSES, 4, w], F32) for g, w in enumerate(W1_LOADS) if g > 0]
+        w1_head = [sb("w1_head%d" % a, [P, 4, W1_LOADS[0]], F32) for a in range(PASSES)]
         w1_start = [sum(W1_LOADS[:g]) for g in range(len(W1_LOADS))]
 
         def load_tab(a):
@@ -71,20 +76,18 @@ def tile_list_phrase_tree_forget_kernel(
             c0 = w1_start[g]
             for a in range(PASSES):
                 nc.sync.dma_start(
-                    w1_raw[g][:, a, :, :],
+                    w1_raw[g - 1][:, a, :, :] if g > 0 else w1_head[a][:],
                     w1[512 * a : 512 * (a + 1), c0 : c0 + W1_LOADS[g]].rearrange("(p j) c -> p j c", j=4),
                 )
 
         load_tab(0)
+        load_w1(0)
+        load_tab(1)
+        load_w1(1)
         pos1_sb = sb("pos1_sb", [P, PH // 16], U16)
         pos2_sb = sb("pos2_sb", [P, PH // 16], U16)
-        pos3_sb = sb("pos3_sb", [P, CL // 16], U16)
-        pos4_sb = sb("pos4_sb", [P, CL // 16], U16)
-        for dst, src in ((pos1_sb, pos1), (pos2_sb, pos2), (pos3_sb, pos3), (pos4_sb, pos4)):
-            nc.sync.dma_start(dst[:], src)
-        load_tab(1)
-        load_w1(0)
-        load_w1(1)
+        nc.sync.dma_start(pos1_sb[:], pos1)
+        nc.sync.dma_start(pos2_sb[:], pos2)
         for g in range(2, len(W1_LOADS)):
             load_w1(g)
 
@@ -105,6 +108,10 @@ def tile_list_phrase_tree_forget_kernel(
         nc.sync.dma_start(wf_sb[:].bitcast(I32), wf_words.rearrange("a p c i -> p a (c i)").bitcast(I32))
         mem_sb = sb("mem_sb", [P, OUT_TILES, PH], F32)
         nc.sync.dma_start(mem_sb[:], mem.rearrange("(n p) m -> p n m", p=P))
+        pos3_sb = sb("pos3_sb", [P, CL // 16], U16)
+        pos4_sb = sb("pos4_sb", [P, CL // 16], U16)
+        nc.sync.dma_start(pos3_sb[:], pos3)
+        nc.sync.dma_start(pos4_sb[:], pos4)
 
         v_sc = [sb("v_sc%d" % hf, [P, BANK], U8) for hf in range(2)]
         v_w = [[sb("v_w%d%d" % (a, hf), [P, BANK], U32) for hf in range(2)] for a in range(PASSES)]
@@ -112,23 +119,41 @@ def tile_list_phrase_tree_forget_kernel(
         def gather_tab(dst, window, hf):
             nc.vector.tensor_copy(dst[:], window[:].indirect(offs_sb[:, 32 * hf : 32 * hf + 32]))
 
-        w1_bf = [sb("w1_bf%d" % r, [P, PASSES, P, 4], BF16) for r in range(3)]
+        w1_bf = [sb("w1_bf%d" % r, [P, PASSES, P, 4], BF16) for r in range(AHEAD - 1)]
+        w1_bf_first = sb("w1_bf_first", [P, PASSES, P, 4], BF16)
+        picked = [sb("picked%d" % r, [P, EARLY + 512], F32) for r in range(RING)]
+
+        def cast_buf(i):
+            if i == 0:
+                return w1_bf_first[:]
+            if i >= AHEAD:
+                return picked[(i - AHEAD) % RING][:, EARLY : EARLY + 512].bitcast(BF16).rearrange("p (a c j) -> p a c j", a=PASSES, j=4)
+            return w1_bf[i - 1][:]
+
         w1_q = [sb("w1_q%d" % i, [P, PASSES * P], U32) for i in range(ROW_TILES)]
         w1_sc = [sb("w1_sc%d" % i, [P, PASSES * P], U8) for i in range(ROW_TILES)]
 
         def cast_w1(i):
             g = max(x for x in range(len(W1_LOADS)) if w1_start[x] <= i * P)
             c0 = i * P - w1_start[g]
-            (nc.vector.tensor_copy if i in VECTOR_CASTS else nc.scalar.copy)(
-                w1_bf[i % 3][:].rearrange("p a (c i) j -> p a c j i", i=4),
-                w1_raw[g][:, :, :, c0 : c0 + P].rearrange("p a j (c i) -> p a c j i", i=4),
-            )
+            copy = nc.vector.tensor_copy if i in VECTOR_CASTS else nc.scalar.copy
+            if g == 0:
+                for a in range(PASSES):
+                    copy(
+                        cast_buf(i)[:, a, :, :].rearrange("p (c i) j -> p c j i", i=2),
+                        w1_head[a][:, :, c0 : c0 + P].rearrange("p j (c i) -> p c j i", i=2),
+                    )
+            else:
+                copy(
+                    cast_buf(i).rearrange("p a (c i) j -> p a c j i", i=2),
+                    w1_raw[g - 1][:, :, :, c0 : c0 + P].rearrange("p a j (c i) -> p a c j i", i=2),
+                )
 
         def quant_w1(i):
             nc.vector.quantize_mx(
                 out=w1_q[i][:].bitcast(FP8X4),
                 scales=w1_sc[i][:],
-                in_=w1_bf[i % 3][:].rearrange("p a c j -> p (a c j)"),
+                in_=cast_buf(i).rearrange("p a c j -> p (a c j)"),
             )
 
         h_sb = [sb("h%d" % i, [P, S], F32) for i in range(ROW_TILES)]
@@ -147,8 +172,6 @@ def tile_list_phrase_tree_forget_kernel(
                         stop=(a == PASSES - 1),
                     )
                 nc.scalar.copy(h_sb[i][:, hf * BANK : (hf + 1) * BANK], bank[:])
-
-        picked = [sb("picked%d" % r, [P, 2 * EARLY], F32) for r in range(RING)]
 
         def gather_h(i, dst, m0, width):
             for s, pos in enumerate((pos1_sb, pos2_sb)):
@@ -171,7 +194,7 @@ def tile_list_phrase_tree_forget_kernel(
         z_sc = [sb("z_sc%d" % a, [P, PH], U8) for a in range(PASSES)]
 
         def turn_early(i):
-            bank = banks[2 * ((i + 2) % 3) if i != 6 else 3]
+            bank = banks[TURN_BANKS[i]]
             for c in range(EARLY // P):
                 add_turned(bank[:, c * P : (c + 1) * P], picked[i % RING], EARLY, c)
             a, t = divmod(i, 4)
@@ -205,9 +228,9 @@ def tile_list_phrase_tree_forget_kernel(
             quant_z(a, 2, 1)
 
         def late_slot(i):
-            if i >= 6:
+            if i >= 5:
                 return z_bf[1][:, (i - 5) * 2 * LATE : (i - 4) * 2 * LATE]
-            return picked[2 + i // 3][:, (i % 3) * 2 * LATE : (i % 3 + 1) * 2 * LATE]
+            return picked[1 + 2 * (i // 3)][:, (i % 3) * 2 * LATE : (i % 3 + 1) * 2 * LATE]
 
         def turn_late(a, bank1, bank2):
             for t in range(4):
@@ -224,45 +247,47 @@ def tile_list_phrase_tree_forget_kernel(
         gate = sb("gate", [P, OUT_TILES, PH], F32)
         y_sb = [sb("y%d" % n, [P, PH], F32) for n in range(OUT_TILES)]
 
-        def content_mm(dst, n, m0):
-            for a in range(PASSES):
-                nc.tensor.matmul_mx(
-                    out=dst,
-                    lhsT=wc_sb[:, a, 2 * n * P : 2 * (n + 1) * P].bitcast(FP4X4),
-                    lhsT_scale=w2_sc[:, a, n * P : (n + 1) * P],
-                    rhs=z_q[a][:, m0 : m0 + P].bitcast(FP8X4),
-                    rhs_scale=z_sc[a][:, m0 : m0 + P],
-                    start=(a == 0), stop=(a == PASSES - 1),
-                )
+        def content_mm(dst, n, a, m0, start, stop):
+            nc.tensor.matmul_mx(
+                out=dst,
+                lhsT=wc_sb[:, a, 2 * n * P : 2 * (n + 1) * P].bitcast(FP4X4),
+                lhsT_scale=w2_sc[:, a, n * P : (n + 1) * P],
+                rhs=z_q[a][:, m0 : m0 + P].bitcast(FP8X4),
+                rhs_scale=z_sc[a][:, m0 : m0 + P],
+                start=start, stop=stop,
+            )
 
-        def forget_mm(dst, n, m0, width):
-            for a in range(PASSES):
-                nc.tensor.matmul_mx(
-                    out=dst,
-                    lhsT=wf_sb[:, a, n * P : (n + 1) * P].bitcast(FP8X4),
-                    lhsT_scale=w2_sc[4:P, a, n * P : (n + 1) * P],
-                    rhs=z_q[a][:, m0 : m0 + width].bitcast(FP8X4),
-                    rhs_scale=z_sc[a][:, m0 : m0 + width],
-                    start=(a == 0), stop=(a == PASSES - 1),
-                )
+        def forget_mm(dst, n, a, m0, width, start, stop):
+            nc.tensor.matmul_mx(
+                out=dst,
+                lhsT=wf_sb[:, a, n * P : (n + 1) * P].bitcast(FP8X4),
+                lhsT_scale=w2_sc[4:P, a, n * P : (n + 1) * P],
+                rhs=z_q[a][:, m0 : m0 + width].bitcast(FP8X4),
+                rhs_scale=z_sc[a][:, m0 : m0 + width],
+                start=start, stop=stop,
+            )
 
-        def stage2_early(n, bank_f, bank_c):
-            forget_mm(bank_f[:, 0:256], n, 0, 256)
-            forget_mm(bank_f[:, 256:EARLY], n, 256, P)
-            nc.scalar.activation(gate[:, n, 0:EARLY], bank_f[:, 0:EARLY], ACT.Sigmoid)
+        def early_pass(n, a):
+            bank_f, bank_c = (banks[b] for b in EARLY_BANKS[n % 3])
+            forget_mm(bank_f[:, 0:256], n, a, 0, 256, a == 0, False)
+            forget_mm(bank_f[:, 256:EARLY], n, a, 256, P, False, a == 1)
+            if a == 1:
+                nc.scalar.activation(gate[:, n, 0:EARLY], bank_f[:, 0:EARLY], ACT.Sigmoid)
             for c in range(EARLY // P):
-                content_mm(bank_c[:, c * P : (c + 1) * P], n, c * P)
-            nc.scalar.activation(content[:, n, 0:EARLY], bank_c[:, 0:EARLY], ACT.Tanh)
+                content_mm(bank_c[:, c * P : (c + 1) * P], n, a, c * P, a == 0 and c == 0, a == 1 and c == EARLY // P - 1)
+            if a == 1:
+                nc.scalar.activation(content[:, n, 0:EARLY], bank_c[:, 0:EARLY], ACT.Tanh)
 
         def state_early(n):
             nc.vector.tensor_tensor(gate[:, n, 0:EARLY], gate[:, n, 0:EARLY], mem_sb[:, n, 0:EARLY], ALU.mult)
             nc.vector.tensor_tensor(y_sb[n][:, 0:EARLY], gate[:, n, 0:EARLY], content[:, n, 0:EARLY], ALU.add)
 
         def stage2_late(n0, bank):
-            for d in range(2):
-                forget_mm(bank[:, d * P : (d + 1) * P], n0 + d, EARLY, P)
-            for d in range(2):
-                content_mm(bank[:, (2 + d) * P : (3 + d) * P], n0 + d, EARLY)
+            for a in range(PASSES):
+                for d in range(2):
+                    forget_mm(bank[:, d * P : (d + 1) * P], n0 + d, a, EARLY, P, a == 0 and d == 0, False)
+                for d in range(2):
+                    content_mm(bank[:, (2 + d) * P : (3 + d) * P], n0 + d, a, EARLY, False, a == 1 and d == 1)
             nc.scalar.activation(
                 gate[:, n0 : n0 + 2, EARLY:PH], bank[:, 0:256].rearrange("p (d m) -> p d m", d=2), ACT.Sigmoid)
             nc.scalar.activation(
@@ -287,49 +312,53 @@ def tile_list_phrase_tree_forget_kernel(
         gather_tab(v_w[0][0], tab_w[0], 0)
         gather_tab(v_w[0][1], tab_w[0], 1)
         gather_tab(v_sc[0], tab_sc, 0)
-        gather_tab(v_w[1][0], tab_w[1], 0)
+        gather_tab(v_sc[1], tab_sc, 1)
         cast_w1(0)
         quant_w1(0)
-        gather_tab(v_sc[1], tab_sc, 1)
+        gather_tab(v_w[1][0], tab_w[1], 0)
         gather_tab(v_w[1][1], tab_w[1], 1)
         cast_w1(1)
         quant_w1(1)
-        cast_w1(2)
-        for i in range(ROW_TILES + 2):
+        for i in range(ROW_TILES + LAG):
             if i < ROW_TILES:
                 stage1(i)
-            if i + 2 < ROW_TILES:
-                quant_w1(i + 2)
-            if i + 3 < ROW_TILES:
-                cast_w1(i + 3)
+            if i + AHEAD < ROW_TILES:
+                cast_w1(i + AHEAD)
+                quant_w1(i + AHEAD)
             if i < ROW_TILES:
                 gather_h(i, picked[i % RING], 0, EARLY)
-            if i >= 2:
-                turn_early(i - 2)
-            if i - 2 == 3:
+            if i >= LAG:
+                turn_early(i - LAG)
+            if i - LAG == 3:
                 finish_early(0)
+        early_pass(0, 0)
+        early_pass(1, 0)
         finish_early(1)
+        early_pass(2, 0)
         for i in range(ROW_TILES):
             gather_h(i, late_slot(i), EARLY, LATE)
-        turn_late(0, banks[6], banks[5])
-        stage2_early(0, banks[2], banks[4])
-        turn_late(1, banks[7], banks[1])
-        stage2_early(1, banks[0], banks[3])
+        turn_late(0, banks[6], banks[7])
+        early_pass(0, 1)
+        turn_late(1, banks[6], banks[7])
+        early_pass(1, 1)
         state_early(0)
-        stage2_early(2, banks[6], banks[5])
+        early_pass(2, 1)
         state_early(1)
-        stage2_late(0, banks[7])
-        stage2_early(3, banks[2], banks[4])
+        stage2_late(0, banks[6])
+        early_pass(3, 0)
+        early_pass(3, 1)
         state_early(2)
         state_late(0)
         clauses(0)
-        stage2_late(2, banks[1])
-        stage2_early(4, banks[0], banks[3])
+        stage2_late(2, banks[7])
+        early_pass(4, 0)
+        early_pass(4, 1)
         state_early(3)
         state_late(2)
         clauses(2)
-        stage2_early(5, banks[6], banks[5])
-        stage2_late(4, banks[7])
+        early_pass(5, 0)
+        early_pass(5, 1)
+        stage2_late(4, banks[6])
         state_early(4)
         state_early(5)
         state_late(4)

@@ -1,7 +1,6 @@
 from contextlib import ExitStack
 
 import concourse.mybir as mybir
-from concourse.masks import make_identity
 
 K, T, S, H, PH, N, CL = 1024, 2048, 1024, 1024, 512, 768, 256
 FLOPS = 2 * K * H * S + 2 * 2 * H * N * PH
@@ -22,15 +21,9 @@ BANK = 512
 PASSES = 2
 ROW_TILES = H // P
 OUT_TILES = N // P
-W1_LOADS = (256, 256, 256, 256)
 EARLY = 384
 LATE = PH - EARLY
-RING = 4
-LAG = 3
-AHEAD = 2
-TURN_BANKS = (0, 2, 4, 0, 2, 3, 4, 0)
-EARLY_BANKS = ((1, 5), (2, 3), (4, 0))
-VECTOR_CASTS = (3, 7)
+SPLIT = 2
 
 
 def tile_list_phrase_tree_forget_kernel(
@@ -56,15 +49,13 @@ def tile_list_phrase_tree_forget_kernel(
                 tab_sc[32 * q : 32 * q + 8, :].bitcast(I32),
                 tab_scales[:, 4 * q : 4 * q + 4, :].bitcast(I32),
             )
-        ident = sb("ident", [P, P], F32)
-        make_identity(nc, ident[:])
-        warm = sb("warm", [P, 1], F32)
-        nc.scalar.activation(warm[:], ident[:, 0:1], ACT.Sigmoid)
+        w2_sc = sb("w2_sc", [P, PASSES, N], U8)
+        nc.gpsimd.memset(w2_sc[:].rearrange("p a c -> p (a c)").bitcast(I32), 0)
+        warm = sb("warm", [P, 16], F32)
+        nc.gpsimd.memset(warm[:, 0:1], 0.0)
+        nc.scalar.activation(warm[:, 8:9], warm[:, 0:1], ACT.Sigmoid)
 
         tab_w = [sb("tab_w%d" % a, [P, T], U32) for a in range(PASSES)]
-        w1_raw = [sb("w1_raw%d" % g, [P, PASSES, 4, w], F32) for g, w in enumerate(W1_LOADS) if g > 0]
-        w1_head = [sb("w1_head%d" % a, [P, 4, W1_LOADS[0]], F32) for a in range(PASSES)]
-        w1_start = [sum(W1_LOADS[:g]) for g in range(len(W1_LOADS))]
 
         def load_tab(a):
             nc.sync.dma_start(
@@ -72,27 +63,25 @@ def tile_list_phrase_tree_forget_kernel(
                 tab_words[a].rearrange("p t i -> p (t i)").bitcast(I32),
             )
 
-        def load_w1(g):
-            c0 = w1_start[g]
-            for a in range(PASSES):
-                nc.sync.dma_start(
-                    w1_raw[g - 1][:, a, :, :] if g > 0 else w1_head[a][:],
-                    w1[512 * a : 512 * (a + 1), c0 : c0 + W1_LOADS[g]].rearrange("(p j) c -> p j c", j=4),
-                )
+        w1_raw = {(g, a): sb("w1_raw%d%d" % (g, a), [P, 4, BANK], F32) for g in range(2) for a in range(PASSES)}
+
+        def load_w1(g, a):
+            nc.sync.dma_start(
+                w1_raw[(g, a)][:],
+                w1[512 * a : 512 * (a + 1), 512 * g : 512 * (g + 1)].rearrange("(p j) c -> p j c", j=4),
+            )
 
         load_tab(0)
-        load_w1(0)
+        load_w1(0, 0)
         load_tab(1)
-        load_w1(1)
+        load_w1(0, 1)
         pos1_sb = sb("pos1_sb", [P, PH // 16], U16)
         pos2_sb = sb("pos2_sb", [P, PH // 16], U16)
         nc.sync.dma_start(pos1_sb[:], pos1)
         nc.sync.dma_start(pos2_sb[:], pos2)
-        for g in range(2, len(W1_LOADS)):
-            load_w1(g)
+        load_w1(1, 0)
+        load_w1(1, 1)
 
-        w2_sc = sb("w2_sc", [P, PASSES, N], U8)
-        nc.gpsimd.memset(w2_sc[:].rearrange("p a c -> p (a c)").bitcast(I32), 0)
         for q in range(4):
             nc.sync.dma_start(
                 w2_sc[32 * q : 32 * q + 4, :, :].bitcast(I32),
@@ -119,53 +108,41 @@ def tile_list_phrase_tree_forget_kernel(
         def gather_tab(dst, window, hf):
             nc.vector.tensor_copy(dst[:], window[:].indirect(offs_sb[:, 32 * hf : 32 * hf + 32]))
 
-        w1_bf = [sb("w1_bf%d" % r, [P, PASSES, P, 4], BF16) for r in range(AHEAD - 1)]
-        w1_bf_first = sb("w1_bf_first", [P, PASSES, P, 4], BF16)
-        picked = [sb("picked%d" % r, [P, EARLY + 512], F32) for r in range(RING)]
+        z_early = [sb("z_early0", [P, 3 * EARLY + 1024], F32), sb("z_early1", [P, 4 * EARLY], F32)]
+        w1_bf_own = {ga: sb("w1_bf%d%d" % ga, [P, 2048], BF16) for ga in ((0, 0), (0, 1), (1, 0))}
+        w1_q = {(g, a): sb("w1_q%d%d" % (g, a), [P, BANK], U32, tag="reuse" if g + a == 2 else None)
+                for g in range(2) for a in range(PASSES)}
+        w1_sc = {(g, a): sb("w1_sc%d%d" % (g, a), [P, BANK], U8) for g in range(2) for a in range(PASSES)}
 
-        def cast_buf(i):
-            if i == 0:
-                return w1_bf_first[:]
-            if i >= AHEAD:
-                return picked[(i - AHEAD) % RING][:, EARLY : EARLY + 512].bitcast(BF16).rearrange("p (a c j) -> p a c j", a=PASSES, j=4)
-            return w1_bf[i - 1][:]
+        def w1_bf(g, a):
+            if (g, a) == (1, 1):
+                return z_early[0][:, 3 * EARLY : 3 * EARLY + 1024].bitcast(BF16)
+            return w1_bf_own[(g, a)][:]
 
-        w1_q = [sb("w1_q%d" % i, [P, PASSES * P], U32) for i in range(ROW_TILES)]
-        w1_sc = [sb("w1_sc%d" % i, [P, PASSES * P], U8) for i in range(ROW_TILES)]
+        def cast_w1(copy, g, a, t0):
+            copy(
+                w1_bf(g, a)[:, t0 * 512 : (t0 + 2) * 512].rearrange("p (t m j) -> p m j t", t=2, j=4),
+                w1_raw[(g, a)][:].rearrange("p j (m t) -> p m j t", t=4)[:, :, :, t0 : t0 + 2],
+            )
 
-        def cast_w1(i):
-            g = max(x for x in range(len(W1_LOADS)) if w1_start[x] <= i * P)
-            c0 = i * P - w1_start[g]
-            copy = nc.vector.tensor_copy if i in VECTOR_CASTS else nc.scalar.copy
-            if g == 0:
-                for a in range(PASSES):
-                    copy(
-                        cast_buf(i)[:, a, :, :].rearrange("p (c i) j -> p c j i", i=2),
-                        w1_head[a][:, :, c0 : c0 + P].rearrange("p j (c i) -> p c j i", i=2),
-                    )
-            else:
-                copy(
-                    cast_buf(i).rearrange("p a (c i) j -> p a c j i", i=2),
-                    w1_raw[g - 1][:, :, :, c0 : c0 + P].rearrange("p a j (c i) -> p a c j i", i=2),
-                )
-
-        def quant_w1(i):
+        def quant_w1(g, a, t0, tiles):
             nc.vector.quantize_mx(
-                out=w1_q[i][:].bitcast(FP8X4),
-                scales=w1_sc[i][:],
-                in_=cast_buf(i).rearrange("p a c j -> p (a c j)"),
+                out=w1_q[(g, a)][:, t0 * P : (t0 + tiles) * P].bitcast(FP8X4),
+                scales=w1_sc[(g, a)][:, t0 * P : (t0 + tiles) * P],
+                in_=w1_bf(g, a)[:, t0 * 512 : (t0 + tiles) * 512],
             )
 
         h_sb = [sb("h%d" % i, [P, S], F32) for i in range(ROW_TILES)]
 
         def stage1(i):
+            g, t = divmod(i, 4)
             for hf in range(2):
-                bank = banks[2 * (i % 3) + hf]
+                bank = banks[2 * t + hf]
                 for a in range(PASSES):
                     nc.tensor.matmul_mx(
                         out=bank[:],
-                        lhsT=w1_q[i][:, a * P : (a + 1) * P].bitcast(FP8X4),
-                        lhsT_scale=w1_sc[i][:, a * P : (a + 1) * P],
+                        lhsT=w1_q[(g, a)][:, t * P : (t + 1) * P].bitcast(FP8X4),
+                        lhsT_scale=w1_sc[(g, a)][:, t * P : (t + 1) * P],
                         rhs=v_w[a][hf][:].bitcast(FP8X4),
                         rhs_scale=v_sc[hf][4 * a : P, :],
                         start=(a == 0),
@@ -173,75 +150,57 @@ def tile_list_phrase_tree_forget_kernel(
                     )
                 nc.scalar.copy(h_sb[i][:, hf * BANK : (hf + 1) * BANK], bank[:])
 
-        def gather_h(i, dst, m0, width):
-            for s, pos in enumerate((pos1_sb, pos2_sb)):
-                nc.vector.tensor_copy(
-                    dst[:, s * width : (s + 1) * width],
-                    h_sb[i][:].indirect(pos[:, m0 // 16 : (m0 + width) // 16]),
-                )
+        first = [sb("first%d" % r, [P, EARLY], F32) for r in range(2)]
 
-        def add_turned(dst, src, width, c):
-            for s in range(2):
-                nc.tensor.matmul(
-                    dst, src[:, s * width + c * P : s * width + (c + 1) * P], ident[:],
-                    start=(s == 0), stop=(s == 1), is_transpose=True,
-                )
+        def pick_first(i, dst, m0, width):
+            nc.vector.tensor_copy(dst, h_sb[i][:].indirect(pos1_sb[:, m0 // 16 : (m0 + width) // 16]))
 
-        zt_e = [sb("zt_e%d" % a, [P, EARLY // P, 2, P, 2], BF16) for a in range(PASSES)]
-        zt_l = [sb("zt_l%d" % a, [P, 2, P, 2], BF16) for a in range(PASSES)]
-        z_bf = [sb("z_bf%d" % a, [P, PH * 2], F32) for a in range(PASSES)]
+        def add_second(i, dst, src, m0, width):
+            nc.vector.tensor_tensor(dst, h_sb[i][:].indirect(pos2_sb[:, m0 // 16 : (m0 + width) // 16]), src, ALU.add)
+
+        def phrases_early(i):
+            g, t = divmod(i, 4)
+            w = EARLY // SPLIT
+            for s in range(SPLIT):
+                pick_first(i, first[i % 2][:, s * w : (s + 1) * w], s * w, w)
+            for s in range(SPLIT):
+                add_second(i, z_early[g][:, t * EARLY + s * w : t * EARLY + (s + 1) * w],
+                           first[i % 2][:, s * w : (s + 1) * w], s * w, w)
+
+        z_bf = {}
         z_q = [sb("z_q%d" % a, [P, PH], U32) for a in range(PASSES)]
         z_sc = [sb("z_sc%d" % a, [P, PH], U8) for a in range(PASSES)]
 
-        def turn_early(i):
-            bank = banks[TURN_BANKS[i]]
-            for c in range(EARLY // P):
-                add_turned(bank[:, c * P : (c + 1) * P], picked[i % RING], EARLY, c)
-            a, t = divmod(i, 4)
+        def weave(a, src, m0, width):
             nc.scalar.copy(
-                zt_e[a][:, :, :, 32 * t : 32 * t + 32, :],
-                bank[:, 0:EARLY].rearrange("p (c q u e) -> p c u q e", q=32, u=2, e=2),
+                z_bf[a][:, 2 * m0 : 2 * (m0 + width)].bitcast(BF16).rearrange("p (c i t) -> p c t i", i=2, t=4),
+                src.rearrange("p t (c i) -> p c t i", i=2),
             )
 
-        def turn_back(words, bank, a, c0, chunks):
-            for c in range(chunks):
-                for u in range(2):
-                    nc.tensor.transpose(bank[:, (2 * c + u) * P : (2 * c + u + 1) * P], words(c0 + c, u), ident[:])
-            nc.scalar.copy(
-                z_bf[a][:, c0 * 256 : (c0 + chunks) * 256].rearrange("p (c m u) -> p c m u", u=2, m=P),
-                bank[:, 0 : 2 * chunks * P].rearrange("p (c u m) -> p c m u", u=2, m=P),
-            )
-
-        def quant_z(a, c0, chunks):
+        def quant_z(a, m0, width):
             nc.vector.quantize_mx(
-                out=z_q[a][:, c0 * P : (c0 + chunks) * P].bitcast(FP8X4),
-                scales=z_sc[a][:, c0 * P : (c0 + chunks) * P],
-                in_=z_bf[a][:, c0 * 256 : (c0 + chunks) * 256].bitcast(BF16),
+                out=z_q[a][:, m0 : m0 + width].bitcast(FP8X4),
+                scales=z_sc[a][:, m0 : m0 + width],
+                in_=z_bf[a][:, 2 * m0 : 2 * (m0 + width)].bitcast(BF16),
             )
 
         def finish_early(a):
-            words = zt_e[a][:].rearrange("p c u q e -> p (c u q e)").bitcast(F32)
-            pick = lambda c, u: words[:, (2 * c + u) * P : (2 * c + u + 1) * P]
-            turn_back(pick, banks[6], a, 0, 2)
-            turn_back(pick, banks[7], a, 2, 1)
-            quant_z(a, 0, 2)
-            quant_z(a, 2, 1)
+            z4 = z_early[a][:, 0 : 4 * EARLY].rearrange("p (t m) -> p t m", t=4)
+            for m0, width in ((0, 256), (256, P)):
+                weave(a, z4[:, :, m0 : m0 + width], m0, width)
+                quant_z(a, m0, width)
 
-        def late_slot(i):
-            if i >= 5:
-                return z_bf[1][:, (i - 5) * 2 * LATE : (i - 4) * 2 * LATE]
-            return picked[1 + 2 * (i // 3)][:, (i % 3) * 2 * LATE : (i % 3 + 1) * 2 * LATE]
+        z_late1 = sb("z_late1", [P, 4 * LATE], F32)
 
-        def turn_late(a, bank1, bank2):
-            for t in range(4):
-                add_turned(bank1[:, t * P : (t + 1) * P], late_slot(4 * a + t), LATE, 0)
-            nc.scalar.copy(
-                zt_l[a][:],
-                bank1[:].rearrange("p (q u e) -> p u q e", u=2, e=2),
-            )
-            words = zt_l[a][:].rearrange("p u q e -> p (u q e)").bitcast(F32)
-            turn_back(lambda c, u: words[:, u * P : (u + 1) * P], bank2, a, 3, 1)
-            quant_z(a, 3, 1)
+        def z_late(a):
+            return z_late1[:] if a == 1 else z_bf[1][:, 0 : 4 * LATE]
+
+        def late_first(i):
+            return first[1][:, (i % 3) * LATE : (i % 3 + 1) * LATE]
+
+        def finish_late(a):
+            weave(a, z_late(a).rearrange("p (t m) -> p t m", t=4), EARLY, LATE)
+            quant_z(a, EARLY, LATE)
 
         content = sb("content", [P, OUT_TILES, PH], F32)
         gate = sb("gate", [P, OUT_TILES, PH], F32)
@@ -268,7 +227,7 @@ def tile_list_phrase_tree_forget_kernel(
             )
 
         def early_pass(n, a):
-            bank_f, bank_c = (banks[b] for b in EARLY_BANKS[n % 3])
+            bank_f, bank_c = (banks[b] for b in (2 * (n % 3), 2 * (n % 3) + 1))
             forget_mm(bank_f[:, 0:256], n, a, 0, 256, a == 0, False)
             forget_mm(bank_f[:, 256:EARLY], n, a, 256, P, False, a == 1)
             if a == 1:
@@ -309,37 +268,55 @@ def tile_list_phrase_tree_forget_kernel(
                 nc.vector.tensor_tensor(result[n][:], y_sb[n][:].indirect(pos3_sb[:]), second[n][:], ALU.subtract)
                 nc.sync.dma_start(out[n * P : (n + 1) * P, :], result[n][:])
 
+        on_scalar, on_vector = nc.scalar.copy, nc.vector.tensor_copy
         gather_tab(v_w[0][0], tab_w[0], 0)
         gather_tab(v_w[0][1], tab_w[0], 1)
         gather_tab(v_sc[0], tab_sc, 0)
         gather_tab(v_sc[1], tab_sc, 1)
-        cast_w1(0)
-        quant_w1(0)
+        cast_w1(on_scalar, 0, 0, 0)
+        cast_w1(on_vector, 0, 0, 2)
+        quant_w1(0, 0, 0, 4)
         gather_tab(v_w[1][0], tab_w[1], 0)
         gather_tab(v_w[1][1], tab_w[1], 1)
-        cast_w1(1)
-        quant_w1(1)
-        for i in range(ROW_TILES + LAG):
-            if i < ROW_TILES:
-                stage1(i)
-            if i + AHEAD < ROW_TILES:
-                cast_w1(i + AHEAD)
-                quant_w1(i + AHEAD)
-            if i < ROW_TILES:
-                gather_h(i, picked[i % RING], 0, EARLY)
-            if i >= LAG:
-                turn_early(i - LAG)
-            if i - LAG == 3:
-                finish_early(0)
-        early_pass(0, 0)
-        early_pass(1, 0)
+        cast_w1(on_vector, 0, 1, 0)
+        cast_w1(on_scalar, 0, 1, 2)
+        quant_w1(0, 1, 0, 1)
+        quant_w1(0, 1, 1, 1)
+        quant_w1(0, 1, 2, 2)
+        cast_w1(on_vector, 1, 0, 0)
+        stage1(0)
+        stage1(1)
+        phrases_early(0)
+        cast_w1(on_scalar, 1, 0, 2)
+        stage1(2)
+        quant_w1(1, 0, 0, 4)
+        phrases_early(1)
+        cast_w1(on_scalar, 1, 1, 0)
+        cast_w1(on_scalar, 1, 1, 2)
+        stage1(3)
+        quant_w1(1, 1, 0, 4)
+        phrases_early(2)
+        phrases_early(3)
+        for i in range(4, ROW_TILES):
+            stage1(i)
+        z_bf[0] = sb("z_bf0", [P, PH * 2], F32, tag="reuse")
+        z_bf[1] = sb("z_bf1", [P, PH * 2], F32)
+        finish_early(0)
+        for i in range(4, ROW_TILES):
+            phrases_early(i)
+        for n in range(3):
+            early_pass(n, 0)
         finish_early(1)
-        early_pass(2, 0)
+        pick_first(0, late_first(0), EARLY, LATE)
         for i in range(ROW_TILES):
-            gather_h(i, late_slot(i), EARLY, LATE)
-        turn_late(0, banks[6], banks[7])
+            if i + 1 < ROW_TILES:
+                pick_first(i + 1, late_first(i + 1), EARLY, LATE)
+            g, t = divmod(i, 4)
+            add_second(i, z_late(g)[:, t * LATE : (t + 1) * LATE], late_first(i), EARLY, LATE)
+            if i == 3:
+                finish_late(0)
         early_pass(0, 1)
-        turn_late(1, banks[6], banks[7])
+        finish_late(1)
         early_pass(1, 1)
         state_early(0)
         early_pass(2, 1)

@@ -21,9 +21,7 @@ BANK = 512
 PASSES = 2
 ROW_TILES = H // P
 OUT_TILES = N // P
-EARLY = 384
-LATE = PH - EARLY
-SPLIT = 2
+HALF = PH // 2
 
 
 def tile_list_phrase_tree_forget_kernel(
@@ -108,7 +106,7 @@ def tile_list_phrase_tree_forget_kernel(
         def gather_tab(dst, window, hf):
             nc.vector.tensor_copy(dst[:], window[:].indirect(offs_sb[:, 32 * hf : 32 * hf + 32]))
 
-        z_early = [sb("z_early0", [P, 3 * EARLY + 1024], F32), sb("z_early1", [P, 4 * EARLY], F32)]
+        z_early = [sb("z_early0", [P, 3 * HALF + 1024], F32)]
         w1_bf_own = {ga: sb("w1_bf%d%d" % ga, [P, 2048], BF16) for ga in ((0, 0), (0, 1), (1, 0))}
         w1_q = {(g, a): sb("w1_q%d%d" % (g, a), [P, BANK], U32, tag="reuse" if g + a == 2 else None)
                 for g in range(2) for a in range(PASSES)}
@@ -116,7 +114,7 @@ def tile_list_phrase_tree_forget_kernel(
 
         def w1_bf(g, a):
             if (g, a) == (1, 1):
-                return z_early[0][:, 3 * EARLY : 3 * EARLY + 1024].bitcast(BF16)
+                return z_early[0][:, 3 * HALF : 3 * HALF + 1024].bitcast(BF16)
             return w1_bf_own[(g, a)][:]
 
         def cast_w1(copy, g, a, t0):
@@ -150,7 +148,10 @@ def tile_list_phrase_tree_forget_kernel(
                     )
                 nc.scalar.copy(h_sb[i][:, hf * BANK : (hf + 1) * BANK], bank[:])
 
-        first = [sb("first%d" % r, [P, EARLY], F32) for r in range(2)]
+        first_early = [sb("first_early%d" % r, [P, HALF], F32, tag="last" if r == 1 else None) for r in range(2)]
+        gate_flat = sb("gate", [P, (OUT_TILES + 1) * PH], F32)
+        gate = gate_flat[:, 0 : OUT_TILES * PH].rearrange("p (n m) -> p n m", m=PH)
+        first_late = [gate_flat[:, 3 * PH + i * HALF : 3 * PH + (i + 1) * HALF] for i in range(ROW_TILES)]
 
         def pick_first(i, dst, m0, width):
             nc.vector.tensor_copy(dst, h_sb[i][:].indirect(pos1_sb[:, m0 // 16 : (m0 + width) // 16]))
@@ -160,12 +161,9 @@ def tile_list_phrase_tree_forget_kernel(
 
         def phrases_early(i):
             g, t = divmod(i, 4)
-            w = EARLY // SPLIT
-            for s in range(SPLIT):
-                pick_first(i, first[i % 2][:, s * w : (s + 1) * w], s * w, w)
-            for s in range(SPLIT):
-                add_second(i, z_early[g][:, t * EARLY + s * w : t * EARLY + (s + 1) * w],
-                           first[i % 2][:, s * w : (s + 1) * w], s * w, w)
+            pick_first(i, first_early[i % 2][:], 0, HALF)
+            pick_first(i, first_late[i], HALF, HALF)
+            add_second(i, z_early[g][:, t * HALF : (t + 1) * HALF], first_early[i % 2][:], 0, HALF)
 
         z_bf = {}
         z_q = [sb("z_q%d" % a, [P, PH], U32) for a in range(PASSES)]
@@ -173,7 +171,7 @@ def tile_list_phrase_tree_forget_kernel(
 
         def weave(a, src, m0, width):
             nc.scalar.copy(
-                z_bf[a][:, 2 * m0 : 2 * (m0 + width)].bitcast(BF16).rearrange("p (c i t) -> p c t i", i=2, t=4),
+                z_bf[(a, m0)].bitcast(BF16).rearrange("p (c i t) -> p c t i", i=2, t=4),
                 src.rearrange("p t (c i) -> p c t i", i=2),
             )
 
@@ -181,29 +179,14 @@ def tile_list_phrase_tree_forget_kernel(
             nc.vector.quantize_mx(
                 out=z_q[a][:, m0 : m0 + width].bitcast(FP8X4),
                 scales=z_sc[a][:, m0 : m0 + width],
-                in_=z_bf[a][:, 2 * m0 : 2 * (m0 + width)].bitcast(BF16),
+                in_=z_bf[(a, m0)].bitcast(BF16),
             )
 
-        def finish_early(a):
-            z4 = z_early[a][:, 0 : 4 * EARLY].rearrange("p (t m) -> p t m", t=4)
-            for m0, width in ((0, 256), (256, P)):
-                weave(a, z4[:, :, m0 : m0 + width], m0, width)
-                quant_z(a, m0, width)
-
-        z_late1 = sb("z_late1", [P, 4 * LATE], F32)
-
-        def z_late(a):
-            return z_late1[:] if a == 1 else z_bf[1][:, 0 : 4 * LATE]
-
-        def late_first(i):
-            return first[1][:, (i % 3) * LATE : (i % 3 + 1) * LATE]
-
-        def finish_late(a):
-            weave(a, z_late(a).rearrange("p (t m) -> p t m", t=4), EARLY, LATE)
-            quant_z(a, EARLY, LATE)
+        def finish(a, z, m0):
+            weave(a, z[:, 0 : 4 * HALF].rearrange("p (t m) -> p t m", t=4), m0, HALF)
+            quant_z(a, m0, HALF)
 
         content = sb("content", [P, OUT_TILES, PH], F32)
-        gate = sb("gate", [P, OUT_TILES, PH], F32)
         y_sb = [sb("y%d" % n, [P, PH], F32) for n in range(OUT_TILES)]
 
         def content_mm(dst, n, a, m0, start, stop):
@@ -226,37 +209,26 @@ def tile_list_phrase_tree_forget_kernel(
                 start=start, stop=stop,
             )
 
-        def early_pass(n, a):
-            bank_f, bank_c = (banks[b] for b in (2 * (n % 3), 2 * (n % 3) + 1))
-            forget_mm(bank_f[:, 0:256], n, a, 0, 256, a == 0, False)
-            forget_mm(bank_f[:, 256:EARLY], n, a, 256, P, False, a == 1)
+        def stage2_pass(n0, m0, a, bank_f, bank_c):
+            cols = slice(m0, m0 + HALF)
+            for d in range(2):
+                forget_mm(bank_f[:, d * HALF : (d + 1) * HALF], n0 + d, a, m0, HALF, a == 0 and d == 0, a == 1 and d == 1)
             if a == 1:
-                nc.scalar.activation(gate[:, n, 0:EARLY], bank_f[:, 0:EARLY], ACT.Sigmoid)
-            for c in range(EARLY // P):
-                content_mm(bank_c[:, c * P : (c + 1) * P], n, a, c * P, a == 0 and c == 0, a == 1 and c == EARLY // P - 1)
+                nc.scalar.activation(
+                    gate[:, n0 : n0 + 2, cols], bank_f[:].rearrange("p (d m) -> p d m", d=2), ACT.Sigmoid)
+            for c in range(4):
+                d, e = divmod(c, 2)
+                content_mm(bank_c[:, c * P : (c + 1) * P], n0 + d, a, m0 + e * P, a == 0 and c == 0, a == 1 and c == 3)
             if a == 1:
-                nc.scalar.activation(content[:, n, 0:EARLY], bank_c[:, 0:EARLY], ACT.Tanh)
+                nc.scalar.activation(
+                    content[:, n0 : n0 + 2, cols], bank_c[:].rearrange("p (d m) -> p d m", d=2), ACT.Tanh)
 
-        def state_early(n):
-            nc.vector.tensor_tensor(gate[:, n, 0:EARLY], gate[:, n, 0:EARLY], mem_sb[:, n, 0:EARLY], ALU.mult)
-            nc.vector.tensor_tensor(y_sb[n][:, 0:EARLY], gate[:, n, 0:EARLY], content[:, n, 0:EARLY], ALU.add)
-
-        def stage2_late(n0, bank):
-            for a in range(PASSES):
-                for d in range(2):
-                    forget_mm(bank[:, d * P : (d + 1) * P], n0 + d, a, EARLY, P, a == 0 and d == 0, False)
-                for d in range(2):
-                    content_mm(bank[:, (2 + d) * P : (3 + d) * P], n0 + d, a, EARLY, False, a == 1 and d == 1)
-            nc.scalar.activation(
-                gate[:, n0 : n0 + 2, EARLY:PH], bank[:, 0:256].rearrange("p (d m) -> p d m", d=2), ACT.Sigmoid)
-            nc.scalar.activation(
-                content[:, n0 : n0 + 2, EARLY:PH], bank[:, 256:512].rearrange("p (d m) -> p d m", d=2), ACT.Tanh)
-
-        def state_late(n0):
+        def state(n0, m0):
+            cols = slice(m0, m0 + HALF)
             nc.vector.tensor_tensor(
-                gate[:, n0 : n0 + 2, EARLY:PH], gate[:, n0 : n0 + 2, EARLY:PH], mem_sb[:, n0 : n0 + 2, EARLY:PH], ALU.mult)
+                gate[:, n0 : n0 + 2, cols], gate[:, n0 : n0 + 2, cols], mem_sb[:, n0 : n0 + 2, cols], ALU.mult)
             for n in (n0, n0 + 1):
-                nc.vector.tensor_tensor(y_sb[n][:, EARLY:PH], gate[:, n, EARLY:PH], content[:, n, EARLY:PH], ALU.add)
+                nc.vector.tensor_tensor(y_sb[n][:, cols], gate[:, n, cols], content[:, n, cols], ALU.add)
 
         second = [sb("second%d" % n, [P, CL], F32) for n in range(OUT_TILES)]
         result = [sb("result%d" % n, [P, CL], F32) for n in range(OUT_TILES)]
@@ -284,59 +256,52 @@ def tile_list_phrase_tree_forget_kernel(
         quant_w1(0, 1, 1, 1)
         quant_w1(0, 1, 2, 2)
         cast_w1(on_vector, 1, 0, 0)
+        quant_w1(1, 0, 0, 2)
         stage1(0)
         stage1(1)
         phrases_early(0)
         cast_w1(on_scalar, 1, 0, 2)
         stage1(2)
-        quant_w1(1, 0, 0, 4)
+        quant_w1(1, 0, 2, 2)
         phrases_early(1)
         cast_w1(on_scalar, 1, 1, 0)
         cast_w1(on_scalar, 1, 1, 2)
         stage1(3)
-        quant_w1(1, 1, 0, 4)
+        quant_w1(1, 1, 0, 2)
+        quant_w1(1, 1, 2, 2)
         phrases_early(2)
         phrases_early(3)
         for i in range(4, ROW_TILES):
             stage1(i)
-        z_bf[0] = sb("z_bf0", [P, PH * 2], F32, tag="reuse")
-        z_bf[1] = sb("z_bf1", [P, PH * 2], F32)
-        finish_early(0)
+        z_early.append(sb("z_early1", [P, 6 * HALF], F32, tag="reuse"))
+        z_bf[(0, 0)] = z_early[1][:, 4 * HALF : 6 * HALF]
+        z_bf[(0, HALF)] = sb("z_bf0_late", [P, 2 * HALF], F32)[:]
+        finish(0, z_early[0], 0)
         for i in range(4, ROW_TILES):
             phrases_early(i)
-        for n in range(3):
-            early_pass(n, 0)
-        finish_early(1)
-        pick_first(0, late_first(0), EARLY, LATE)
+        for j in range(3):
+            stage2_pass(2 * j, 0, 0, banks[2 * j], banks[2 * j + 1])
+        late = sb("late", [P, 4 * HALF], F32, tag="last")
+        z_late = [late[:], gate_flat[:, 4 * PH : 6 * PH]]
+        z_bf[(1, 0)] = late[:, 2 * HALF : 4 * HALF]
+        z_bf[(1, HALF)] = y_sb[2][:]
+        finish(1, z_early[1], 0)
         for i in range(ROW_TILES):
-            if i + 1 < ROW_TILES:
-                pick_first(i + 1, late_first(i + 1), EARLY, LATE)
             g, t = divmod(i, 4)
-            add_second(i, z_late(g)[:, t * LATE : (t + 1) * LATE], late_first(i), EARLY, LATE)
+            add_second(i, z_late[g][:, t * HALF : (t + 1) * HALF], first_late[i], HALF, HALF)
             if i == 3:
-                finish_late(0)
-        early_pass(0, 1)
-        finish_late(1)
-        early_pass(1, 1)
-        state_early(0)
-        early_pass(2, 1)
-        state_early(1)
-        stage2_late(0, banks[6])
-        early_pass(3, 0)
-        early_pass(3, 1)
-        state_early(2)
-        state_late(0)
-        clauses(0)
-        stage2_late(2, banks[7])
-        early_pass(4, 0)
-        early_pass(4, 1)
-        state_early(3)
-        state_late(2)
-        clauses(2)
-        early_pass(5, 0)
-        early_pass(5, 1)
-        stage2_late(4, banks[6])
-        state_early(4)
-        state_early(5)
-        state_late(4)
-        clauses(4)
+                finish(0, z_late[0], HALF)
+        for j in range(2):
+            stage2_pass(2 * j, 0, 1, banks[2 * j], banks[2 * j + 1])
+        stage2_pass(0, HALF, 0, banks[6], banks[7])
+        finish(1, z_late[1], HALF)
+        stage2_pass(4, 0, 1, banks[4], banks[5])
+        for j in range(3):
+            state(2 * j, 0)
+        stage2_pass(0, HALF, 1, banks[6], banks[7])
+        for j in (1, 2):
+            for a in range(PASSES):
+                stage2_pass(2 * j, HALF, a, banks[2 * j - 2], banks[2 * j - 1])
+        for j in range(3):
+            state(2 * j, HALF)
+            clauses(2 * j)

@@ -22,6 +22,7 @@ PASSES = 2
 ROW_TILES = H // P
 OUT_TILES = N // P
 HALF = PH // 2
+QUARTER = HALF // 2
 
 
 def tile_list_phrase_tree_forget_kernel(
@@ -41,7 +42,7 @@ def tile_list_phrase_tree_forget_kernel(
         offs_sb = sb("offs_sb", [P, S // 16], U16)
         nc.sync.dma_start(offs_sb[:], offs)
         tab_sc = sb("tab_sc", [P, T], U8)
-        nc.vector.memset(tab_sc[:].bitcast(I32), 0)
+        nc.gpsimd.memset(tab_sc[:].bitcast(I32), 0)
         for q in range(4):
             nc.sync.dma_start(
                 tab_sc[32 * q : 32 * q + 8, :].bitcast(I32),
@@ -49,9 +50,6 @@ def tile_list_phrase_tree_forget_kernel(
             )
         w2_sc = sb("w2_sc", [P, PASSES, N], U8)
         nc.gpsimd.memset(w2_sc[:].rearrange("p a c -> p (a c)").bitcast(I32), 0)
-        warm = sb("warm", [P, 16], F32)
-        nc.gpsimd.memset(warm[:, 0:1], 0.0)
-        nc.scalar.activation(warm[:, 8:9], warm[:, 0:1], ACT.Sigmoid)
 
         tab_w = [sb("tab_w%d" % a, [P, T], U32) for a in range(PASSES)]
 
@@ -61,24 +59,29 @@ def tile_list_phrase_tree_forget_kernel(
                 tab_words[a].rearrange("p t i -> p (t i)").bitcast(I32),
             )
 
-        w1_raw = {(g, a): sb("w1_raw%d%d" % (g, a), [P, 4, BANK], F32) for g in range(2) for a in range(PASSES)}
-
-        def load_w1(g, a):
+        def load_w1(name, a, c0, width):
+            raw = sb(name, [P, 4, width], F32)
             nc.sync.dma_start(
-                w1_raw[(g, a)][:],
-                w1[512 * a : 512 * (a + 1), 512 * g : 512 * (g + 1)].rearrange("(p j) c -> p j c", j=4),
-            )
+                raw[:], w1[512 * a : 512 * (a + 1), c0 : c0 + width].rearrange("(p j) c -> p j c", j=4))
+            return raw
+
+        low_raw = {}
+
+        def load_low(i):
+            for a in range(PASSES):
+                low_raw[(i, a)] = load_w1("low_raw%d%d" % (i, a), a, i * P, P)
 
         load_tab(0)
-        load_w1(0, 0)
+        load_low(0)
         load_tab(1)
-        load_w1(0, 1)
+        load_low(1)
         pos1_sb = sb("pos1_sb", [P, PH // 16], U16)
         pos2_sb = sb("pos2_sb", [P, PH // 16], U16)
         nc.sync.dma_start(pos1_sb[:], pos1)
         nc.sync.dma_start(pos2_sb[:], pos2)
-        load_w1(1, 0)
-        load_w1(1, 1)
+        load_low(2)
+        load_low(3)
+        high_raw = [load_w1("high_raw%d" % a, a, 512, 512) for a in range(PASSES)]
 
         for q in range(4):
             nc.sync.dma_start(
@@ -93,65 +96,73 @@ def tile_list_phrase_tree_forget_kernel(
         nc.sync.dma_start(wc_sb[:].bitcast(I32), wc_words.rearrange("a p c -> p a c").bitcast(I32))
         wf_sb = sb("wf_sb", [P, PASSES, N], U32)
         nc.sync.dma_start(wf_sb[:].bitcast(I32), wf_words.rearrange("a p c i -> p a (c i)").bitcast(I32))
-        mem_sb = sb("mem_sb", [P, OUT_TILES, PH], F32)
-        nc.sync.dma_start(mem_sb[:], mem.rearrange("(n p) m -> p n m", p=P))
         pos3_sb = sb("pos3_sb", [P, CL // 16], U16)
         pos4_sb = sb("pos4_sb", [P, CL // 16], U16)
         nc.sync.dma_start(pos3_sb[:], pos3)
         nc.sync.dma_start(pos4_sb[:], pos4)
 
-        v_sc = [sb("v_sc%d" % hf, [P, BANK], U8) for hf in range(2)]
-        v_w = [[sb("v_w%d%d" % (a, hf), [P, BANK], U32) for hf in range(2)] for a in range(PASSES)]
+        v_sc = sb("v_sc", [P, S], U8)
+        v_w0 = sb("v_w0", [P, S], U32)
+        v_w1 = [sb("v_w1%d" % hf, [P, BANK], U32) for hf in range(2)]
 
-        def gather_tab(dst, window, hf):
-            nc.vector.tensor_copy(dst[:], window[:].indirect(offs_sb[:, 32 * hf : 32 * hf + 32]))
+        def weave(copy, dst, src):
+            copy(dst.rearrange("p (c i t) -> p c t i", i=2, t=4), src.rearrange("p t (c i) -> p c t i", i=2))
 
-        z_early = [sb("z_early0", [P, 3 * HALF + 1024], F32)]
-        w1_bf_own = {ga: sb("w1_bf%d%d" % ga, [P, 2048], BF16) for ga in ((0, 0), (0, 1), (1, 0))}
-        w1_q = {(g, a): sb("w1_q%d%d" % (g, a), [P, BANK], U32, tag="reuse" if g + a == 2 else None)
-                for g in range(2) for a in range(PASSES)}
-        w1_sc = {(g, a): sb("w1_sc%d%d" % (g, a), [P, BANK], U8) for g in range(2) for a in range(PASSES)}
+        def quantize(codes, scales, src):
+            nc.vector.quantize_mx(out=codes.bitcast(FP8X4), scales=scales, in_=src)
 
-        def w1_bf(g, a):
-            if (g, a) == (1, 1):
-                return z_early[0][:, 3 * HALF : 3 * HALF + 1024].bitcast(BF16)
-            return w1_bf_own[(g, a)][:]
+        first_low = [sb("first_low%d" % r, [P, PH], F32) for r in range(2)]
+        first_low.append(first_low[0])
+        low_bf = [sb("low_bf%d" % i, [P, 1024], BF16)[:] for i in range(4)]
+        low_q = [sb("low_q%d" % i, [P, PASSES * P], U32) for i in range(4)]
+        low_sc = [sb("low_sc%d" % i, [P, PASSES * P], U8) for i in range(4)]
 
-        def cast_w1(copy, g, a, t0):
-            copy(
-                w1_bf(g, a)[:, t0 * 512 : (t0 + 2) * 512].rearrange("p (t m j) -> p m j t", t=2, j=4),
-                w1_raw[(g, a)][:].rearrange("p j (m t) -> p m j t", t=4)[:, :, :, t0 : t0 + 2],
+        def prepare_low(copy, i):
+            for a in range(PASSES):
+                weave(copy, low_bf[i][:, a * 512 : (a + 1) * 512], low_raw[(i, a)][:])
+            quantize(low_q[i][:], low_sc[i][:], low_bf[i])
+
+        early = sb("early", [P, 7 * HALF], F32)
+        z_early = early[:, 0 : 4 * HALF].rearrange("p (t m) -> p t m", t=4)
+        low_z_bf = early[:, 3 * HALF : 7 * HALF].bitcast(BF16)
+        high_bf = [sb("high_bf%d" % u, [P, 2048], BF16, tag="then_mem" if u == 0 else None)[:] for u in range(2)]
+        high_q = [sb("high_q%d" % u, [P, BANK], U32) for u in range(2)]
+        high_sc = [sb("high_sc%d" % u, [P, BANK], U8) for u in range(2)]
+
+        def round_high(u, a):
+            nc.scalar.copy(
+                high_bf[u][:, a * 1024 : (a + 1) * 1024].rearrange("p (t m j) -> p m j t", t=2, j=4),
+                high_raw[a][:].rearrange("p j (m t) -> p m j t", t=4)[:, :, :, 2 * u : 2 * u + 2],
             )
 
-        def quant_w1(g, a, t0, tiles):
-            nc.vector.quantize_mx(
-                out=w1_q[(g, a)][:, t0 * P : (t0 + tiles) * P].bitcast(FP8X4),
-                scales=w1_sc[(g, a)][:, t0 * P : (t0 + tiles) * P],
-                in_=w1_bf(g, a)[:, t0 * 512 : (t0 + tiles) * 512],
-            )
+        def quant_high(u):
+            quantize(high_q[u][:], high_sc[u][:], high_bf[u])
 
-        h_sb = [sb("h%d" % i, [P, S], F32) for i in range(ROW_TILES)]
+        def stationary(i, a):
+            if i < 4:
+                return low_q[i], low_sc[i], a * P
+            return high_q[(i - 4) // 2], high_sc[(i - 4) // 2], a * 2 * P + (i % 2) * P
+
+        h_sb = []
 
         def stage1(i):
-            g, t = divmod(i, 4)
+            h_sb.append(sb("h%d" % i, [P, S], F32, tag="low_raw%d1" % (i + 2) if i < 2 else None))
             for hf in range(2):
-                bank = banks[2 * t + hf]
+                bank = banks[2 * (i % 4) + hf]
+                cols = slice(hf * BANK, (hf + 1) * BANK)
                 for a in range(PASSES):
+                    codes, scales, c0 = stationary(i, a)
+                    moving = v_w0[:, cols] if a == 0 else v_w1[hf][:]
                     nc.tensor.matmul_mx(
                         out=bank[:],
-                        lhsT=w1_q[(g, a)][:, t * P : (t + 1) * P].bitcast(FP8X4),
-                        lhsT_scale=w1_sc[(g, a)][:, t * P : (t + 1) * P],
-                        rhs=v_w[a][hf][:].bitcast(FP8X4),
-                        rhs_scale=v_sc[hf][4 * a : P, :],
+                        lhsT=codes[:, c0 : c0 + P].bitcast(FP8X4),
+                        lhsT_scale=scales[:, c0 : c0 + P],
+                        rhs=moving.bitcast(FP8X4),
+                        rhs_scale=v_sc[4 * a : P, cols],
                         start=(a == 0),
                         stop=(a == PASSES - 1),
                     )
-                nc.scalar.copy(h_sb[i][:, hf * BANK : (hf + 1) * BANK], bank[:])
-
-        first_early = [sb("first_early%d" % r, [P, HALF], F32, tag="last" if r == 1 else None) for r in range(2)]
-        gate_flat = sb("gate", [P, (OUT_TILES + 1) * PH], F32)
-        gate = gate_flat[:, 0 : OUT_TILES * PH].rearrange("p (n m) -> p n m", m=PH)
-        first_late = [gate_flat[:, 3 * PH + i * HALF : 3 * PH + (i + 1) * HALF] for i in range(ROW_TILES)]
+                nc.scalar.copy(h_sb[i][:, cols], bank[:])
 
         def pick_first(i, dst, m0, width):
             nc.vector.tensor_copy(dst, h_sb[i][:].indirect(pos1_sb[:, m0 // 16 : (m0 + width) // 16]))
@@ -159,76 +170,62 @@ def tile_list_phrase_tree_forget_kernel(
         def add_second(i, dst, src, m0, width):
             nc.vector.tensor_tensor(dst, h_sb[i][:].indirect(pos2_sb[:, m0 // 16 : (m0 + width) // 16]), src, ALU.add)
 
-        def phrases_early(i):
-            g, t = divmod(i, 4)
-            pick_first(i, first_early[i % 2][:], 0, HALF)
-            pick_first(i, first_late[i], HALF, HALF)
-            add_second(i, z_early[g][:, t * HALF : (t + 1) * HALF], first_early[i % 2][:], 0, HALF)
+        z_rows = [sb("z_rows%d" % i, [P, PH], F32) for i in range(4)]
+        z_low = sb("z_low", [P, 4, PH], F32)
 
-        z_bf = {}
+        def phrases_low(i):
+            for m0 in (0, HALF):
+                pick_first(i, first_low[i][:, m0 : m0 + HALF], m0, HALF)
+            for m0 in (0, HALF):
+                add_second(i, z_rows[i][:, m0 : m0 + HALF], first_low[i][:, m0 : m0 + HALF], m0, HALF)
+            for t in range(4):
+                nc.sync.dma_start(z_low[32 * i : 32 * i + 32, t, :], z_rows[i][t:P:4, :])
+
+        late_picks = sb("late_picks", [P, 3 * HALF], F32)
+        first_late = [late_picks[:, t * HALF : (t + 1) * HALF] for t in range(3)] + [early[:, 4 * HALF : 5 * HALF]]
+        first_even = sb("first_even", [P, HALF], F32)
+        first_early = [first_even[:], late_picks[:, QUARTER : 3 * QUARTER]]
+
+        def pick_late(t, c0, width):
+            pick_first(4 + t, first_late[t][:, c0 : c0 + width], HALF + c0, width)
+
+        def pick_early(t):
+            pick_first(4 + t, first_early[t % 2], 0, HALF)
+
+        def add_early(t):
+            add_second(4 + t, z_early[:, t, :], first_early[t % 2], 0, HALF)
+
         z_q = [sb("z_q%d" % a, [P, PH], U32) for a in range(PASSES)]
         z_sc = [sb("z_sc%d" % a, [P, PH], U8) for a in range(PASSES)]
 
-        def weave(a, src, m0, width):
-            nc.scalar.copy(
-                z_bf[(a, m0)].bitcast(BF16).rearrange("p (c i t) -> p c t i", i=2, t=4),
-                src.rearrange("p t (c i) -> p c t i", i=2),
-            )
+        def quant_z(m0, src):
+            quantize(z_q[1][:, m0 : m0 + HALF], z_sc[1][:, m0 : m0 + HALF], src)
 
-        def quant_z(a, m0, width):
-            nc.vector.quantize_mx(
-                out=z_q[a][:, m0 : m0 + width].bitcast(FP8X4),
-                scales=z_sc[a][:, m0 : m0 + width],
-                in_=z_bf[(a, m0)].bitcast(BF16),
-            )
-
-        def finish(a, z, m0):
-            weave(a, z[:, 0 : 4 * HALF].rearrange("p (t m) -> p t m", t=4), m0, HALF)
-            quant_z(a, m0, HALF)
-
-        content = sb("content", [P, OUT_TILES, PH], F32)
         y_sb = [sb("y%d" % n, [P, PH], F32) for n in range(OUT_TILES)]
 
-        def content_mm(dst, n, a, m0, start, stop):
-            nc.tensor.matmul_mx(
-                out=dst,
-                lhsT=wc_sb[:, a, 2 * n * P : 2 * (n + 1) * P].bitcast(FP4X4),
-                lhsT_scale=w2_sc[:, a, n * P : (n + 1) * P],
-                rhs=z_q[a][:, m0 : m0 + P].bitcast(FP8X4),
-                rhs_scale=z_sc[a][:, m0 : m0 + P],
-                start=start, stop=stop,
-            )
-
-        def forget_mm(dst, n, a, m0, width, start, stop):
-            nc.tensor.matmul_mx(
-                out=dst,
-                lhsT=wf_sb[:, a, n * P : (n + 1) * P].bitcast(FP8X4),
-                lhsT_scale=w2_sc[4:P, a, n * P : (n + 1) * P],
-                rhs=z_q[a][:, m0 : m0 + width].bitcast(FP8X4),
-                rhs_scale=z_sc[a][:, m0 : m0 + width],
-                start=start, stop=stop,
-            )
-
-        def stage2_pass(n0, m0, a, bank_f, bank_c):
-            cols = slice(m0, m0 + HALF)
+        def forget_mm(n0, m0, a, bank):
             for d in range(2):
-                forget_mm(bank_f[:, d * HALF : (d + 1) * HALF], n0 + d, a, m0, HALF, a == 0 and d == 0, a == 1 and d == 1)
-            if a == 1:
-                nc.scalar.activation(
-                    gate[:, n0 : n0 + 2, cols], bank_f[:].rearrange("p (d m) -> p d m", d=2), ACT.Sigmoid)
-            for c in range(4):
-                d, e = divmod(c, 2)
-                content_mm(bank_c[:, c * P : (c + 1) * P], n0 + d, a, m0 + e * P, a == 0 and c == 0, a == 1 and c == 3)
-            if a == 1:
-                nc.scalar.activation(
-                    content[:, n0 : n0 + 2, cols], bank_c[:].rearrange("p (d m) -> p d m", d=2), ACT.Tanh)
+                n = n0 + d
+                nc.tensor.matmul_mx(
+                    out=bank[:, d * HALF : (d + 1) * HALF],
+                    lhsT=wf_sb[:, a, n * P : (n + 1) * P].bitcast(FP8X4),
+                    lhsT_scale=w2_sc[4:P, a, n * P : (n + 1) * P],
+                    rhs=z_q[a][:, m0 : m0 + HALF].bitcast(FP8X4),
+                    rhs_scale=z_sc[a][:, m0 : m0 + HALF],
+                    start=(a == 0 and d == 0), stop=(a == 1 and d == 1),
+                )
 
-        def state(n0, m0):
-            cols = slice(m0, m0 + HALF)
-            nc.vector.tensor_tensor(
-                gate[:, n0 : n0 + 2, cols], gate[:, n0 : n0 + 2, cols], mem_sb[:, n0 : n0 + 2, cols], ALU.mult)
-            for n in (n0, n0 + 1):
-                nc.vector.tensor_tensor(y_sb[n][:, cols], gate[:, n, cols], content[:, n, cols], ALU.add)
+        def content_mm(n0, m0, a, bank):
+            for c in range(4):
+                n, m = n0 + c // 2, m0 + (c % 2) * P
+                nc.tensor.matmul_mx(
+                    out=bank[:, c * P : (c + 1) * P],
+                    lhsT=wc_sb[:, a, 2 * n * P : 2 * (n + 1) * P].bitcast(FP4X4),
+                    lhsT_scale=w2_sc[:, a, n * P : (n + 1) * P],
+                    rhs=z_q[a][:, m : m + P].bitcast(FP8X4),
+                    rhs_scale=z_sc[a][:, m : m + P],
+                    start=(a == 0 and c == 0), stop=(a == 1 and c == 3),
+                )
 
         second = [sb("second%d" % n, [P, CL], F32) for n in range(OUT_TILES)]
         result = [sb("result%d" % n, [P, CL], F32) for n in range(OUT_TILES)]
@@ -240,68 +237,122 @@ def tile_list_phrase_tree_forget_kernel(
                 nc.vector.tensor_tensor(result[n][:], y_sb[n][:].indirect(pos3_sb[:]), second[n][:], ALU.subtract)
                 nc.sync.dma_start(out[n * P : (n + 1) * P, :], result[n][:])
 
-        on_scalar, on_vector = nc.scalar.copy, nc.vector.tensor_copy
-        gather_tab(v_w[0][0], tab_w[0], 0)
-        gather_tab(v_w[0][1], tab_w[0], 1)
-        gather_tab(v_sc[0], tab_sc, 0)
-        gather_tab(v_sc[1], tab_sc, 1)
-        cast_w1(on_scalar, 0, 0, 0)
-        cast_w1(on_vector, 0, 0, 2)
-        quant_w1(0, 0, 0, 4)
-        gather_tab(v_w[1][0], tab_w[1], 0)
-        gather_tab(v_w[1][1], tab_w[1], 1)
-        cast_w1(on_vector, 0, 1, 0)
-        cast_w1(on_scalar, 0, 1, 2)
-        quant_w1(0, 1, 0, 1)
-        quant_w1(0, 1, 1, 1)
-        quant_w1(0, 1, 2, 2)
-        cast_w1(on_vector, 1, 0, 0)
-        quant_w1(1, 0, 0, 2)
+        nc.vector.tensor_copy(v_w0[:], tab_w[0][:].indirect(offs_sb[:]))
+        nc.vector.tensor_copy(v_sc[:], tab_sc[:].indirect(offs_sb[:]))
+        prepare_low(nc.scalar.copy, 0)
+        for hf in range(2):
+            nc.vector.tensor_copy(v_w1[hf][:], tab_w[1][:].indirect(offs_sb[:, 32 * hf : 32 * hf + 32]))
+        prepare_low(nc.vector.tensor_copy, 1)
+        prepare_low(nc.scalar.copy, 2)
         stage1(0)
+        prepare_low(nc.scalar.copy, 3)
+        phrases_low(0)
         stage1(1)
-        phrases_early(0)
-        cast_w1(on_scalar, 1, 0, 2)
+        round_high(0, 0)
+        phrases_low(1)
         stage1(2)
-        quant_w1(1, 0, 2, 2)
-        phrases_early(1)
-        cast_w1(on_scalar, 1, 1, 0)
-        cast_w1(on_scalar, 1, 1, 2)
+        round_high(0, 1)
+        quant_high(0)
+        phrases_low(2)
         stage1(3)
-        quant_w1(1, 1, 0, 2)
-        quant_w1(1, 1, 2, 2)
-        phrases_early(2)
-        phrases_early(3)
+        round_high(1, 0)
+        round_high(1, 1)
+        quant_high(1)
+        first_low.append(sb("first_low3", [P, PH], F32, tag="then_mem"))
+        phrases_low(3)
         for i in range(4, ROW_TILES):
             stage1(i)
-        z_early.append(sb("z_early1", [P, 6 * HALF], F32, tag="reuse"))
-        z_bf[(0, 0)] = z_early[1][:, 4 * HALF : 6 * HALF]
-        z_bf[(0, HALF)] = sb("z_bf0_late", [P, 2 * HALF], F32)[:]
-        finish(0, z_early[0], 0)
-        for i in range(4, ROW_TILES):
-            phrases_early(i)
+
+        mem_sb = sb("mem_sb", [P, OUT_TILES, PH], F32, tag="then_mem")
+        nc.sync.dma_start(mem_sb[:], mem.rearrange("(n p) m -> p n m", p=P))
+        content = sb("content", [P, OUT_TILES, PH], F32, tag="high_raw0")
+        gate = sb("gate", [P, OUT_TILES, PH], F32, tag="high_raw1")
+
+        def gate_act(n0, m0, bank):
+            nc.scalar.activation(
+                gate[:, n0 : n0 + 2, m0 : m0 + HALF], bank[:].rearrange("p (d m) -> p d m", d=2), ACT.Tanh, scale=0.5)
+
+        def content_act(n0, m0, bank):
+            nc.scalar.activation(
+                content[:, n0 : n0 + 2, m0 : m0 + HALF], bank[:].rearrange("p (d m) -> p d m", d=2), ACT.Tanh)
+
+        def gated_mem(n0, m0):
+            part = gate[:, n0 : n0 + 2, m0 : m0 + HALF]
+            nc.vector.scalar_tensor_tensor(
+                part, part, 1.0, mem_sb[:, n0 : n0 + 2, m0 : m0 + HALF], ALU.add, ALU.mult)
+
+        def state(n0, m0):
+            cols = slice(m0, m0 + HALF)
+            for n in (n0, n0 + 1):
+                nc.vector.scalar_tensor_tensor(
+                    y_sb[n][:, cols], gate[:, n, cols], 0.5, content[:, n, cols], ALU.mult, ALU.add)
+
+        for t in range(2):
+            pick_early(t)
+            pick_late(t, t * QUARTER, QUARTER)
+            add_early(t)
+        pick_early(2)
+        pick_late(2, 0, HALF)
+        add_early(2)
+        pick_early(3)
+        weave(nc.scalar.copy, low_z_bf, z_low[:])
+        quantize(z_q[0][:], z_sc[0][:], low_z_bf)
+        add_early(3)
         for j in range(3):
-            stage2_pass(2 * j, 0, 0, banks[2 * j], banks[2 * j + 1])
-        late = sb("late", [P, 4 * HALF], F32, tag="last")
-        z_late = [late[:], gate_flat[:, 4 * PH : 6 * PH]]
-        z_bf[(1, 0)] = late[:, 2 * HALF : 4 * HALF]
-        z_bf[(1, HALF)] = y_sb[2][:]
-        finish(1, z_early[1], 0)
-        for i in range(ROW_TILES):
-            g, t = divmod(i, 4)
-            add_second(i, z_late[g][:, t * HALF : (t + 1) * HALF], first_late[i], HALF, HALF)
-            if i == 3:
-                finish(0, z_late[0], HALF)
-        for j in range(2):
-            stage2_pass(2 * j, 0, 1, banks[2 * j], banks[2 * j + 1])
-        stage2_pass(0, HALF, 0, banks[6], banks[7])
-        finish(1, z_late[1], HALF)
-        stage2_pass(4, 0, 1, banks[4], banks[5])
+            forget_mm(2 * j, 0, 0, banks[2 * j])
+            content_mm(2 * j, 0, 0, banks[2 * j + 1])
+
+        late = sb("late", [P, 4 * HALF], F32)
+        z_late = late[:].rearrange("p (t m) -> p t m", t=4)
+        early_bf = late[:, 3 * QUARTER : 7 * QUARTER].bitcast(BF16)
+        weave(nc.scalar.copy, early_bf, z_early)
+
+        def late_add(t):
+            add_second(4 + t, z_late[:, t, :], first_late[t], HALF, HALF)
+
+        for t in range(2):
+            pick_late(t, (1 - t) * QUARTER, QUARTER)
+        pick_late(3, 0, HALF)
+        late_add(0)
+        quant_z(0, early_bf)
+        for t in range(1, 4):
+            late_add(t)
         for j in range(3):
-            state(2 * j, 0)
-        stage2_pass(0, HALF, 1, banks[6], banks[7])
+            forget_mm(2 * j, 0, 1, banks[2 * j])
+            content_mm(2 * j, 0, 1, banks[2 * j + 1])
+        forget_mm(0, HALF, 0, banks[6])
+        content_mm(0, HALF, 0, banks[7])
+
+        gate_act(0, 0, banks[0])
+        content_act(0, 0, banks[1])
+        gate_act(2, 0, banks[2])
+        late_bf = sb("late_bf", [P, 4 * HALF], BF16)
+        weave(nc.scalar.copy, late_bf[:], z_late)
+        content_act(2, 0, banks[3])
+        gate_act(4, 0, banks[4])
+        content_act(4, 0, banks[5])
+        gated_mem(0, 0)
+        gated_mem(2, 0)
+        state(0, 0)
+        quant_z(HALF, late_bf[:])
+        gated_mem(4, 0)
+        state(2, 0)
+        state(4, 0)
+
+        late_banks = ((6, 7), (0, 1), (2, 3))
+        forget_mm(0, HALF, 1, banks[6])
+        content_mm(0, HALF, 1, banks[7])
         for j in (1, 2):
             for a in range(PASSES):
-                stage2_pass(2 * j, HALF, a, banks[2 * j - 2], banks[2 * j - 1])
+                forget_mm(2 * j, HALF, a, banks[late_banks[j][0]])
+            for a in range(PASSES):
+                content_mm(2 * j, HALF, a, banks[late_banks[j][1]])
         for j in range(3):
+            gate_act(2 * j, HALF, banks[late_banks[j][0]])
+            content_act(2 * j, HALF, banks[late_banks[j][1]])
+        gated_mem(0, HALF)
+        for j in range(3):
+            if j < 2:
+                gated_mem(2 * j + 2, HALF)
             state(2 * j, HALF)
             clauses(2 * j)

@@ -48,9 +48,6 @@ def tile_list_phrase_tree_forget_kernel(
                 tab_sc[32 * q : 32 * q + 8, :].bitcast(I32),
                 tab_scales[:, 4 * q : 4 * q + 4, :].bitcast(I32),
             )
-        w2_sc = sb("w2_sc", [P, PASSES, N], U8)
-        nc.gpsimd.memset(w2_sc[:].rearrange("p a c -> p (a c)").bitcast(I32), 0)
-
         tab_w = [sb("tab_w%d" % a, [P, T], U32) for a in range(PASSES)]
 
         def load_tab(a):
@@ -59,30 +56,27 @@ def tile_list_phrase_tree_forget_kernel(
                 tab_words[a].rearrange("p t i -> p (t i)").bitcast(I32),
             )
 
-        def load_w1(name, a, c0, width):
-            raw = sb(name, [P, 4, width], F32)
-            nc.sync.dma_start(
-                raw[:], w1[512 * a : 512 * (a + 1), c0 : c0 + width].rearrange("(p j) c -> p j c", j=4))
+        def load_w1(name, c0, width):
+            raw = sb(name, [P, PASSES * 4 * width], F32)[:].rearrange("p (a j c) -> p a j c", a=PASSES, j=4)
+            for a in range(PASSES):
+                nc.sync.dma_start(
+                    raw[:, a], w1[512 * a : 512 * (a + 1), c0 : c0 + width].rearrange("(p j) c -> p j c", j=4))
             return raw
 
-        low_raw = {}
-
-        def load_low(i):
-            for a in range(PASSES):
-                low_raw[(i, a)] = load_w1("low_raw%d%d" % (i, a), a, i * P, P)
+        def load_list(name, src, entries):
+            tile = sb(name, [P, entries // 16], U16)
+            nc.sync.dma_start(tile[:], src)
+            return tile
 
         load_tab(0)
-        load_low(0)
+        first_raw = load_w1("first_raw", 0, P)
         load_tab(1)
-        load_low(1)
-        pos1_sb = sb("pos1_sb", [P, PH // 16], U16)
-        pos2_sb = sb("pos2_sb", [P, PH // 16], U16)
-        nc.sync.dma_start(pos1_sb[:], pos1)
-        nc.sync.dma_start(pos2_sb[:], pos2)
-        load_low(2)
-        load_low(3)
-        high_raw = [load_w1("high_raw%d" % a, a, 512, 512) for a in range(PASSES)]
-
+        low_raw = load_w1("low_raw", P, 3 * P)
+        pos1_sb = load_list("pos1_sb", pos1, PH)
+        pos2_sb = load_list("pos2_sb", pos2, PH)
+        high_raw = load_w1("high_raw", 512, 512)
+        w2_sc = sb("w2_sc", [P, PASSES, N], U8)
+        nc.gpsimd.memset(w2_sc[:].rearrange("p a c -> p (a c)").bitcast(I32), 0)
         for q in range(4):
             nc.sync.dma_start(
                 w2_sc[32 * q : 32 * q + 4, :, :].bitcast(I32),
@@ -96,46 +90,49 @@ def tile_list_phrase_tree_forget_kernel(
         nc.sync.dma_start(wc_sb[:].bitcast(I32), wc_words.rearrange("a p c -> p a c").bitcast(I32))
         wf_sb = sb("wf_sb", [P, PASSES, N], U32)
         nc.sync.dma_start(wf_sb[:].bitcast(I32), wf_words.rearrange("a p c i -> p a (c i)").bitcast(I32))
-        pos3_sb = sb("pos3_sb", [P, CL // 16], U16)
-        pos4_sb = sb("pos4_sb", [P, CL // 16], U16)
-        nc.sync.dma_start(pos3_sb[:], pos3)
-        nc.sync.dma_start(pos4_sb[:], pos4)
+
+        pos3_sb = load_list("pos3_sb", pos3, CL)
+        pos4_sb = load_list("pos4_sb", pos4, CL)
 
         v_sc = sb("v_sc", [P, S], U8)
         v_w0 = sb("v_w0", [P, S], U32)
         v_w1 = [sb("v_w1%d" % hf, [P, BANK], U32) for hf in range(2)]
 
         def weave(copy, dst, src):
-            copy(dst.rearrange("p (c i t) -> p c t i", i=2, t=4), src.rearrange("p t (c i) -> p c t i", i=2))
+            copy(dst.rearrange("p (c i t) -> p c t i", i=4, t=4), src.rearrange("p t (c i) -> p c t i", i=4))
 
         def quantize(codes, scales, src):
             nc.vector.quantize_mx(out=codes.bitcast(FP8X4), scales=scales, in_=src)
 
-        first_low = [sb("first_low%d" % r, [P, PH], F32) for r in range(2)]
-        first_low.append(first_low[0])
         low_bf = [sb("low_bf%d" % i, [P, 1024], BF16)[:] for i in range(4)]
         low_q = [sb("low_q%d" % i, [P, PASSES * P], U32) for i in range(4)]
         low_sc = [sb("low_sc%d" % i, [P, PASSES * P], U8) for i in range(4)]
 
-        def prepare_low(copy, i):
-            for a in range(PASSES):
-                weave(copy, low_bf[i][:, a * 512 : (a + 1) * 512], low_raw[(i, a)][:])
+        def round_low(copy, i):
+            dst = low_bf[i].rearrange("p (a c i t) -> p a c t i", a=PASSES, i=4, t=4)
+            raw = first_raw if i == 0 else low_raw[:, :, :, (i - 1) * P : i * P]
+            src = raw.rearrange("p a t (c i) -> p a c t i", i=4)
+            if i == 0:
+                for a in range(PASSES):
+                    copy(dst[:, a], src[:, a])
+            else:
+                copy(dst, src)
+
+        def quant_low(i):
             quantize(low_q[i][:], low_sc[i][:], low_bf[i])
 
-        early = sb("early", [P, 7 * HALF], F32)
+        early = sb("early", [P, 5 * HALF], F32)
         z_early = early[:, 0 : 4 * HALF].rearrange("p (t m) -> p t m", t=4)
-        low_z_bf = early[:, 3 * HALF : 7 * HALF].bitcast(BF16)
+        low_z_bf = early[:, 3 * HALF : 5 * HALF].bitcast(BF16)
         high_bf = [sb("high_bf%d" % u, [P, 2048], BF16, tag="then_mem" if u == 0 else None)[:] for u in range(2)]
         high_q = [sb("high_q%d" % u, [P, BANK], U32) for u in range(2)]
         high_sc = [sb("high_sc%d" % u, [P, BANK], U8) for u in range(2)]
 
-        def round_high(u, a):
+        def prepare_high(u):
             nc.scalar.copy(
-                high_bf[u][:, a * 1024 : (a + 1) * 1024].rearrange("p (t m j) -> p m j t", t=2, j=4),
-                high_raw[a][:].rearrange("p j (m t) -> p m j t", t=4)[:, :, :, 2 * u : 2 * u + 2],
+                high_bf[u].rearrange("p (a t m j) -> p a m j t", a=PASSES, t=2, j=4),
+                high_raw.rearrange("p a j (m t) -> p a m j t", t=4)[:, :, :, :, 2 * u : 2 * u + 2],
             )
-
-        def quant_high(u):
             quantize(high_q[u][:], high_sc[u][:], high_bf[u])
 
         def stationary(i, a):
@@ -146,7 +143,7 @@ def tile_list_phrase_tree_forget_kernel(
         h_sb = []
 
         def stage1(i):
-            h_sb.append(sb("h%d" % i, [P, S], F32, tag="low_raw%d1" % (i + 2) if i < 2 else None))
+            h_sb.append(sb("h%d" % i, [P, S], F32))
             for hf in range(2):
                 bank = banks[2 * (i % 4) + hf]
                 cols = slice(hf * BANK, (hf + 1) * BANK)
@@ -170,7 +167,7 @@ def tile_list_phrase_tree_forget_kernel(
         def add_second(i, dst, src, m0, width):
             nc.vector.tensor_tensor(dst, h_sb[i][:].indirect(pos2_sb[:, m0 // 16 : (m0 + width) // 16]), src, ALU.add)
 
-        z_rows = [sb("z_rows%d" % i, [P, PH], F32) for i in range(4)]
+        z_rows = [sb("z_rows%d" % i, [P, PH], F32)[:] for i in range(4)]
         z_low = sb("z_low", [P, 4, PH], F32)
 
         def phrases_low(i):
@@ -198,8 +195,8 @@ def tile_list_phrase_tree_forget_kernel(
         z_q = [sb("z_q%d" % a, [P, PH], U32) for a in range(PASSES)]
         z_sc = [sb("z_sc%d" % a, [P, PH], U8) for a in range(PASSES)]
 
-        def quant_z(m0, src):
-            quantize(z_q[1][:, m0 : m0 + HALF], z_sc[1][:, m0 : m0 + HALF], src)
+        def quant_z(a, m0, src):
+            quantize(z_q[a][:, m0 : m0 + HALF], z_sc[a][:, m0 : m0 + HALF], src)
 
         y_sb = [sb("y%d" % n, [P, PH], F32) for n in range(OUT_TILES)]
 
@@ -239,34 +236,37 @@ def tile_list_phrase_tree_forget_kernel(
 
         nc.vector.tensor_copy(v_w0[:], tab_w[0][:].indirect(offs_sb[:]))
         nc.vector.tensor_copy(v_sc[:], tab_sc[:].indirect(offs_sb[:]))
-        prepare_low(nc.scalar.copy, 0)
+        round_low(nc.scalar.copy, 0)
+        quant_low(0)
+
         for hf in range(2):
             nc.vector.tensor_copy(v_w1[hf][:], tab_w[1][:].indirect(offs_sb[:, 32 * hf : 32 * hf + 32]))
-        prepare_low(nc.vector.tensor_copy, 1)
-        prepare_low(nc.scalar.copy, 2)
         stage1(0)
-        prepare_low(nc.scalar.copy, 3)
+        for i in (1, 2):
+            round_low(nc.vector.tensor_copy, i)
+        for i in (1, 2):
+            quant_low(i)
+        first_low = [sb("first_low%d" % r, [P, PH], F32, tag="low_bf1" if r == 0 else None)[:] for r in range(2)]
+        first_low.append(first_low[0])
         phrases_low(0)
+        round_low(nc.scalar.copy, 3)
+        quant_low(3)
         stage1(1)
-        round_high(0, 0)
         phrases_low(1)
         stage1(2)
-        round_high(0, 1)
-        quant_high(0)
         phrases_low(2)
         stage1(3)
-        round_high(1, 0)
-        round_high(1, 1)
-        quant_high(1)
-        first_low.append(sb("first_low3", [P, PH], F32, tag="then_mem"))
+        prepare_high(0)
+        prepare_high(1)
+        first_low.append(sb("first_low3", [P, PH], F32, tag="then_mem")[:])
         phrases_low(3)
         for i in range(4, ROW_TILES):
             stage1(i)
 
         mem_sb = sb("mem_sb", [P, OUT_TILES, PH], F32, tag="then_mem")
         nc.sync.dma_start(mem_sb[:], mem.rearrange("(n p) m -> p n m", p=P))
-        content = sb("content", [P, OUT_TILES, PH], F32, tag="high_raw0")
-        gate = sb("gate", [P, OUT_TILES, PH], F32, tag="high_raw1")
+        content = sb("content", [P, OUT_TILES, PH], F32, tag="high_raw")
+        gate = sb("gate", [P, OUT_TILES, PH], F32)
 
         def gate_act(n0, m0, bank):
             nc.scalar.activation(
@@ -295,8 +295,8 @@ def tile_list_phrase_tree_forget_kernel(
         pick_late(2, 0, HALF)
         add_early(2)
         pick_early(3)
-        weave(nc.scalar.copy, low_z_bf, z_low[:])
-        quantize(z_q[0][:], z_sc[0][:], low_z_bf)
+        weave(nc.scalar.copy, low_z_bf, z_low[:, :, 0:HALF])
+        quant_z(0, 0, low_z_bf)
         add_early(3)
         for j in range(3):
             forget_mm(2 * j, 0, 0, banks[2 * j])
@@ -306,6 +306,8 @@ def tile_list_phrase_tree_forget_kernel(
         z_late = late[:].rearrange("p (t m) -> p t m", t=4)
         early_bf = late[:, 3 * QUARTER : 7 * QUARTER].bitcast(BF16)
         weave(nc.scalar.copy, early_bf, z_early)
+        low_late_bf = sb("low_late_bf", [P, 4 * HALF], BF16)
+        weave(nc.scalar.copy, low_late_bf[:], z_low[:, :, HALF:PH])
 
         def late_add(t):
             add_second(4 + t, z_late[:, t, :], first_late[t], HALF, HALF)
@@ -314,7 +316,8 @@ def tile_list_phrase_tree_forget_kernel(
             pick_late(t, (1 - t) * QUARTER, QUARTER)
         pick_late(3, 0, HALF)
         late_add(0)
-        quant_z(0, early_bf)
+        quant_z(1, 0, early_bf)
+        quant_z(0, HALF, low_late_bf[:])
         for t in range(1, 4):
             late_add(t)
         for j in range(3):
@@ -334,7 +337,7 @@ def tile_list_phrase_tree_forget_kernel(
         gated_mem(0, 0)
         gated_mem(2, 0)
         state(0, 0)
-        quant_z(HALF, late_bf[:])
+        quant_z(1, HALF, late_bf[:])
         gated_mem(4, 0)
         state(2, 0)
         state(4, 0)

@@ -56,25 +56,25 @@ def tile_list_phrase_tree_forget_kernel(
                 tab_words[a].rearrange("p t i -> p (t i)").bitcast(I32),
             )
 
-        def load_w1(name, c0, width):
-            raw = sb(name, [P, PASSES * 4 * width], F32)[:].rearrange("p (a j c) -> p a j c", a=PASSES, j=4)
-            for a in range(PASSES):
-                nc.sync.dma_start(
-                    raw[:, a], w1[512 * a : 512 * (a + 1), c0 : c0 + width].rearrange("(p j) c -> p j c", j=4))
-            return raw
+        def load_w1(dst, g, a):
+            nc.sync.dma_start(
+                dst, w1[512 * a : 512 * (a + 1), 512 * g : 512 * (g + 1)].rearrange("(p j) c -> p j c", j=4))
 
         def load_list(name, src, entries):
             tile = sb(name, [P, entries // 16], U16)
             nc.sync.dma_start(tile[:], src)
             return tile
 
-        load_tab(0)
-        first_raw = load_w1("first_raw", 0, P)
-        load_tab(1)
-        low_raw = load_w1("low_raw", P, 3 * P)
+        low_raw = [sb("low_raw%d" % a, [P, 4, 512], F32) for a in range(PASSES)]
+        high_raw = sb("high_raw", [P, PASSES, 4, 512], F32)
+        for a in range(PASSES):
+            load_tab(a)
+            load_w1(low_raw[a][:], 0, a)
         pos1_sb = load_list("pos1_sb", pos1, PH)
         pos2_sb = load_list("pos2_sb", pos2, PH)
-        high_raw = load_w1("high_raw", 512, 512)
+        for a in range(PASSES):
+            load_w1(high_raw[:, a], 1, a)
+
         w2_sc = sb("w2_sc", [P, PASSES, N], U8)
         nc.gpsimd.memset(w2_sc[:].rearrange("p a c -> p (a c)").bitcast(I32), 0)
         for q in range(4):
@@ -91,53 +91,49 @@ def tile_list_phrase_tree_forget_kernel(
         wf_sb = sb("wf_sb", [P, PASSES, N], U32)
         nc.sync.dma_start(wf_sb[:].bitcast(I32), wf_words.rearrange("a p c i -> p a (c i)").bitcast(I32))
 
+        mem_sb = sb("mem_sb", [P, OUT_TILES, PH], F32)
+        nc.sync.dma_start(mem_sb[:], mem.rearrange("(n p) m -> p n m", p=P))
         pos3_sb = load_list("pos3_sb", pos3, CL)
         pos4_sb = load_list("pos4_sb", pos4, CL)
 
         v_sc = sb("v_sc", [P, S], U8)
         v_w0 = sb("v_w0", [P, S], U32)
-        v_w1 = [sb("v_w1%d" % hf, [P, BANK], U32) for hf in range(2)]
 
         def weave(copy, dst, src):
-            copy(dst.rearrange("p (c i t) -> p c t i", i=4, t=4), src.rearrange("p t (c i) -> p c t i", i=4))
+            copy(dst.rearrange("p (c i t) -> p c t i", i=2, t=4), src.rearrange("p t (c i) -> p c t i", i=2))
 
         def quantize(codes, scales, src):
             nc.vector.quantize_mx(out=codes.bitcast(FP8X4), scales=scales, in_=src)
 
-        low_bf = [sb("low_bf%d" % i, [P, 1024], BF16)[:] for i in range(4)]
-        low_q = [sb("low_q%d" % i, [P, PASSES * P], U32) for i in range(4)]
-        low_sc = [sb("low_sc%d" % i, [P, PASSES * P], U8) for i in range(4)]
+        low_q = [sb("low_q%d" % a, [P, BANK], U32) for a in range(PASSES)]
+        low_sc = [sb("low_sc%d" % a, [P, BANK], U8) for a in range(PASSES)]
 
-        def round_low(copy, i):
-            dst = low_bf[i].rearrange("p (a c i t) -> p a c t i", a=PASSES, i=4, t=4)
-            raw = first_raw if i == 0 else low_raw[:, :, :, (i - 1) * P : i * P]
-            src = raw.rearrange("p a t (c i) -> p a c t i", i=4)
-            if i == 0:
-                for a in range(PASSES):
-                    copy(dst[:, a], src[:, a])
-            else:
-                copy(dst, src)
-
-        def quant_low(i):
-            quantize(low_q[i][:], low_sc[i][:], low_bf[i])
+        def prepare_low(copy, a, u, tag):
+            rounded = sb("low_bf%d%d" % (a, u), [P, 1024], BF16, tag=tag)
+            copy(
+                rounded[:].rearrange("p (t m j) -> p m j t", t=2, j=4),
+                low_raw[a][:].rearrange("p j (m t) -> p m j t", t=4)[:, :, :, 2 * u : 2 * u + 2],
+            )
+            cols = slice(2 * u * P, 2 * (u + 1) * P)
+            quantize(low_q[a][:, cols], low_sc[a][:, cols], rounded[:])
 
         early = sb("early", [P, 5 * HALF], F32)
         z_early = early[:, 0 : 4 * HALF].rearrange("p (t m) -> p t m", t=4)
         low_z_bf = early[:, 3 * HALF : 5 * HALF].bitcast(BF16)
-        high_bf = [sb("high_bf%d" % u, [P, 2048], BF16, tag="then_mem" if u == 0 else None)[:] for u in range(2)]
         high_q = [sb("high_q%d" % u, [P, BANK], U32) for u in range(2)]
         high_sc = [sb("high_sc%d" % u, [P, BANK], U8) for u in range(2)]
 
         def prepare_high(u):
+            rounded = sb("high_bf%d" % u, [P, 2048], BF16, tag="first_low%d" % u)[:]
             nc.scalar.copy(
-                high_bf[u].rearrange("p (a t m j) -> p a m j t", a=PASSES, t=2, j=4),
-                high_raw.rearrange("p a j (m t) -> p a m j t", t=4)[:, :, :, :, 2 * u : 2 * u + 2],
+                rounded.rearrange("p (a t m j) -> p a m j t", a=PASSES, t=2, j=4),
+                high_raw[:].rearrange("p a j (m t) -> p a m j t", t=4)[:, :, :, :, 2 * u : 2 * u + 2],
             )
-            quantize(high_q[u][:], high_sc[u][:], high_bf[u])
+            quantize(high_q[u][:], high_sc[u][:], rounded)
 
         def stationary(i, a):
             if i < 4:
-                return low_q[i], low_sc[i], a * P
+                return low_q[a], low_sc[a], i * P
             return high_q[(i - 4) // 2], high_sc[(i - 4) // 2], a * 2 * P + (i % 2) * P
 
         h_sb = []
@@ -167,21 +163,19 @@ def tile_list_phrase_tree_forget_kernel(
         def add_second(i, dst, src, m0, width):
             nc.vector.tensor_tensor(dst, h_sb[i][:].indirect(pos2_sb[:, m0 // 16 : (m0 + width) // 16]), src, ALU.add)
 
-        z_rows = [sb("z_rows%d" % i, [P, PH], F32)[:] for i in range(4)]
         z_low = sb("z_low", [P, 4, PH], F32)
 
         def phrases_low(i):
             for m0 in (0, HALF):
                 pick_first(i, first_low[i][:, m0 : m0 + HALF], m0, HALF)
             for m0 in (0, HALF):
-                add_second(i, z_rows[i][:, m0 : m0 + HALF], first_low[i][:, m0 : m0 + HALF], m0, HALF)
-            for t in range(4):
-                nc.sync.dma_start(z_low[32 * i : 32 * i + 32, t, :], z_rows[i][t:P:4, :])
+                add_second(i, z_low[:, i, m0 : m0 + HALF], first_low[i][:, m0 : m0 + HALF], m0, HALF)
 
         late_picks = sb("late_picks", [P, 3 * HALF], F32)
         first_late = [late_picks[:, t * HALF : (t + 1) * HALF] for t in range(3)] + [early[:, 4 * HALF : 5 * HALF]]
-        first_even = sb("first_even", [P, HALF], F32)
-        first_early = [first_even[:], late_picks[:, QUARTER : 3 * QUARTER]]
+        even = sb("even", [P, 2 * HALF], F32)
+        low_late_bf = even[:].bitcast(BF16)
+        first_early = [even[:, 0:HALF], late_picks[:, QUARTER : 3 * QUARTER]]
 
         def pick_late(t, c0, width):
             pick_first(4 + t, first_late[t][:, c0 : c0 + width], HALF + c0, width)
@@ -236,35 +230,25 @@ def tile_list_phrase_tree_forget_kernel(
 
         nc.vector.tensor_copy(v_w0[:], tab_w[0][:].indirect(offs_sb[:]))
         nc.vector.tensor_copy(v_sc[:], tab_sc[:].indirect(offs_sb[:]))
-        round_low(nc.scalar.copy, 0)
-        quant_low(0)
-
+        for u in range(2):
+            prepare_low(nc.scalar.copy, 0, u, "low_bf0%d" % u)
+        v_w1 = [sb("v_w1%d" % hf, [P, BANK], U32, tag="low_bf0%d" % hf) for hf in range(2)]
         for hf in range(2):
             nc.vector.tensor_copy(v_w1[hf][:], tab_w[1][:].indirect(offs_sb[:, 32 * hf : 32 * hf + 32]))
-        stage1(0)
-        for i in (1, 2):
-            round_low(nc.vector.tensor_copy, i)
-        for i in (1, 2):
-            quant_low(i)
-        first_low = [sb("first_low%d" % r, [P, PH], F32, tag="low_bf1" if r == 0 else None)[:] for r in range(2)]
-        first_low.append(first_low[0])
-        phrases_low(0)
-        round_low(nc.scalar.copy, 3)
-        quant_low(3)
-        stage1(1)
-        phrases_low(1)
-        stage1(2)
-        phrases_low(2)
-        stage1(3)
+        prepare_low(nc.scalar.copy, 1, 0, "low_bf1")
+        prepare_low(nc.vector.tensor_copy, 1, 1, "low_bf1")
+        first_low = [sb("first_low%d" % r, [P, PH], F32)[:] for r in range(3)]
+        for i in range(4):
+            stage1(i)
+        for i in range(3):
+            phrases_low(i)
         prepare_high(0)
         prepare_high(1)
-        first_low.append(sb("first_low3", [P, PH], F32, tag="then_mem")[:])
+        first_low.append(sb("first_low3", [P, PH], F32, tag="first_low0")[:])
         phrases_low(3)
         for i in range(4, ROW_TILES):
             stage1(i)
 
-        mem_sb = sb("mem_sb", [P, OUT_TILES, PH], F32, tag="then_mem")
-        nc.sync.dma_start(mem_sb[:], mem.rearrange("(n p) m -> p n m", p=P))
         content = sb("content", [P, OUT_TILES, PH], F32, tag="high_raw")
         gate = sb("gate", [P, OUT_TILES, PH], F32)
 
@@ -306,8 +290,7 @@ def tile_list_phrase_tree_forget_kernel(
         z_late = late[:].rearrange("p (t m) -> p t m", t=4)
         early_bf = late[:, 3 * QUARTER : 7 * QUARTER].bitcast(BF16)
         weave(nc.scalar.copy, early_bf, z_early)
-        low_late_bf = sb("low_late_bf", [P, 4 * HALF], BF16)
-        weave(nc.scalar.copy, low_late_bf[:], z_low[:, :, HALF:PH])
+        weave(nc.scalar.copy, low_late_bf, z_low[:, :, HALF:PH])
 
         def late_add(t):
             add_second(4 + t, z_late[:, t, :], first_late[t], HALF, HALF)
@@ -317,7 +300,7 @@ def tile_list_phrase_tree_forget_kernel(
         pick_late(3, 0, HALF)
         late_add(0)
         quant_z(1, 0, early_bf)
-        quant_z(0, HALF, low_late_bf[:])
+        quant_z(0, HALF, low_late_bf)
         for t in range(1, 4):
             late_add(t)
         for j in range(3):

@@ -67,9 +67,10 @@ def tile_list_phrase_tree_forget_kernel(
 
         low_raw = [sb("low_raw%d" % a, [P, 4, 512], F32) for a in range(PASSES)]
         high_raw = sb("high_raw", [P, PASSES, 4, 512], F32)
+        load_tab(0)
         for a in range(PASSES):
-            load_tab(a)
             load_w1(low_raw[a][:], 0, a)
+        load_tab(1)
         pos1_sb = load_list("pos1_sb", pos1, PH)
         pos2_sb = load_list("pos2_sb", pos2, PH)
         for a in range(PASSES):
@@ -108,23 +109,21 @@ def tile_list_phrase_tree_forget_kernel(
         low_q = [sb("low_q%d" % a, [P, BANK], U32) for a in range(PASSES)]
         low_sc = [sb("low_sc%d" % a, [P, BANK], U8) for a in range(PASSES)]
 
-        def prepare_low(copy, a, u, tag):
-            rounded = sb("low_bf%d%d" % (a, u), [P, 1024], BF16, tag=tag)
-            copy(
+        def prepare_low(a, u):
+            rounded = sb("low_bf%d%d" % (a, u), [P, 1024], BF16)
+            nc.scalar.copy(
                 rounded[:].rearrange("p (t m j) -> p m j t", t=2, j=4),
                 low_raw[a][:].rearrange("p j (m t) -> p m j t", t=4)[:, :, :, 2 * u : 2 * u + 2],
             )
             cols = slice(2 * u * P, 2 * (u + 1) * P)
             quantize(low_q[a][:, cols], low_sc[a][:, cols], rounded[:])
 
-        early = sb("early", [P, 5 * HALF], F32)
-        z_early = early[:, 0 : 4 * HALF].rearrange("p (t m) -> p t m", t=4)
-        low_z_bf = early[:, 3 * HALF : 5 * HALF].bitcast(BF16)
+        z_early = sb("z_early", [P, 4, HALF], F32)[:]
+        low_z_bf = sb("low_z_bf", [P, 4 * HALF], BF16)[:]
         high_q = [sb("high_q%d" % u, [P, BANK], U32) for u in range(2)]
         high_sc = [sb("high_sc%d" % u, [P, BANK], U8) for u in range(2)]
 
-        def prepare_high(u):
-            rounded = sb("high_bf%d" % u, [P, 2048], BF16, tag="first_low%d" % u)[:]
+        def prepare_high(u, rounded):
             nc.scalar.copy(
                 rounded.rearrange("p (a t m j) -> p a m j t", a=PASSES, t=2, j=4),
                 high_raw[:].rearrange("p a j (m t) -> p a m j t", t=4)[:, :, :, :, 2 * u : 2 * u + 2],
@@ -145,7 +144,7 @@ def tile_list_phrase_tree_forget_kernel(
                 cols = slice(hf * BANK, (hf + 1) * BANK)
                 for a in range(PASSES):
                     codes, scales, c0 = stationary(i, a)
-                    moving = v_w0[:, cols] if a == 0 else v_w1[hf][:]
+                    moving = (v_w0, v_w1)[a][:, cols]
                     nc.tensor.matmul_mx(
                         out=bank[:],
                         lhsT=codes[:, c0 : c0 + P].bitcast(FP8X4),
@@ -163,28 +162,27 @@ def tile_list_phrase_tree_forget_kernel(
         def add_second(i, dst, src, m0, width):
             nc.vector.tensor_tensor(dst, h_sb[i][:].indirect(pos2_sb[:, m0 // 16 : (m0 + width) // 16]), src, ALU.add)
 
-        z_low = sb("z_low", [P, 4, PH], F32)
+        low = sb("low", [P, 8 * HALF], F32)
+        z_low_late = low[:, 0 : 4 * HALF].rearrange("p (t m) -> p t m", t=4)
+        z_low_early = low[:, 2 * HALF : 6 * HALF].rearrange("p (t m) -> p t m", t=4)
+        ends = low[:, 6 * HALF : 8 * HALF]
+        first_low = [ends] + [sb("first_low%d" % i, [P, PH], F32)[:] for i in (1, 2)] + [ends]
 
-        def phrases_low(i):
+        def low_early(i):
             for m0 in (0, HALF):
                 pick_first(i, first_low[i][:, m0 : m0 + HALF], m0, HALF)
+            add_second(i, z_low_early[:, i, :], first_low[i][:, 0:HALF], 0, HALF)
+
+        def low_late(i):
+            add_second(i, z_low_late[:, i, :], first_low[i][:, HALF:PH], HALF, HALF)
+
+        low_late_bf = sb("low_late_bf", [P, 4 * HALF], BF16)[:]
+        first_high = [sb("first_high%d" % t, [P, PH], F32)[:] for t in range(4)]
+
+        def high_early(t):
             for m0 in (0, HALF):
-                add_second(i, z_low[:, i, m0 : m0 + HALF], first_low[i][:, m0 : m0 + HALF], m0, HALF)
-
-        late_picks = sb("late_picks", [P, 3 * HALF], F32)
-        first_late = [late_picks[:, t * HALF : (t + 1) * HALF] for t in range(3)] + [early[:, 4 * HALF : 5 * HALF]]
-        even = sb("even", [P, 2 * HALF], F32)
-        low_late_bf = even[:].bitcast(BF16)
-        first_early = [even[:, 0:HALF], late_picks[:, QUARTER : 3 * QUARTER]]
-
-        def pick_late(t, c0, width):
-            pick_first(4 + t, first_late[t][:, c0 : c0 + width], HALF + c0, width)
-
-        def pick_early(t):
-            pick_first(4 + t, first_early[t % 2], 0, HALF)
-
-        def add_early(t):
-            add_second(4 + t, z_early[:, t, :], first_early[t % 2], 0, HALF)
+                pick_first(4 + t, first_high[t][:, m0 : m0 + HALF], m0, HALF)
+            add_second(4 + t, z_early[:, t, :], first_high[t][:, 0:HALF], 0, HALF)
 
         z_q = [sb("z_q%d" % a, [P, PH], U32) for a in range(PASSES)]
         z_sc = [sb("z_sc%d" % a, [P, PH], U8) for a in range(PASSES)]
@@ -230,22 +228,23 @@ def tile_list_phrase_tree_forget_kernel(
 
         nc.vector.tensor_copy(v_w0[:], tab_w[0][:].indirect(offs_sb[:]))
         nc.vector.tensor_copy(v_sc[:], tab_sc[:].indirect(offs_sb[:]))
-        for u in range(2):
-            prepare_low(nc.scalar.copy, 0, u, "low_bf0%d" % u)
-        v_w1 = [sb("v_w1%d" % hf, [P, BANK], U32, tag="low_bf0%d" % hf) for hf in range(2)]
+        for a, u in ((0, 0), (0, 1), (1, 0)):
+            prepare_low(a, u)
+        v_w1 = sb("v_w1", [P, S], U32, tag="low_bf10")
         for hf in range(2):
-            nc.vector.tensor_copy(v_w1[hf][:], tab_w[1][:].indirect(offs_sb[:, 32 * hf : 32 * hf + 32]))
-        prepare_low(nc.scalar.copy, 1, 0, "low_bf1")
-        prepare_low(nc.vector.tensor_copy, 1, 1, "low_bf1")
-        first_low = [sb("first_low%d" % r, [P, PH], F32)[:] for r in range(3)]
-        for i in range(4):
-            stage1(i)
+            nc.vector.tensor_copy(
+                v_w1[:, hf * BANK : (hf + 1) * BANK], tab_w[1][:].indirect(offs_sb[:, 32 * hf : 32 * hf + 32]))
+        prepare_low(1, 1)
         for i in range(3):
-            phrases_low(i)
-        prepare_high(0)
-        prepare_high(1)
-        first_low.append(sb("first_low3", [P, PH], F32, tag="first_low0")[:])
-        phrases_low(3)
+            stage1(i)
+        for i in range(2):
+            low_early(i)
+            low_late(i)
+        prepare_high(0, low[:, 4 * HALF : 8 * HALF].bitcast(BF16))
+        stage1(3)
+        prepare_high(1, sb("high_bf1", [P, 2048], BF16, tag="first_low1")[:])
+        for i in range(2, 4):
+            low_early(i)
         for i in range(4, ROW_TILES):
             stage1(i)
 
@@ -271,41 +270,27 @@ def tile_list_phrase_tree_forget_kernel(
                 nc.vector.scalar_tensor_tensor(
                     y_sb[n][:, cols], gate[:, n, cols], 0.5, content[:, n, cols], ALU.mult, ALU.add)
 
-        for t in range(2):
-            pick_early(t)
-            pick_late(t, t * QUARTER, QUARTER)
-            add_early(t)
-        pick_early(2)
-        pick_late(2, 0, HALF)
-        add_early(2)
-        pick_early(3)
-        weave(nc.scalar.copy, low_z_bf, z_low[:, :, 0:HALF])
+        for t in range(4):
+            high_early(t)
+        weave(nc.scalar.copy, low_z_bf, z_low_early)
         quant_z(0, 0, low_z_bf)
-        add_early(3)
-        for j in range(3):
-            forget_mm(2 * j, 0, 0, banks[2 * j])
-            content_mm(2 * j, 0, 0, banks[2 * j + 1])
 
         late = sb("late", [P, 4 * HALF], F32)
         z_late = late[:].rearrange("p (t m) -> p t m", t=4)
-        early_bf = late[:, 3 * QUARTER : 7 * QUARTER].bitcast(BF16)
+        early_bf = late[:, QUARTER : 5 * QUARTER].bitcast(BF16)
         weave(nc.scalar.copy, early_bf, z_early)
-        weave(nc.scalar.copy, low_late_bf, z_low[:, :, HALF:PH])
-
-        def late_add(t):
-            add_second(4 + t, z_late[:, t, :], first_late[t], HALF, HALF)
-
-        for t in range(2):
-            pick_late(t, (1 - t) * QUARTER, QUARTER)
-        pick_late(3, 0, HALF)
-        late_add(0)
         quant_z(1, 0, early_bf)
+        for i in range(2, 4):
+            low_late(i)
+        weave(nc.scalar.copy, low_late_bf, z_low_late)
+        for t in (3, 0, 1, 2):
+            add_second(4 + t, z_late[:, t, :], first_high[t][:, HALF:PH], HALF, HALF)
         quant_z(0, HALF, low_late_bf)
-        for t in range(1, 4):
-            late_add(t)
         for j in range(3):
-            forget_mm(2 * j, 0, 1, banks[2 * j])
-            content_mm(2 * j, 0, 1, banks[2 * j + 1])
+            for a in range(PASSES):
+                forget_mm(2 * j, 0, a, banks[2 * j])
+            for a in range(PASSES):
+                content_mm(2 * j, 0, a, banks[2 * j + 1])
         forget_mm(0, HALF, 0, banks[6])
         content_mm(0, HALF, 0, banks[7])
 

@@ -18,11 +18,15 @@ ALU = mybir.AluOpType
 
 P = 128
 BANK = 512
-PASSES = 2
+PASS_K = 512
+PASSES = K // PASS_K
+GROUP = 4
 ROW_TILES = H // P
 OUT_TILES = N // P
 HALF = PH // 2
-QUARTER = HALF // 2
+PAIR = 2 * P * GROUP
+LIST_ROWS = 16
+OPEN_EARLY = 3
 
 
 def tile_list_phrase_tree_forget_kernel(
@@ -39,10 +43,15 @@ def tile_list_phrase_tree_forget_kernel(
 
         banks = [psum.tile([P, BANK], F32, name="bank%d" % b) for b in range(8)]
 
-        offs_sb = sb("offs_sb", [P, S // 16], U16)
-        nc.sync.dma_start(offs_sb[:], offs)
+        def load_list(name, src, entries):
+            tile = sb(name, [P, entries // LIST_ROWS], U16)
+            nc.sync.dma_start(tile[:], src)
+            return tile
+
+        offs_sb = load_list("offs_sb", offs, S)
+
         tab_sc = sb("tab_sc", [P, T], U8)
-        nc.gpsimd.memset(tab_sc[:].bitcast(I32), 0)
+        nc.vector.memset(tab_sc[:].bitcast(I32), 0)
         for q in range(4):
             nc.sync.dma_start(
                 tab_sc[32 * q : 32 * q + 8, :].bitcast(I32),
@@ -57,16 +66,11 @@ def tile_list_phrase_tree_forget_kernel(
             )
 
         def load_w1(dst, g, a):
-            nc.sync.dma_start(
-                dst, w1[512 * a : 512 * (a + 1), 512 * g : 512 * (g + 1)].rearrange("(p j) c -> p j c", j=4))
+            rows = slice(PASS_K * a, PASS_K * (a + 1))
+            nc.sync.dma_start(dst, w1[rows, PASS_K * g : PASS_K * (g + 1)].rearrange("(p j) c -> p j c", j=4))
 
-        def load_list(name, src, entries):
-            tile = sb(name, [P, entries // 16], U16)
-            nc.sync.dma_start(tile[:], src)
-            return tile
-
-        low_raw = [sb("low_raw%d" % a, [P, 4, 512], F32) for a in range(PASSES)]
-        high_raw = sb("high_raw", [P, PASSES, 4, 512], F32)
+        low_raw = [sb("low_raw%d" % a, [P, 4, PASS_K], F32) for a in range(PASSES)]
+        high_raw = sb("high_raw", [P, PASSES, 4, PASS_K], F32)
         load_tab(0)
         for a in range(PASSES):
             load_w1(low_raw[a][:], 0, a)
@@ -91,7 +95,6 @@ def tile_list_phrase_tree_forget_kernel(
         nc.sync.dma_start(wc_sb[:].bitcast(I32), wc_words.rearrange("a p c -> p a c").bitcast(I32))
         wf_sb = sb("wf_sb", [P, PASSES, N], U32)
         nc.sync.dma_start(wf_sb[:].bitcast(I32), wf_words.rearrange("a p c i -> p a (c i)").bitcast(I32))
-
         mem_sb = sb("mem_sb", [P, OUT_TILES, PH], F32)
         nc.sync.dma_start(mem_sb[:], mem.rearrange("(n p) m -> p n m", p=P))
         pos3_sb = load_list("pos3_sb", pos3, CL)
@@ -100,17 +103,14 @@ def tile_list_phrase_tree_forget_kernel(
         v_sc = sb("v_sc", [P, S], U8)
         v_w0 = sb("v_w0", [P, S], U32)
 
-        def weave(copy, dst, src):
-            copy(dst.rearrange("p (c i t) -> p c t i", i=2, t=4), src.rearrange("p t (c i) -> p c t i", i=2))
-
         def quantize(codes, scales, src):
             nc.vector.quantize_mx(out=codes.bitcast(FP8X4), scales=scales, in_=src)
 
-        low_q = [sb("low_q%d" % a, [P, BANK], U32) for a in range(PASSES)]
-        low_sc = [sb("low_sc%d" % a, [P, BANK], U8) for a in range(PASSES)]
+        low_q = [sb("low_q%d" % a, [P, GROUP * P], U32) for a in range(PASSES)]
+        low_sc = [sb("low_sc%d" % a, [P, GROUP * P], U8) for a in range(PASSES)]
 
         def prepare_low(a, u):
-            rounded = sb("low_bf%d%d" % (a, u), [P, 1024], BF16)
+            rounded = sb("low_bf%d%d" % (a, u), [P, PAIR], BF16)
             nc.scalar.copy(
                 rounded[:].rearrange("p (t m j) -> p m j t", t=2, j=4),
                 low_raw[a][:].rearrange("p j (m t) -> p m j t", t=4)[:, :, :, 2 * u : 2 * u + 2],
@@ -118,10 +118,10 @@ def tile_list_phrase_tree_forget_kernel(
             cols = slice(2 * u * P, 2 * (u + 1) * P)
             quantize(low_q[a][:, cols], low_sc[a][:, cols], rounded[:])
 
-        z_early = sb("z_early", [P, 4, HALF], F32)[:]
-        low_z_bf = sb("low_z_bf", [P, 4 * HALF], BF16)[:]
-        high_q = [sb("high_q%d" % u, [P, BANK], U32) for u in range(2)]
-        high_sc = [sb("high_sc%d" % u, [P, BANK], U8) for u in range(2)]
+        z_high_early = sb("z_high_early", [P, GROUP, HALF], F32)[:]
+        low_early_bf = sb("low_early_bf", [P, GROUP * HALF], BF16)[:]
+        high_q = [sb("high_q%d" % u, [P, PASSES * 2 * P], U32) for u in range(2)]
+        high_sc = [sb("high_sc%d" % u, [P, PASSES * 2 * P], U8) for u in range(2)]
 
         def prepare_high(u, rounded):
             nc.scalar.copy(
@@ -131,16 +131,16 @@ def tile_list_phrase_tree_forget_kernel(
             quantize(high_q[u][:], high_sc[u][:], rounded)
 
         def stationary(i, a):
-            if i < 4:
+            if i < GROUP:
                 return low_q[a], low_sc[a], i * P
-            return high_q[(i - 4) // 2], high_sc[(i - 4) // 2], a * 2 * P + (i % 2) * P
+            return high_q[(i - GROUP) // 2], high_sc[(i - GROUP) // 2], a * 2 * P + (i % 2) * P
 
         h_sb = []
 
         def stage1(i):
             h_sb.append(sb("h%d" % i, [P, S], F32))
             for hf in range(2):
-                bank = banks[2 * (i % 4) + hf]
+                bank = banks[2 * (i % GROUP) + hf]
                 cols = slice(hf * BANK, (hf + 1) * BANK)
                 for a in range(PASSES):
                     codes, scales, c0 = stationary(i, a)
@@ -156,43 +156,38 @@ def tile_list_phrase_tree_forget_kernel(
                     )
                 nc.scalar.copy(h_sb[i][:, cols], bank[:])
 
-        def pick_first(i, dst, m0, width):
-            nc.vector.tensor_copy(dst, h_sb[i][:].indirect(pos1_sb[:, m0 // 16 : (m0 + width) // 16]))
+        def half_of(list_sb, m0):
+            return list_sb[:, m0 // LIST_ROWS : (m0 + HALF) // LIST_ROWS]
 
-        def add_second(i, dst, src, m0, width):
-            nc.vector.tensor_tensor(dst, h_sb[i][:].indirect(pos2_sb[:, m0 // 16 : (m0 + width) // 16]), src, ALU.add)
+        def add_second(i, dst, picks, m0):
+            nc.vector.tensor_tensor(dst, h_sb[i][:].indirect(half_of(pos2_sb, m0)), picks[:, m0 : m0 + HALF], ALU.add)
+
+        def pick_and_add_early(i, dst, picks):
+            for m0 in (0, HALF):
+                nc.vector.tensor_copy(picks[:, m0 : m0 + HALF], h_sb[i][:].indirect(half_of(pos1_sb, m0)))
+            add_second(i, dst, picks, 0)
 
         low = sb("low", [P, 8 * HALF], F32)
-        z_low_late = low[:, 0 : 4 * HALF].rearrange("p (t m) -> p t m", t=4)
-        z_low_early = low[:, 2 * HALF : 6 * HALF].rearrange("p (t m) -> p t m", t=4)
-        ends = low[:, 6 * HALF : 8 * HALF]
-        first_low = [ends] + [sb("first_low%d" % i, [P, PH], F32)[:] for i in (1, 2)] + [ends]
-
-        def low_early(i):
-            for m0 in (0, HALF):
-                pick_first(i, first_low[i][:, m0 : m0 + HALF], m0, HALF)
-            add_second(i, z_low_early[:, i, :], first_low[i][:, 0:HALF], 0, HALF)
-
-        def low_late(i):
-            add_second(i, z_low_late[:, i, :], first_low[i][:, HALF:PH], HALF, HALF)
-
-        low_late_bf = sb("low_late_bf", [P, 4 * HALF], BF16)[:]
-        first_high = [sb("first_high%d" % t, [P, PH], F32)[:] for t in range(4)]
-
-        def high_early(t):
-            for m0 in (0, HALF):
-                pick_first(4 + t, first_high[t][:, m0 : m0 + HALF], m0, HALF)
-            add_second(4 + t, z_early[:, t, :], first_high[t][:, 0:HALF], 0, HALF)
+        z_low_late = low[:, 0 : 4 * HALF].rearrange("p (t m) -> p t m", t=GROUP)
+        z_low_early = low[:, 2 * HALF : 6 * HALF].rearrange("p (t m) -> p t m", t=GROUP)
+        outer_picks = low[:, 6 * HALF : 8 * HALF]
+        low_picks = [outer_picks] + [sb("low_picks%d" % i, [P, PH], F32)[:] for i in (1, 2)] + [outer_picks]
+        low_late_bf = sb("low_late_bf", [P, GROUP * HALF], BF16)[:]
+        high_picks = [sb("high_picks%d" % t, [P, PH], F32)[:] for t in range(GROUP)]
 
         z_q = [sb("z_q%d" % a, [P, PH], U32) for a in range(PASSES)]
         z_sc = [sb("z_sc%d" % a, [P, PH], U8) for a in range(PASSES)]
+
+        def round_z(dst, src):
+            nc.scalar.copy(
+                dst.rearrange("p (c i t) -> p c t i", i=2, t=GROUP), src.rearrange("p t (c i) -> p c t i", i=2))
 
         def quant_z(a, m0, src):
             quantize(z_q[a][:, m0 : m0 + HALF], z_sc[a][:, m0 : m0 + HALF], src)
 
         y_sb = [sb("y%d" % n, [P, PH], F32) for n in range(OUT_TILES)]
 
-        def forget_mm(n0, m0, a, bank):
+        def forget_mm(n0, m0, a, bank, opens):
             for d in range(2):
                 n = n0 + d
                 nc.tensor.matmul_mx(
@@ -201,10 +196,10 @@ def tile_list_phrase_tree_forget_kernel(
                     lhsT_scale=w2_sc[4:P, a, n * P : (n + 1) * P],
                     rhs=z_q[a][:, m0 : m0 + HALF].bitcast(FP8X4),
                     rhs_scale=z_sc[a][:, m0 : m0 + HALF],
-                    start=(a == 0 and d == 0), stop=(a == 1 and d == 1),
+                    start=(opens and d == 0), stop=(not opens and d == 1),
                 )
 
-        def content_mm(n0, m0, a, bank):
+        def content_mm(n0, m0, a, bank, opens):
             for c in range(4):
                 n, m = n0 + c // 2, m0 + (c % 2) * P
                 nc.tensor.matmul_mx(
@@ -213,7 +208,7 @@ def tile_list_phrase_tree_forget_kernel(
                     lhsT_scale=w2_sc[:, a, n * P : (n + 1) * P],
                     rhs=z_q[a][:, m : m + P].bitcast(FP8X4),
                     rhs_scale=z_sc[a][:, m : m + P],
-                    start=(a == 0 and c == 0), stop=(a == 1 and c == 3),
+                    start=(opens and c == 0), stop=(not opens and c == 3),
                 )
 
         second = [sb("second%d" % n, [P, CL], F32) for n in range(OUT_TILES)]
@@ -232,20 +227,21 @@ def tile_list_phrase_tree_forget_kernel(
             prepare_low(a, u)
         v_w1 = sb("v_w1", [P, S], U32, tag="low_bf10")
         for hf in range(2):
-            nc.vector.tensor_copy(
-                v_w1[:, hf * BANK : (hf + 1) * BANK], tab_w[1][:].indirect(offs_sb[:, 32 * hf : 32 * hf + 32]))
+            entries = offs_sb[:, hf * BANK // LIST_ROWS : (hf + 1) * BANK // LIST_ROWS]
+            nc.vector.tensor_copy(v_w1[:, hf * BANK : (hf + 1) * BANK], tab_w[1][:].indirect(entries))
         prepare_low(1, 1)
+
         for i in range(3):
             stage1(i)
         for i in range(2):
-            low_early(i)
-            low_late(i)
+            pick_and_add_early(i, z_low_early[:, i, :], low_picks[i])
+            add_second(i, z_low_late[:, i, :], low_picks[i], HALF)
         prepare_high(0, low[:, 4 * HALF : 8 * HALF].bitcast(BF16))
         stage1(3)
-        prepare_high(1, sb("high_bf1", [P, 2048], BF16, tag="first_low1")[:])
-        for i in range(2, 4):
-            low_early(i)
-        for i in range(4, ROW_TILES):
+        prepare_high(1, sb("high_bf1", [P, PASSES * PAIR], BF16, tag="low_picks1")[:])
+        for i in range(2, GROUP):
+            pick_and_add_early(i, z_low_early[:, i, :], low_picks[i])
+        for i in range(GROUP, ROW_TILES):
             stage1(i)
 
         content = sb("content", [P, OUT_TILES, PH], F32, tag="high_raw")
@@ -270,54 +266,55 @@ def tile_list_phrase_tree_forget_kernel(
                 nc.vector.scalar_tensor_tensor(
                     y_sb[n][:, cols], gate[:, n, cols], 0.5, content[:, n, cols], ALU.mult, ALU.add)
 
-        for t in range(4):
-            high_early(t)
-        weave(nc.scalar.copy, low_z_bf, z_low_early)
-        quant_z(0, 0, low_z_bf)
+        for t in range(GROUP):
+            pick_and_add_early(GROUP + t, z_high_early[:, t, :], high_picks[t])
+        round_z(low_early_bf, z_low_early)
+        quant_z(0, 0, low_early_bf)
 
-        late = sb("late", [P, 4 * HALF], F32)
-        z_late = late[:].rearrange("p (t m) -> p t m", t=4)
-        early_bf = late[:, QUARTER : 5 * QUARTER].bitcast(BF16)
-        weave(nc.scalar.copy, early_bf, z_early)
-        quant_z(1, 0, early_bf)
-        for i in range(2, 4):
-            low_late(i)
-        weave(nc.scalar.copy, low_late_bf, z_low_late)
+        late = sb("late", [P, GROUP * HALF], F32)
+        z_high_late = late[:].rearrange("p (t m) -> p t m", t=GROUP)
+        high_early_bf = late[:, HALF // 2 : 5 * HALF // 2].bitcast(BF16)
+        round_z(high_early_bf, z_high_early)
+        quant_z(1, 0, high_early_bf)
+
+        for i in range(2, GROUP):
+            add_second(i, z_low_late[:, i, :], low_picks[i], HALF)
+        round_z(low_late_bf, z_low_late)
         for t in (3, 0, 1, 2):
-            add_second(4 + t, z_late[:, t, :], first_high[t][:, HALF:PH], HALF, HALF)
+            add_second(GROUP + t, z_high_late[:, t, :], high_picks[t], HALF)
         quant_z(0, HALF, low_late_bf)
-        for j in range(3):
-            for a in range(PASSES):
-                forget_mm(2 * j, 0, a, banks[2 * j])
-            for a in range(PASSES):
-                content_mm(2 * j, 0, a, banks[2 * j + 1])
-        forget_mm(0, HALF, 0, banks[6])
-        content_mm(0, HALF, 0, banks[7])
+        for b in range(OUT_TILES):
+            product = content_mm if b % 2 else forget_mm
+            opening = 0 if b < OPEN_EARLY else 1
+            product(b - b % 2, 0, opening, banks[b], True)
+            product(b - b % 2, 0, 1 - opening, banks[b], False)
+        forget_mm(0, HALF, 0, banks[6], True)
+        content_mm(0, HALF, 0, banks[7], True)
 
         gate_act(0, 0, banks[0])
         content_act(0, 0, banks[1])
         gate_act(2, 0, banks[2])
-        late_bf = sb("late_bf", [P, 4 * HALF], BF16)
-        weave(nc.scalar.copy, late_bf[:], z_late)
+        high_late_bf = sb("high_late_bf", [P, GROUP * HALF], BF16)
+        round_z(high_late_bf[:], z_high_late)
         content_act(2, 0, banks[3])
         gate_act(4, 0, banks[4])
         content_act(4, 0, banks[5])
         gated_mem(0, 0)
         gated_mem(2, 0)
         state(0, 0)
-        quant_z(1, HALF, late_bf[:])
+        quant_z(1, HALF, high_late_bf[:])
         gated_mem(4, 0)
         state(2, 0)
         state(4, 0)
 
         late_banks = ((6, 7), (0, 1), (2, 3))
-        forget_mm(0, HALF, 1, banks[6])
-        content_mm(0, HALF, 1, banks[7])
+        forget_mm(0, HALF, 1, banks[6], False)
+        content_mm(0, HALF, 1, banks[7], False)
         for j in (1, 2):
             for a in range(PASSES):
-                forget_mm(2 * j, HALF, a, banks[late_banks[j][0]])
+                forget_mm(2 * j, HALF, a, banks[late_banks[j][0]], a == 0)
             for a in range(PASSES):
-                content_mm(2 * j, HALF, a, banks[late_banks[j][1]])
+                content_mm(2 * j, HALF, a, banks[late_banks[j][1]], a == 0)
         for j in range(3):
             gate_act(2 * j, HALF, banks[late_banks[j][0]])
             content_act(2 * j, HALF, banks[late_banks[j][1]])

@@ -178,9 +178,8 @@ def tile_list_phrase_tree_forget_kernel(
         z_q = [sb("z_q%d" % a, [P, PH], U32) for a in range(PASSES)]
         z_sc = [sb("z_sc%d" % a, [P, PH], U8) for a in range(PASSES)]
 
-        def round_z(dst, src):
-            nc.scalar.copy(
-                dst.rearrange("p (c i t) -> p c t i", i=2, t=GROUP), src.rearrange("p t (c i) -> p c t i", i=2))
+        def round_z(copy, dst, src):
+            copy(dst.rearrange("p (c i t) -> p c t i", i=2, t=GROUP), src.rearrange("p t (c i) -> p c t i", i=2))
 
         def quant_z(a, m0, src):
             quantize(z_q[a][:, m0 : m0 + HALF], z_sc[a][:, m0 : m0 + HALF], src)
@@ -268,18 +267,18 @@ def tile_list_phrase_tree_forget_kernel(
 
         for t in range(GROUP):
             pick_and_add_early(GROUP + t, z_high_early[:, t, :], high_picks[t])
-        round_z(low_early_bf, z_low_early)
+        round_z(nc.scalar.copy, low_early_bf, z_low_early)
         quant_z(0, 0, low_early_bf)
 
         late = sb("late", [P, GROUP * HALF], F32)
         z_high_late = late[:].rearrange("p (t m) -> p t m", t=GROUP)
         high_early_bf = late[:, HALF // 2 : 5 * HALF // 2].bitcast(BF16)
-        round_z(high_early_bf, z_high_early)
+        round_z(nc.scalar.copy, high_early_bf, z_high_early)
         quant_z(1, 0, high_early_bf)
 
         for i in range(2, GROUP):
             add_second(i, z_low_late[:, i, :], low_picks[i], HALF)
-        round_z(low_late_bf, z_low_late)
+        round_z(nc.scalar.copy, low_late_bf, z_low_late)
         for t in (3, 0, 1, 2):
             add_second(GROUP + t, z_high_late[:, t, :], high_picks[t], HALF)
         quant_z(0, HALF, low_late_bf)
@@ -291,18 +290,15 @@ def tile_list_phrase_tree_forget_kernel(
         forget_mm(0, HALF, 0, banks[6], True)
         content_mm(0, HALF, 0, banks[7], True)
 
-        gate_act(0, 0, banks[0])
-        content_act(0, 0, banks[1])
-        gate_act(2, 0, banks[2])
-        high_late_bf = sb("high_late_bf", [P, GROUP * HALF], BF16)
-        round_z(high_late_bf[:], z_high_late)
-        content_act(2, 0, banks[3])
-        gate_act(4, 0, banks[4])
-        content_act(4, 0, banks[5])
+        for j in range(3):
+            gate_act(2 * j, 0, banks[2 * j])
+            content_act(2 * j, 0, banks[2 * j + 1])
         gated_mem(0, 0)
+        high_late_bf = sb("high_late_bf", [P, GROUP * HALF], BF16)
+        round_z(nc.vector.tensor_copy, high_late_bf[:], z_high_late)
         gated_mem(2, 0)
-        state(0, 0)
         quant_z(1, HALF, high_late_bf[:])
+        state(0, 0)
         gated_mem(4, 0)
         state(2, 0)
         state(4, 0)

@@ -48,6 +48,10 @@ def tile_list_phrase_tree_forget_kernel(
             nc.sync.dma_start(tile[:], src)
             return tile
 
+        warm = sb("warm", [P, 2], F32)
+        nc.gpsimd.memset(warm[:], 0.0)
+        nc.scalar.activation(warm[:, 1:2], warm[:, 0:1], ACT.Sigmoid)
+
         offs_sb = load_list("offs_sb", offs, S)
 
         tab_sc = sb("tab_sc", [P, T], U8)
@@ -106,17 +110,17 @@ def tile_list_phrase_tree_forget_kernel(
         def quantize(codes, scales, src):
             nc.vector.quantize_mx(out=codes.bitcast(FP8X4), scales=scales, in_=src)
 
-        low_q = [sb("low_q%d" % a, [P, GROUP * P], U32) for a in range(PASSES)]
-        low_sc = [sb("low_sc%d" % a, [P, GROUP * P], U8) for a in range(PASSES)]
+        low_q, low_sc = {}, {}
 
-        def prepare_low(a, u):
-            rounded = sb("low_bf%d%d" % (a, u), [P, PAIR], BF16)
-            nc.scalar.copy(
-                rounded[:].rearrange("p (t m j) -> p m j t", t=2, j=4),
-                low_raw[a][:].rearrange("p j (m t) -> p m j t", t=4)[:, :, :, 2 * u : 2 * u + 2],
+        def round_low(copy, dst, a, u, m0=0, m1=P):
+            copy(
+                dst.rearrange("p (t m j) -> p m j t", t=2, j=4)[:, m0:m1],
+                low_raw[a][:].rearrange("p j (m t) -> p m j t", t=4)[:, m0:m1, :, 2 * u : 2 * u + 2],
             )
-            cols = slice(2 * u * P, 2 * (u + 1) * P)
-            quantize(low_q[a][:, cols], low_sc[a][:, cols], rounded[:])
+
+        def quant_low(a, u, rounded):
+            cols = slice(2 * a * P, 2 * (a + 1) * P)
+            quantize(low_q[u][:, cols], low_sc[u][:, cols], rounded)
 
         z_high_early = sb("z_high_early", [P, GROUP, HALF], F32)[:]
         low_early_bf = sb("low_early_bf", [P, GROUP * HALF], BF16)[:]
@@ -132,7 +136,7 @@ def tile_list_phrase_tree_forget_kernel(
 
         def stationary(i, a):
             if i < GROUP:
-                return low_q[a], low_sc[a], i * P
+                return low_q[i // 2], low_sc[i // 2], a * 2 * P + (i % 2) * P
             return high_q[(i - GROUP) // 2], high_sc[(i - GROUP) // 2], a * 2 * P + (i % 2) * P
 
         h_sb = []
@@ -184,7 +188,8 @@ def tile_list_phrase_tree_forget_kernel(
         def quant_z(a, m0, src):
             quantize(z_q[a][:, m0 : m0 + HALF], z_sc[a][:, m0 : m0 + HALF], src)
 
-        y_sb = [sb("y%d" % n, [P, PH], F32) for n in range(OUT_TILES)]
+        y01 = sb("y01", [P, 2 * PH], F32)
+        y_sb = [y01[:, 0:PH], y01[:, PH : 2 * PH]] + [sb("y%d" % n, [P, PH], F32)[:] for n in range(2, OUT_TILES)]
 
         def forget_mm(n0, m0, a, bank, opens):
             for d in range(2):
@@ -210,25 +215,24 @@ def tile_list_phrase_tree_forget_kernel(
                     start=(opens and c == 0), stop=(not opens and c == 3),
                 )
 
-        second = [sb("second%d" % n, [P, CL], F32) for n in range(OUT_TILES)]
-        result = [sb("result%d" % n, [P, CL], F32) for n in range(OUT_TILES)]
-
-        def clauses(n0):
-            for n in (n0, n0 + 1):
-                nc.vector.tensor_copy(second[n][:], y_sb[n][:].indirect(pos4_sb[:]))
-            for n in (n0, n0 + 1):
-                nc.vector.tensor_tensor(result[n][:], y_sb[n][:].indirect(pos3_sb[:]), second[n][:], ALU.subtract)
-                nc.sync.dma_start(out[n * P : (n + 1) * P, :], result[n][:])
-
         nc.vector.tensor_copy(v_w0[:], tab_w[0][:].indirect(offs_sb[:]))
         nc.vector.tensor_copy(v_sc[:], tab_sc[:].indirect(offs_sb[:]))
-        for a, u in ((0, 0), (0, 1), (1, 0)):
-            prepare_low(a, u)
+        for u in range(2):
+            low_sc[u] = sb("low_sc%d" % u, [P, PASSES * 2 * P], U8)
+        low_q[0] = sb("low_q0", [P, PASSES * 2 * P], U32)
+        low_bf = {}
+        for a in range(PASSES):
+            for u in range(2):
+                low_bf[a, u] = sb("low_bf%d%d" % (a, u), [P, PAIR], BF16)[:]
+                round_low(nc.scalar.copy, low_bf[a, u], a, u)
+            quant_low(a, 0, low_bf[a, 0])
         v_w1 = sb("v_w1", [P, S], U32, tag="low_bf10")
         for hf in range(2):
             entries = offs_sb[:, hf * BANK // LIST_ROWS : (hf + 1) * BANK // LIST_ROWS]
             nc.vector.tensor_copy(v_w1[:, hf * BANK : (hf + 1) * BANK], tab_w[1][:].indirect(entries))
-        prepare_low(1, 1)
+        low_q[1] = sb("low_q1", [P, PASSES * 2 * P], U32, tag="tab_w1")
+        for a in range(PASSES):
+            quant_low(a, 1, low_bf[a, 1])
 
         for i in range(3):
             stage1(i)
@@ -248,22 +252,28 @@ def tile_list_phrase_tree_forget_kernel(
 
         def gate_act(n0, m0, bank):
             nc.scalar.activation(
-                gate[:, n0 : n0 + 2, m0 : m0 + HALF], bank[:].rearrange("p (d m) -> p d m", d=2), ACT.Tanh, scale=0.5)
+                gate[:, n0 : n0 + 2, m0 : m0 + HALF], bank[:].rearrange("p (d m) -> p d m", d=2), ACT.Sigmoid)
 
         def content_act(n0, m0, bank):
             nc.scalar.activation(
                 content[:, n0 : n0 + 2, m0 : m0 + HALF], bank[:].rearrange("p (d m) -> p d m", d=2), ACT.Tanh)
 
-        def gated_mem(n0, m0):
-            part = gate[:, n0 : n0 + 2, m0 : m0 + HALF]
-            nc.vector.scalar_tensor_tensor(
-                part, part, 1.0, mem_sb[:, n0 : n0 + 2, m0 : m0 + HALF], ALU.add, ALU.mult)
-
-        def state(n0, m0):
+        def gated_mem(engine, dst, n0, m0):
             cols = slice(m0, m0 + HALF)
-            for n in (n0, n0 + 1):
-                nc.vector.scalar_tensor_tensor(
-                    y_sb[n][:, cols], gate[:, n, cols], 0.5, content[:, n, cols], ALU.mult, ALU.add)
+            engine.tensor_tensor(dst, gate[:, n0 : n0 + 2, cols], mem_sb[:, n0 : n0 + 2, cols], ALU.mult)
+            return dst
+
+        def in_place(n0, m0):
+            return gated_mem(nc.vector, gate[:, n0 : n0 + 2, m0 : m0 + HALF], n0, m0)
+
+        def state(engine, gated, n0, m0):
+            cols = slice(m0, m0 + HALF)
+            if n0 == 0:
+                pair = y01[:].rearrange("p (d m) -> p d m", d=2)
+                engine.tensor_tensor(pair[:, :, cols], gated, content[:, 0:2, cols], ALU.add)
+            else:
+                for d in range(2):
+                    engine.tensor_tensor(y_sb[n0 + d][:, cols], gated[:, d, :], content[:, n0 + d, cols], ALU.add)
 
         for t in range(GROUP):
             pick_and_add_early(GROUP + t, z_high_early[:, t, :], high_picks[t])
@@ -293,15 +303,15 @@ def tile_list_phrase_tree_forget_kernel(
         for j in range(3):
             gate_act(2 * j, 0, banks[2 * j])
             content_act(2 * j, 0, banks[2 * j + 1])
-        gated_mem(0, 0)
+        early0 = in_place(0, 0)
         high_late_bf = sb("high_late_bf", [P, GROUP * HALF], BF16)
         round_z(nc.vector.tensor_copy, high_late_bf[:], z_high_late)
-        gated_mem(2, 0)
+        early2 = in_place(2, 0)
         quant_z(1, HALF, high_late_bf[:])
-        state(0, 0)
-        gated_mem(4, 0)
-        state(2, 0)
-        state(4, 0)
+        state(nc.vector, early0, 0, 0)
+        early4 = in_place(4, 0)
+        state(nc.vector, early2, 2, 0)
+        state(nc.vector, early4, 4, 0)
 
         late_banks = ((6, 7), (0, 1), (2, 3))
         forget_mm(0, HALF, 1, banks[6], False)
@@ -314,9 +324,34 @@ def tile_list_phrase_tree_forget_kernel(
         for j in range(3):
             gate_act(2 * j, HALF, banks[late_banks[j][0]])
             content_act(2 * j, HALF, banks[late_banks[j][1]])
-        gated_mem(0, HALF)
-        for j in range(3):
-            if j < 2:
-                gated_mem(2 * j + 2, HALF)
-            state(2 * j, HALF)
-            clauses(2 * j)
+        def two(ap):
+            return ap.rearrange("p (d m) -> p d m", d=2)
+
+        last = sb("last", [P, 4 * HALF], F32)
+        late0 = in_place(0, HALF)
+        late2 = gated_mem(nc.vector, two(last[:, 7 * HALF // 4 : 15 * HALF // 4]), 2, HALF)
+        state(nc.vector, late0, 0, HALF)
+        state(nc.vector, late2, 2, HALF)
+        late4 = gated_mem(nc.gpsimd, two(last[:, 0 : 2 * HALF]), 4, HALF)
+        state(nc.gpsimd, late4, 4, HALF)
+        plus01, minus01 = mem_sb[:, 2:4, HALF:PH], content[:, 2:4, HALF:PH]
+        minus = {n: last[:, n * CL : (n + 1) * CL] for n in (2, 3)}
+        for n in (4, 5):
+            minus[n] = sb("minus%d" % n, [P, CL], F32)[:]
+
+        def pick_y(dst, n, list_sb):
+            nc.vector.tensor_copy(dst, y_sb[n].indirect(list_sb[:]))
+
+        for n in range(2):
+            pick_y(plus01[:, n, :], n, pos3_sb)
+        for n in range(2):
+            pick_y(minus01[:, n, :], n, pos4_sb)
+        nc.gpsimd.tensor_tensor(late4, plus01, minus01, ALU.subtract)
+        for n in range(2):
+            nc.sync.dma_start(out[n * P : (n + 1) * P, :], late4[:, n, :])
+        for n in range(2, OUT_TILES):
+            pick_y(minus[n], n, pos4_sb)
+        for n in range(2, OUT_TILES):
+            result = (plus01, minus01)[n // 4][:, n % 2, :]
+            nc.vector.tensor_tensor(result, y_sb[n].indirect(pos3_sb[:]), minus[n], ALU.subtract)
+            nc.sync.dma_start(out[n * P : (n + 1) * P, :], result)

@@ -26,6 +26,7 @@ OUT_TILES = N // P
 HALF = PH // 2
 PAIR = 2 * P * GROUP
 LIST_ROWS = 16
+FIRST_PIECES = ((0, 512), (512, 768), (768, 1024))
 OPEN_EARLY = 3
 
 
@@ -118,11 +119,13 @@ def tile_list_phrase_tree_forget_kernel(
                 low_raw[a][:].rearrange("p j (m t) -> p m j t", t=4)[:, m0:m1, :, 2 * u : 2 * u + 2],
             )
 
-        def quant_low(a, u, rounded):
-            cols = slice(2 * a * P, 2 * (a + 1) * P)
-            quantize(low_q[u][:, cols], low_sc[u][:, cols], rounded)
+        def quant_low(a, u, rounded, tag=None):
+            low_q[a, u] = sb("low_q%d%d" % (a, u), [P, 2 * P], U32, tag=tag)
+            low_sc[a, u] = sb("low_sc%d%d" % (a, u), [P, 2 * P], U8)
+            quantize(low_q[a, u][:], low_sc[a, u][:], rounded)
 
-        z_high_early = sb("z_high_early", [P, GROUP, HALF], F32)[:]
+        z_rows = sb("z_rows", [P, 13 * HALF], F32)
+        z_high_early = z_rows[:, 0 : 4 * HALF].rearrange("p (t m) -> p t m", t=GROUP)
         low_early_bf = sb("low_early_bf", [P, GROUP * HALF], BF16)[:]
         high_q = [sb("high_q%d" % u, [P, PASSES * 2 * P], U32) for u in range(2)]
         high_sc = [sb("high_sc%d" % u, [P, PASSES * 2 * P], U8) for u in range(2)]
@@ -136,21 +139,24 @@ def tile_list_phrase_tree_forget_kernel(
 
         def stationary(i, a):
             if i < GROUP:
-                return low_q[i // 2], low_sc[i // 2], a * 2 * P + (i % 2) * P
+                return low_q[a, i // 2], low_sc[a, i // 2], (i % 2) * P
             return high_q[(i - GROUP) // 2], high_sc[(i - GROUP) // 2], a * 2 * P + (i % 2) * P
 
         h_sb = []
 
         def stage1(i):
             h_sb.append(sb("h%d" % i, [P, S], F32))
-            for hf in range(2):
-                bank = banks[2 * (i % GROUP) + hf]
-                cols = slice(hf * BANK, (hf + 1) * BANK)
+            pieces = [(banks[2 * (i % GROUP) + hf], hf * BANK, (hf + 1) * BANK) for hf in range(2)]
+            if i == 0:
+                pieces = [(banks[b], c0, c1) for b, (c0, c1) in zip((0, 1, 7), FIRST_PIECES)]
+            for bank, t0, t1 in pieces:
+                cols = slice(t0, t1)
+                sums = bank[:, 0 : t1 - t0]
                 for a in range(PASSES):
                     codes, scales, c0 = stationary(i, a)
                     moving = (v_w0, v_w1)[a][:, cols]
                     nc.tensor.matmul_mx(
-                        out=bank[:],
+                        out=sums,
                         lhsT=codes[:, c0 : c0 + P].bitcast(FP8X4),
                         lhsT_scale=scales[:, c0 : c0 + P],
                         rhs=moving.bitcast(FP8X4),
@@ -158,26 +164,31 @@ def tile_list_phrase_tree_forget_kernel(
                         start=(a == 0),
                         stop=(a == PASSES - 1),
                     )
-                nc.scalar.copy(h_sb[i][:, cols], bank[:])
+                copy = nc.vector.tensor_copy if (i, t1) == (0, S) else nc.scalar.copy
+                copy(h_sb[i][:, cols], sums)
 
         def half_of(list_sb, m0):
             return list_sb[:, m0 // LIST_ROWS : (m0 + HALF) // LIST_ROWS]
 
+        def halves(ap):
+            return ap[:, 0:HALF], ap[:, HALF:PH]
+
         def add_second(i, dst, picks, m0):
-            nc.vector.tensor_tensor(dst, h_sb[i][:].indirect(half_of(pos2_sb, m0)), picks[:, m0 : m0 + HALF], ALU.add)
+            nc.vector.tensor_tensor(dst, h_sb[i][:].indirect(half_of(pos2_sb, m0)), picks[m0 // HALF], ALU.add)
 
         def pick_and_add_early(i, dst, picks):
             for m0 in (0, HALF):
-                nc.vector.tensor_copy(picks[:, m0 : m0 + HALF], h_sb[i][:].indirect(half_of(pos1_sb, m0)))
+                nc.vector.tensor_copy(picks[m0 // HALF], h_sb[i][:].indirect(half_of(pos1_sb, m0)))
             add_second(i, dst, picks, 0)
 
-        low = sb("low", [P, 8 * HALF], F32)
-        z_low_late = low[:, 0 : 4 * HALF].rearrange("p (t m) -> p t m", t=GROUP)
-        z_low_early = low[:, 2 * HALF : 6 * HALF].rearrange("p (t m) -> p t m", t=GROUP)
-        outer_picks = low[:, 6 * HALF : 8 * HALF]
-        low_picks = [outer_picks] + [sb("low_picks%d" % i, [P, PH], F32)[:] for i in (1, 2)] + [outer_picks]
+        low = z_rows[:, 4 * HALF : 13 * HALF]
+        z_low_early = low[:, 0 : 4 * HALF].rearrange("p (t m) -> p t m", t=GROUP)
+        z_low_late = low[:, 3 * HALF : 7 * HALF].rearrange("p (t m) -> p t m", t=GROUP)
+        low_picks = [halves(sb("low_picks%d" % i, [P, PH], F32)[:]) for i in range(3)]
+        low_picks[0] = (low[:, 7 * HALF : 8 * HALF], low_picks[0][1])
+        low_picks.append(halves(low[:, 7 * HALF : 9 * HALF]))
         low_late_bf = sb("low_late_bf", [P, GROUP * HALF], BF16)[:]
-        high_picks = [sb("high_picks%d" % t, [P, PH], F32)[:] for t in range(GROUP)]
+        high_picks = [halves(sb("high_picks%d" % t, [P, PH], F32)[:]) for t in range(GROUP)]
 
         z_q = [sb("z_q%d" % a, [P, PH], U32) for a in range(PASSES)]
         z_sc = [sb("z_sc%d" % a, [P, PH], U8) for a in range(PASSES)]
@@ -217,33 +228,31 @@ def tile_list_phrase_tree_forget_kernel(
 
         nc.vector.tensor_copy(v_w0[:], tab_w[0][:].indirect(offs_sb[:]))
         nc.vector.tensor_copy(v_sc[:], tab_sc[:].indirect(offs_sb[:]))
-        for u in range(2):
-            low_sc[u] = sb("low_sc%d" % u, [P, PASSES * 2 * P], U8)
-        low_q[0] = sb("low_q0", [P, PASSES * 2 * P], U32)
         low_bf = {}
         for a in range(PASSES):
             for u in range(2):
                 low_bf[a, u] = sb("low_bf%d%d" % (a, u), [P, PAIR], BF16)[:]
-                round_low(nc.scalar.copy, low_bf[a, u], a, u)
-            quant_low(a, 0, low_bf[a, 0])
+                round_low(nc.vector.tensor_copy if (a, u) == (0, 1) else nc.scalar.copy, low_bf[a, u], a, u)
+        for a, u in ((0, 0), (0, 1), (1, 0)):
+            quant_low(a, u, low_bf[a, u])
         v_w1 = sb("v_w1", [P, S], U32, tag="low_bf10")
-        for hf in range(2):
-            entries = offs_sb[:, hf * BANK // LIST_ROWS : (hf + 1) * BANK // LIST_ROWS]
-            nc.vector.tensor_copy(v_w1[:, hf * BANK : (hf + 1) * BANK], tab_w[1][:].indirect(entries))
-        low_q[1] = sb("low_q1", [P, PASSES * 2 * P], U32, tag="tab_w1")
-        for a in range(PASSES):
-            quant_low(a, 1, low_bf[a, 1])
+        for c0, c1 in FIRST_PIECES:
+            entries = offs_sb[:, c0 // LIST_ROWS : c1 // LIST_ROWS]
+            nc.vector.tensor_copy(v_w1[:, c0:c1], tab_w[1][:].indirect(entries))
+        quant_low(1, 1, low_bf[1, 1], tag="tab_w1")
 
         for i in range(3):
             stage1(i)
-        for i in range(2):
-            pick_and_add_early(i, z_low_early[:, i, :], low_picks[i])
-            add_second(i, z_low_late[:, i, :], low_picks[i], HALF)
-        prepare_high(0, low[:, 4 * HALF : 8 * HALF].bitcast(BF16))
+        pick_and_add_early(0, z_low_early[:, 0, :], low_picks[0])
+        pick_and_add_early(1, z_low_early[:, 1, :], low_picks[1])
+        add_second(1, z_low_late[:, 1, :], low_picks[1], HALF)
+        prepare_high(0, low[:, 5 * HALF : 9 * HALF].bitcast(BF16))
         stage1(3)
         prepare_high(1, sb("high_bf1", [P, PASSES * PAIR], BF16, tag="low_picks1")[:])
-        for i in range(2, GROUP):
-            pick_and_add_early(i, z_low_early[:, i, :], low_picks[i])
+        pick_and_add_early(2, z_low_early[:, 2, :], low_picks[2])
+        add_second(2, z_low_late[:, 2, :], low_picks[2], HALF)
+        pick_and_add_early(3, z_low_early[:, 3, :], low_picks[3])
+        add_second(3, z_low_late[:, 3, :], low_picks[3], HALF)
         for i in range(GROUP, ROW_TILES):
             stage1(i)
 
@@ -280,16 +289,14 @@ def tile_list_phrase_tree_forget_kernel(
         round_z(nc.scalar.copy, low_early_bf, z_low_early)
         quant_z(0, 0, low_early_bf)
 
-        late = sb("late", [P, GROUP * HALF], F32)
-        z_high_late = late[:].rearrange("p (t m) -> p t m", t=GROUP)
-        high_early_bf = late[:, HALF // 2 : 5 * HALF // 2].bitcast(BF16)
+        z_high_late = z_rows[:, 2 * HALF : 6 * HALF].rearrange("p (t m) -> p t m", t=GROUP)
+        high_early_bf = sb("high_early_bf", [P, GROUP * HALF], BF16)[:]
         round_z(nc.scalar.copy, high_early_bf, z_high_early)
         quant_z(1, 0, high_early_bf)
 
-        for i in range(2, GROUP):
-            add_second(i, z_low_late[:, i, :], low_picks[i], HALF)
+        add_second(0, z_low_late[:, 0, :], low_picks[0], HALF)
         round_z(nc.scalar.copy, low_late_bf, z_low_late)
-        for t in (3, 0, 1, 2):
+        for t in (3, 2, 0, 1):
             add_second(GROUP + t, z_high_late[:, t, :], high_picks[t], HALF)
         quant_z(0, HALF, low_late_bf)
         for b in range(OUT_TILES):

@@ -26,7 +26,7 @@ OUT_TILES = N // P
 HALF = PH // 2
 PAIR = 2 * P * GROUP
 LIST_ROWS = 16
-FIRST_PIECES = ((0, 512), (512, 768), (768, 1024))
+SCALAR_WORDS = 48
 OPEN_EARLY = 3
 
 
@@ -37,6 +37,7 @@ def tile_list_phrase_tree_forget_kernel(
     nc = tc.nc
     with ExitStack() as ctx:
         keep = ctx.enter_context(tc.tile_pool(name="keep", bufs=1))
+        placed = ctx.enter_context(tc.tile_pool(name="placed", bufs=1))
         psum = ctx.enter_context(tc.psum_pool(name="psum", bufs=1))
 
         def sb(name, shape, dtype, tag=None):
@@ -62,7 +63,7 @@ def tile_list_phrase_tree_forget_kernel(
                 tab_sc[32 * q : 32 * q + 8, :].bitcast(I32),
                 tab_scales[:, 4 * q : 4 * q + 4, :].bitcast(I32),
             )
-        tab_w = [sb("tab_w%d" % a, [P, T], U32) for a in range(PASSES)]
+        tab_w = [sb("tab_w0", [P, T], U32), placed.tile([P, T], U32, name="tab_w1", align_bytes=64, offset=0)]
 
         def load_tab(a):
             nc.sync.dma_start(
@@ -77,9 +78,9 @@ def tile_list_phrase_tree_forget_kernel(
         low_raw = [sb("low_raw%d" % a, [P, 4, PASS_K], F32) for a in range(PASSES)]
         high_raw = sb("high_raw", [P, PASSES, 4, PASS_K], F32)
         load_tab(0)
-        for a in range(PASSES):
-            load_w1(low_raw[a][:], 0, a)
+        load_w1(low_raw[0][:], 0, 0)
         load_tab(1)
+        load_w1(low_raw[1][:], 0, 1)
         pos1_sb = load_list("pos1_sb", pos1, PH)
         pos2_sb = load_list("pos2_sb", pos2, PH)
         for a in range(PASSES):
@@ -119,8 +120,8 @@ def tile_list_phrase_tree_forget_kernel(
                 low_raw[a][:].rearrange("p j (m t) -> p m j t", t=4)[:, m0:m1, :, 2 * u : 2 * u + 2],
             )
 
-        def quant_low(a, u, rounded, tag=None):
-            low_q[a, u] = sb("low_q%d%d" % (a, u), [P, 2 * P], U32, tag=tag)
+        def quant_low(a, u, rounded, codes=None):
+            low_q[a, u] = sb("low_q%d%d" % (a, u), [P, 2 * P], U32) if codes is None else codes
             low_sc[a, u] = sb("low_sc%d%d" % (a, u), [P, 2 * P], U8)
             quantize(low_q[a, u][:], low_sc[a, u][:], rounded)
 
@@ -148,7 +149,7 @@ def tile_list_phrase_tree_forget_kernel(
             h_sb.append(sb("h%d" % i, [P, S], F32))
             pieces = [(banks[2 * (i % GROUP) + hf], hf * BANK, (hf + 1) * BANK) for hf in range(2)]
             if i == 0:
-                pieces = [(banks[b], c0, c1) for b, (c0, c1) in zip((0, 1, 7), FIRST_PIECES)]
+                pieces = [(banks[b], q * HALF, (q + 1) * HALF) for q, b in enumerate((0, 1, 6, 7))]
             for bank, t0, t1 in pieces:
                 cols = slice(t0, t1)
                 sums = bank[:, 0 : t1 - t0]
@@ -164,7 +165,7 @@ def tile_list_phrase_tree_forget_kernel(
                         start=(a == 0),
                         stop=(a == PASSES - 1),
                     )
-                copy = nc.vector.tensor_copy if (i, t1) == (0, S) else nc.scalar.copy
+                copy = nc.vector.tensor_copy if i == 0 and t1 % BANK else nc.scalar.copy
                 copy(h_sb[i][:, cols], sums)
 
         def half_of(list_sb, m0):
@@ -228,18 +229,25 @@ def tile_list_phrase_tree_forget_kernel(
 
         nc.vector.tensor_copy(v_w0[:], tab_w[0][:].indirect(offs_sb[:]))
         nc.vector.tensor_copy(v_sc[:], tab_sc[:].indirect(offs_sb[:]))
-        low_bf = {}
-        for a in range(PASSES):
-            for u in range(2):
-                low_bf[a, u] = sb("low_bf%d%d" % (a, u), [P, PAIR], BF16)[:]
-                round_low(nc.vector.tensor_copy if (a, u) == (0, 1) else nc.scalar.copy, low_bf[a, u], a, u)
-        for a, u in ((0, 0), (0, 1), (1, 0)):
-            quant_low(a, u, low_bf[a, u])
-        v_w1 = sb("v_w1", [P, S], U32, tag="low_bf10")
-        for c0, c1 in FIRST_PIECES:
-            entries = offs_sb[:, c0 // LIST_ROWS : c1 // LIST_ROWS]
-            nc.vector.tensor_copy(v_w1[:, c0:c1], tab_w[1][:].indirect(entries))
-        quant_low(1, 1, low_bf[1, 1], tag="tab_w1")
+        low00 = sb("low00", [P, PAIR], BF16)[:]
+        round_low(nc.scalar.copy, low00, 0, 0)
+        quant_low(0, 0, low00)
+        low01 = sb("low01", [P, PAIR], BF16)[:]
+        round_low(nc.scalar.copy, low01, 0, 1)
+        v_w1 = sb("v_w1", [P, S], U32, tag="low00")
+        nc.vector.tensor_copy(v_w1[:], tab_w[1][:].indirect(offs_sb[:]))
+        low10 = placed.tile([P, PAIR], BF16, name="low10", align_bytes=64, offset=0)[:]
+        low11 = placed.tile([P, PAIR], BF16, name="low11", align_bytes=64, offset=2 * PAIR)[:]
+        round_low(nc.scalar.copy, low10, 1, 0, 0, SCALAR_WORDS)
+        round_low(nc.vector.tensor_copy, low10, 1, 0, SCALAR_WORDS, P)
+        low_q[1, 0] = sb("low_q10", [P, 2 * P], U32)
+        low_sc[1, 0] = sb("low_sc10", [P, 2 * P], U8)
+        for t in range(2):
+            cols = slice(t * P, (t + 1) * P)
+            quantize(low_q[1, 0][:, cols], low_sc[1, 0][:, cols], low10[:, t * PASS_K : (t + 1) * PASS_K])
+        quant_low(0, 1, low01, placed.tile([P, 2 * P], U32, name="low_q01", align_bytes=64, offset=0))
+        round_low(nc.scalar.copy, low11, 1, 1)
+        quant_low(1, 1, low11)
 
         for i in range(3):
             stage1(i)

@@ -1,6 +1,7 @@
 from contextlib import ExitStack
 
 import concourse.mybir as mybir
+from concourse.masks import make_identity
 
 K, T, S, H, PH, N, CL = 1024, 2048, 1024, 1024, 512, 768, 256
 FLOPS = 2 * K * H * S + 2 * 2 * H * N * PH
@@ -53,6 +54,9 @@ def tile_list_phrase_tree_forget_kernel(
         warm = sb("warm", [P, 2], F32)
         nc.gpsimd.memset(warm[:], 0.0)
         nc.scalar.activation(warm[:, 1:2], warm[:, 0:1], ACT.Sigmoid)
+
+        identity = sb("identity", [P, P], F32)
+        make_identity(nc, identity[:])
 
         offs_sb = load_list("offs_sb", offs, S)
 
@@ -125,7 +129,7 @@ def tile_list_phrase_tree_forget_kernel(
             low_sc[a, u] = sb("low_sc%d%d" % (a, u), [P, 2 * P], U8)
             quantize(low_q[a, u][:], low_sc[a, u][:], rounded)
 
-        z_rows = sb("z_rows", [P, 13 * HALF], F32)
+        z_rows = sb("z_rows", [P, 12 * HALF], F32)
         z_high_early = z_rows[:, 0 : 4 * HALF].rearrange("p (t m) -> p t m", t=GROUP)
         low_early_bf = sb("low_early_bf", [P, GROUP * HALF], BF16)[:]
         high_q = [sb("high_q%d" % u, [P, PASSES * 2 * P], U32) for u in range(2)]
@@ -182,12 +186,15 @@ def tile_list_phrase_tree_forget_kernel(
                 nc.vector.tensor_copy(picks[m0 // HALF], h_sb[i][:].indirect(half_of(pos1_sb, m0)))
             add_second(i, dst, picks, 0)
 
-        low = z_rows[:, 4 * HALF : 13 * HALF]
+        low = z_rows[:, 4 * HALF : 12 * HALF]
         z_low_early = low[:, 0 : 4 * HALF].rearrange("p (t m) -> p t m", t=GROUP)
-        z_low_late = low[:, 3 * HALF : 7 * HALF].rearrange("p (t m) -> p t m", t=GROUP)
-        low_picks = [halves(sb("low_picks%d" % i, [P, PH], F32)[:]) for i in range(3)]
-        low_picks[0] = (low[:, 7 * HALF : 8 * HALF], low_picks[0][1])
-        low_picks.append(halves(low[:, 7 * HALF : 9 * HALF]))
+        z_low_late = low[:, 2 * HALF : 6 * HALF].rearrange("p (t m) -> p t m", t=GROUP)
+        low_picks = [
+            (low[:, 6 * HALF : 7 * HALF], sb("late_picks0", [P, HALF], F32)[:]),
+            (sb("early_picks1", [P, HALF], F32)[:], sb("late_picks1", [P, HALF], F32)[:]),
+            halves(sb("low_picks2", [P, PH], F32)[:]),
+            halves(low[:, 6 * HALF : 8 * HALF]),
+        ]
         low_late_bf = sb("low_late_bf", [P, GROUP * HALF], BF16)[:]
         high_picks = [halves(sb("high_picks%d" % t, [P, PH], F32)[:]) for t in range(GROUP)]
 
@@ -253,10 +260,9 @@ def tile_list_phrase_tree_forget_kernel(
             stage1(i)
         pick_and_add_early(0, z_low_early[:, 0, :], low_picks[0])
         pick_and_add_early(1, z_low_early[:, 1, :], low_picks[1])
-        add_second(1, z_low_late[:, 1, :], low_picks[1], HALF)
-        prepare_high(0, low[:, 5 * HALF : 9 * HALF].bitcast(BF16))
+        prepare_high(0, low[:, 4 * HALF : 8 * HALF].bitcast(BF16))
         stage1(3)
-        prepare_high(1, sb("high_bf1", [P, PASSES * PAIR], BF16, tag="low_picks1")[:])
+        prepare_high(1, sb("high_bf1", [P, PASSES * PAIR], BF16, tag="early_picks1")[:])
         pick_and_add_early(2, z_low_early[:, 2, :], low_picks[2])
         add_second(2, z_low_late[:, 2, :], low_picks[2], HALF)
         pick_and_add_early(3, z_low_early[:, 3, :], low_picks[3])
@@ -297,14 +303,15 @@ def tile_list_phrase_tree_forget_kernel(
         round_z(nc.scalar.copy, low_early_bf, z_low_early)
         quant_z(0, 0, low_early_bf)
 
-        z_high_late = z_rows[:, 2 * HALF : 6 * HALF].rearrange("p (t m) -> p t m", t=GROUP)
+        z_high_late = z_rows[:, HALF : 5 * HALF].rearrange("p (t m) -> p t m", t=GROUP)
         high_early_bf = sb("high_early_bf", [P, GROUP * HALF], BF16)[:]
         round_z(nc.scalar.copy, high_early_bf, z_high_early)
         quant_z(1, 0, high_early_bf)
 
-        add_second(0, z_low_late[:, 0, :], low_picks[0], HALF)
+        for i in range(2):
+            add_second(i, z_low_late[:, i, :], low_picks[i], HALF)
         round_z(nc.scalar.copy, low_late_bf, z_low_late)
-        for t in (3, 2, 0, 1):
+        for t in (3, 0, 1, 2):
             add_second(GROUP + t, z_high_late[:, t, :], high_picks[t], HALF)
         quant_z(0, HALF, low_late_bf)
         for b in range(OUT_TILES):
@@ -318,39 +325,63 @@ def tile_list_phrase_tree_forget_kernel(
         for j in range(3):
             gate_act(2 * j, 0, banks[2 * j])
             content_act(2 * j, 0, banks[2 * j + 1])
-        early0 = in_place(0, 0)
         high_late_bf = sb("high_late_bf", [P, GROUP * HALF], BF16)
         round_z(nc.vector.tensor_copy, high_late_bf[:], z_high_late)
-        early2 = in_place(2, 0)
         quant_z(1, HALF, high_late_bf[:])
+        early0 = gated_mem(nc.vector, z_high_late[:, 0:2, :], 0, 0)
+        in_place(4, 0)
         state(nc.vector, early0, 0, 0)
-        early4 = in_place(4, 0)
-        state(nc.vector, early2, 2, 0)
-        state(nc.vector, early4, 4, 0)
+        state(nc.vector, in_place(2, 0), 2, 0)
 
         late_banks = ((6, 7), (0, 1), (2, 3))
         forget_mm(0, HALF, 1, banks[6], False)
+        for a in range(PASSES):
+            forget_mm(2, HALF, a, banks[0], a == 0)
         content_mm(0, HALF, 1, banks[7], False)
         for j in (1, 2):
             for a in range(PASSES):
-                forget_mm(2 * j, HALF, a, banks[late_banks[j][0]], a == 0)
-            for a in range(PASSES):
                 content_mm(2 * j, HALF, a, banks[late_banks[j][1]], a == 0)
-        for j in range(3):
-            gate_act(2 * j, HALF, banks[late_banks[j][0]])
-            content_act(2 * j, HALF, banks[late_banks[j][1]])
+            if j == 1:
+                for a in range(PASSES):
+                    forget_mm(4, HALF, a, banks[2], a == 0)
+
+        def blocks(n0):
+            return [((2 * d + b) * P, n0 + d, b * P) for d in range(2) for b in range(2)]
+
+        def turned_sum(n0, bank, turned):
+            for c, n, m in blocks(n0):
+                for first, src in ((True, content), (False, gate)):
+                    nc.tensor.matmul(
+                        bank[:, c : c + P], src[:, n, m : m + P], identity[:],
+                        start=first, stop=not first, is_transpose=True)
+            nc.scalar.copy(turned, bank[:])
+            return turned
+
+        def turn_back(n0, turned, bank):
+            for d in range(2):
+                for c, n, m in blocks(n0)[2 * d : 2 * d + 2]:
+                    nc.tensor.transpose(bank[:, c : c + P], turned[:, c : c + P], identity[:])
+                nc.scalar.copy(y_sb[n0 + d][:, 0:HALF], bank[:, d * HALF : (d + 1) * HALF])
+
+        for act, side in ((gate_act, 0), (content_act, 1)):
+            for j in range(2):
+                act(2 * j, HALF, banks[late_banks[j][side]])
+        gate_act(4, HALF, banks[2])
+        content_act(4, HALF, banks[3])
+        last = sb("last", [P, 6 * HALF], F32)
+        turned4 = turned_sum(4, banks[6], last[:, 0 : 2 * HALF])
+        turn_back(4, turned4, banks[4])
         def two(ap):
             return ap.rearrange("p (d m) -> p d m", d=2)
 
-        last = sb("last", [P, 4 * HALF], F32)
         late0 = in_place(0, HALF)
-        late2 = gated_mem(nc.vector, two(last[:, 7 * HALF // 4 : 15 * HALF // 4]), 2, HALF)
+        late2 = gated_mem(nc.vector, two(last[:, 15 * HALF // 4 : 23 * HALF // 4]), 2, HALF)
         state(nc.vector, late0, 0, HALF)
         state(nc.vector, late2, 2, HALF)
-        late4 = gated_mem(nc.gpsimd, two(last[:, 0 : 2 * HALF]), 4, HALF)
+        late4 = gated_mem(nc.gpsimd, two(last[:, 2 * HALF : 4 * HALF]), 4, HALF)
         state(nc.gpsimd, late4, 4, HALF)
         plus01, minus01 = mem_sb[:, 2:4, HALF:PH], content[:, 2:4, HALF:PH]
-        minus = {n: last[:, n * CL : (n + 1) * CL] for n in (2, 3)}
+        minus = {n: last[:, (n + 2) * CL : (n + 3) * CL] for n in (2, 3)}
         for n in (4, 5):
             minus[n] = sb("minus%d" % n, [P, CL], F32)[:]
 
@@ -361,9 +392,10 @@ def tile_list_phrase_tree_forget_kernel(
             pick_y(plus01[:, n, :], n, pos3_sb)
         for n in range(2):
             pick_y(minus01[:, n, :], n, pos4_sb)
-        nc.gpsimd.tensor_tensor(late4, plus01, minus01, ALU.subtract)
+        result01 = two(last[:, 0 : 4 * HALF])[:, :, HALF : 2 * HALF]
+        nc.gpsimd.tensor_tensor(result01, plus01, minus01, ALU.subtract)
         for n in range(2):
-            nc.sync.dma_start(out[n * P : (n + 1) * P, :], late4[:, n, :])
+            nc.sync.dma_start(out[n * P : (n + 1) * P, :], result01[:, n, :])
         for n in range(2, OUT_TILES):
             pick_y(minus[n], n, pos4_sb)
         for n in range(2, OUT_TILES):

@@ -345,23 +345,18 @@ def tile_list_phrase_tree_forget_kernel(
                 for a in range(PASSES):
                     forget_mm(4, HALF, a, banks[2], a == 0)
 
-        def blocks(n0):
-            return [((2 * d + b) * P, n0 + d, b * P) for d in range(2) for b in range(2)]
-
-        def turned_sum(n0, bank, turned):
-            for c, n, m in blocks(n0):
+        def turned_sum(n, bank, turned):
+            for m in range(0, HALF, P):
                 for first, src in ((True, content), (False, gate)):
                     nc.tensor.matmul(
-                        bank[:, c : c + P], src[:, n, m : m + P], identity[:],
+                        bank[:, m : m + P], src[:, n, m : m + P], identity[:],
                         start=first, stop=not first, is_transpose=True)
-            nc.scalar.copy(turned, bank[:])
-            return turned
+            nc.scalar.copy(turned, bank[:, 0:HALF])
 
-        def turn_back(n0, turned, bank):
-            for d in range(2):
-                for c, n, m in blocks(n0)[2 * d : 2 * d + 2]:
-                    nc.tensor.transpose(bank[:, c : c + P], turned[:, c : c + P], identity[:])
-                nc.scalar.copy(y_sb[n0 + d][:, 0:HALF], bank[:, d * HALF : (d + 1) * HALF])
+        def turn_back(n, turned, bank):
+            for m in range(0, HALF, P):
+                nc.tensor.transpose(bank[:, m : m + P], turned[:, m : m + P], identity[:])
+            nc.scalar.copy(y_sb[n][:, 0:HALF], bank[:, 0:HALF])
 
         for act, side in ((gate_act, 0), (content_act, 1)):
             for j in range(2):
@@ -369,8 +364,11 @@ def tile_list_phrase_tree_forget_kernel(
         gate_act(4, HALF, banks[2])
         content_act(4, HALF, banks[3])
         last = sb("last", [P, 6 * HALF], F32)
-        turned4 = turned_sum(4, banks[6], last[:, 0 : 2 * HALF])
-        turn_back(4, turned4, banks[4])
+        turned = {n: last[:, (n - 4) * HALF : (n - 3) * HALF] for n in (4, 5)}
+        for n in (4, 5):
+            turned_sum(n, banks[n + 2], turned[n])
+        for n in (4, 5):
+            turn_back(n, turned[n], banks[n])
         def two(ap):
             return ap.rearrange("p (d m) -> p d m", d=2)
 

@@ -28,6 +28,7 @@ HALF = PH // 2
 PAIR = 2 * P * GROUP
 LIST_ROWS = 16
 SCALAR_WORDS = 48
+WARM_PASSES = 3
 OPEN_EARLY = 3
 
 
@@ -256,8 +257,19 @@ def tile_list_phrase_tree_forget_kernel(
         round_low(nc.scalar.copy, low11, 1, 1)
         quant_low(1, 1, low11)
 
-        for i in range(3):
+        for i in range(2):
             stage1(i)
+        for r in range(WARM_PASSES):
+            nc.tensor.matmul_mx(
+                out=banks[4][:],
+                lhsT=low_q[0, 0][:, 0:P].bitcast(FP8X4),
+                lhsT_scale=low_sc[0, 0][:, 0:P],
+                rhs=v_w0[:, 0:BANK].bitcast(FP8X4),
+                rhs_scale=v_sc[:, 0:BANK],
+                start=(r == 0),
+                stop=(r == WARM_PASSES - 1),
+            )
+        stage1(2)
         pick_and_add_early(0, z_low_early[:, 0, :], low_picks[0])
         pick_and_add_early(1, z_low_early[:, 1, :], low_picks[1])
         prepare_high(0, low[:, 4 * HALF : 8 * HALF].bitcast(BF16))

@@ -52,12 +52,11 @@ def tile_list_phrase_tree_forget_kernel(
             nc.sync.dma_start(tile[:], src)
             return tile
 
-        warm = sb("warm", [P, 2], F32)
-        nc.gpsimd.memset(warm[:], 0.0)
-        nc.scalar.activation(warm[:, 1:2], warm[:, 0:1], ACT.Sigmoid)
-
         identity = sb("identity", [P, P], F32)
         make_identity(nc, identity[:])
+
+        warm = sb("warm", [P, 1], F32)
+        nc.scalar.activation(warm[:], identity[:, 0:1], ACT.Sigmoid)
 
         offs_sb = load_list("offs_sb", offs, S)
 

@@ -25,10 +25,8 @@ GROUP = 4
 ROW_TILES = H // P
 OUT_TILES = N // P
 HALF = PH // 2
-PAIR = 2 * P * GROUP
 LIST_ROWS = 16
-SCALAR_WORDS = 48
-WARM_PASSES = 3
+LAST_TOKENS = 768
 OPEN_EARLY = 3
 
 
@@ -39,7 +37,6 @@ def tile_list_phrase_tree_forget_kernel(
     nc = tc.nc
     with ExitStack() as ctx:
         keep = ctx.enter_context(tc.tile_pool(name="keep", bufs=1))
-        placed = ctx.enter_context(tc.tile_pool(name="placed", bufs=1))
         psum = ctx.enter_context(tc.psum_pool(name="psum", bufs=1))
 
         def sb(name, shape, dtype, tag=None):
@@ -52,22 +49,24 @@ def tile_list_phrase_tree_forget_kernel(
             nc.sync.dma_start(tile[:], src)
             return tile
 
+        tab_sc = sb("tab_sc", [P, T], U8)
+        nc.gpsimd.memset(tab_sc[:].bitcast(I32), 0)
         identity = sb("identity", [P, P], F32)
         make_identity(nc, identity[:])
 
-        warm = sb("warm", [P, 1], F32)
-        nc.scalar.activation(warm[:], identity[:, 0:1], ACT.Sigmoid)
+        warm = sb("warm", [P, 2], F32)
+        nc.vector.memset(warm[:, 0:1], 0.0)
+        nc.scalar.activation(warm[:, 1:2], warm[:, 0:1], ACT.Sigmoid)
 
         offs_sb = load_list("offs_sb", offs, S)
-
-        tab_sc = sb("tab_sc", [P, T], U8)
-        nc.vector.memset(tab_sc[:].bitcast(I32), 0)
+        pos1_sb = load_list("pos1_sb", pos1, PH)
+        pos2_sb = load_list("pos2_sb", pos2, PH)
         for q in range(4):
             nc.sync.dma_start(
                 tab_sc[32 * q : 32 * q + 8, :].bitcast(I32),
                 tab_scales[:, 4 * q : 4 * q + 4, :].bitcast(I32),
             )
-        tab_w = [sb("tab_w0", [P, T], U32), placed.tile([P, T], U32, name="tab_w1", align_bytes=64, offset=0)]
+        tab_w = [sb("tab_w%d" % a, [P, T], U32) for a in range(PASSES)]
 
         def load_tab(a):
             nc.sync.dma_start(
@@ -75,30 +74,30 @@ def tile_list_phrase_tree_forget_kernel(
                 tab_words[a].rearrange("p t i -> p (t i)").bitcast(I32),
             )
 
-        def load_w1(dst, g, a):
-            rows = slice(PASS_K * a, PASS_K * (a + 1))
-            nc.sync.dma_start(dst, w1[rows, PASS_K * g : PASS_K * (g + 1)].rearrange("(p j) c -> p j c", j=4))
+        def load_w1(name, a, c0, c1):
+            tile = sb(name, [P, 4, c1 - c0], F32)
+            nc.sync.dma_start(tile[:], w1[PASS_K * a : PASS_K * (a + 1), c0:c1].rearrange("(p j) c -> p j c", j=4))
+            return tile
 
-        low_raw = [sb("low_raw%d" % a, [P, 4, PASS_K], F32) for a in range(PASSES)]
-        high_raw = sb("high_raw", [P, PASSES, 4, PASS_K], F32)
         load_tab(0)
-        load_w1(low_raw[0][:], 0, 0)
+        raw01 = [load_w1("raw01_0", 0, 0, 2 * P)]
         load_tab(1)
-        load_w1(low_raw[1][:], 0, 1)
-        pos1_sb = load_list("pos1_sb", pos1, PH)
-        pos2_sb = load_list("pos2_sb", pos2, PH)
+        raw01.append(load_w1("raw01_1", 1, 0, 2 * P))
+        raw23 = [load_w1("raw23_%d" % a, a, 2 * P, 4 * P) for a in range(PASSES)]
+        high_raw = sb("high_raw", [P, PASSES, 4, PASS_K], F32)
         for a in range(PASSES):
-            load_w1(high_raw[:, a], 1, a)
+            rows = slice(PASS_K * a, PASS_K * (a + 1))
+            nc.sync.dma_start(high_raw[:, a], w1[rows, PASS_K:H].rearrange("(p j) c -> p j c", j=4))
 
-        w2_sc = sb("w2_sc", [P, PASSES, N], U8)
-        nc.gpsimd.memset(w2_sc[:].rearrange("p a c -> p (a c)").bitcast(I32), 0)
+        wcf_sc = sb("wcf_sc", [P, PASSES, N], U8)
+        nc.gpsimd.memset(wcf_sc[:].rearrange("p a c -> p (a c)").bitcast(I32), 0)
         for q in range(4):
             nc.sync.dma_start(
-                w2_sc[32 * q : 32 * q + 4, :, :].bitcast(I32),
+                wcf_sc[32 * q : 32 * q + 4, :, :].bitcast(I32),
                 wc_scales[:, 4 * q : 4 * q + 4, :].rearrange("a r c -> r a c").bitcast(I32),
             )
             nc.sync.dma_start(
-                w2_sc[32 * q + 4 : 32 * q + 8, :, :].bitcast(I32),
+                wcf_sc[32 * q + 4 : 32 * q + 8, :, :].bitcast(I32),
                 wf_scales[:, 4 * q : 4 * q + 4, :].rearrange("a r c -> r a c").bitcast(I32),
             )
         wc_sb = sb("wc_sb", [P, PASSES, 2 * N], U8)
@@ -110,187 +109,227 @@ def tile_list_phrase_tree_forget_kernel(
         pos3_sb = load_list("pos3_sb", pos3, CL)
         pos4_sb = load_list("pos4_sb", pos4, CL)
 
+        def quantize(name, rounded, words):
+            codes = sb(name + "_q", [P, words], U32)
+            scales = sb(name + "_sc", [P, words], U8)
+            nc.vector.quantize_mx(out=codes[:].bitcast(FP8X4), scales=scales[:], in_=rounded)
+            return codes, scales
+
+        def weave(copy, dst, src):
+            copy(dst.rearrange("p (c i j) -> p c j i", i=2, j=4), src.rearrange("p j (c i) -> p c j i", i=2))
+
         v_sc = sb("v_sc", [P, S], U8)
-        v_w0 = sb("v_w0", [P, S], U32)
+        v_w = [sb("v_w0", [P, S], U32)]
+        weights = {}
+        h_sb = {}
 
-        def quantize(codes, scales, src):
-            nc.vector.quantize_mx(out=codes.bitcast(FP8X4), scales=scales, in_=src)
+        def stage1_pass(i, a, bank, t0, t1):
+            codes, scales, c0 = weights[i, a]
+            cuts = [t0, LAST_TOKENS, t1] if a == 1 and t0 < LAST_TOKENS < t1 else [t0, t1]
+            for u0, u1 in zip(cuts, cuts[1:]):
+                words = v_last[:] if a == 1 and u0 == LAST_TOKENS else v_w[a][:, u0:u1]
+                nc.tensor.matmul_mx(
+                    out=bank[:, u0 - t0 : u1 - t0],
+                    lhsT=codes[:, c0 : c0 + P].bitcast(FP8X4),
+                    lhsT_scale=scales[:, c0 : c0 + P],
+                    rhs=words.bitcast(FP8X4),
+                    rhs_scale=v_sc[4 * a : P, u0:u1],
+                    start=(a == 0),
+                    stop=(a == PASSES - 1 and u1 == t1),
+                )
 
-        low_q, low_sc = {}, {}
-
-        def round_low(copy, dst, a, u, m0=0, m1=P):
-            copy(
-                dst.rearrange("p (t m j) -> p m j t", t=2, j=4)[:, m0:m1],
-                low_raw[a][:].rearrange("p j (m t) -> p m j t", t=4)[:, m0:m1, :, 2 * u : 2 * u + 2],
-            )
-
-        def quant_low(a, u, rounded, codes=None):
-            low_q[a, u] = sb("low_q%d%d" % (a, u), [P, 2 * P], U32) if codes is None else codes
-            low_sc[a, u] = sb("low_sc%d%d" % (a, u), [P, 2 * P], U8)
-            quantize(low_q[a, u][:], low_sc[a, u][:], rounded)
-
-        z_rows = sb("z_rows", [P, 12 * HALF], F32)
-        z_high_early = z_rows[:, 0 : 4 * HALF].rearrange("p (t m) -> p t m", t=GROUP)
-        low_early_bf = sb("low_early_bf", [P, GROUP * HALF], BF16)[:]
-        high_q = [sb("high_q%d" % u, [P, PASSES * 2 * P], U32) for u in range(2)]
-        high_sc = [sb("high_sc%d" % u, [P, PASSES * 2 * P], U8) for u in range(2)]
-
-        def prepare_high(u, rounded):
-            nc.scalar.copy(
-                rounded.rearrange("p (a t m j) -> p a m j t", a=PASSES, t=2, j=4),
-                high_raw[:].rearrange("p a j (m t) -> p a m j t", t=4)[:, :, :, :, 2 * u : 2 * u + 2],
-            )
-            quantize(high_q[u][:], high_sc[u][:], rounded)
-
-        def stationary(i, a):
-            if i < GROUP:
-                return low_q[a, i // 2], low_sc[a, i // 2], (i % 2) * P
-            return high_q[(i - GROUP) // 2], high_sc[(i - GROUP) // 2], a * 2 * P + (i % 2) * P
-
-        h_sb = []
-
-        def stage1(i):
-            h_sb.append(sb("h%d" % i, [P, S], F32))
-            pieces = [(banks[2 * (i % GROUP) + hf], hf * BANK, (hf + 1) * BANK) for hf in range(2)]
-            if i == 0:
-                pieces = [(banks[b], q * HALF, (q + 1) * HALF) for q, b in enumerate((0, 1, 6, 7))]
-            for bank, t0, t1 in pieces:
-                cols = slice(t0, t1)
-                sums = bank[:, 0 : t1 - t0]
+        def stage1(i, pieces):
+            h_sb[i] = sb("h%d" % i, [P, S], F32)
+            for b, t0, t1, copy in pieces:
                 for a in range(PASSES):
-                    codes, scales, c0 = stationary(i, a)
-                    moving = (v_w0, v_w1)[a][:, cols]
-                    nc.tensor.matmul_mx(
-                        out=sums,
-                        lhsT=codes[:, c0 : c0 + P].bitcast(FP8X4),
-                        lhsT_scale=scales[:, c0 : c0 + P],
-                        rhs=moving.bitcast(FP8X4),
-                        rhs_scale=v_sc[4 * a : P, cols],
-                        start=(a == 0),
-                        stop=(a == PASSES - 1),
-                    )
-                copy = nc.vector.tensor_copy if i == 0 and t1 % BANK else nc.scalar.copy
-                copy(h_sb[i][:, cols], sums)
+                    stage1_pass(i, a, banks[b], t0, t1)
+                copy(h_sb[i][:, t0:t1], banks[b][:, 0 : t1 - t0])
+
+        def two_banks(b0, b1):
+            return [(b0, 0, BANK, nc.scalar.copy), (b1, BANK, S, nc.scalar.copy)]
 
         def half_of(list_sb, m0):
             return list_sb[:, m0 // LIST_ROWS : (m0 + HALF) // LIST_ROWS]
 
-        def halves(ap):
-            return ap[:, 0:HALF], ap[:, HALF:PH]
-
-        def add_second(i, dst, picks, m0):
-            nc.vector.tensor_tensor(dst, h_sb[i][:].indirect(half_of(pos2_sb, m0)), picks[m0 // HALF], ALU.add)
-
-        def pick_and_add_early(i, dst, picks):
+        def pick_first(i, tag=None):
+            tile = sb("picks%d" % i, [P, PH], F32, tag=tag)
             for m0 in (0, HALF):
-                nc.vector.tensor_copy(picks[m0 // HALF], h_sb[i][:].indirect(half_of(pos1_sb, m0)))
-            add_second(i, dst, picks, 0)
+                nc.vector.tensor_copy(tile[:, m0 : m0 + HALF], h_sb[i][:].indirect(half_of(pos1_sb, m0)))
+            return tile
 
-        low = z_rows[:, 4 * HALF : 12 * HALF]
-        z_low_early = low[:, 0 : 4 * HALF].rearrange("p (t m) -> p t m", t=GROUP)
-        z_low_late = low[:, 2 * HALF : 6 * HALF].rearrange("p (t m) -> p t m", t=GROUP)
-        low_picks = [
-            (low[:, 6 * HALF : 7 * HALF], sb("late_picks0", [P, HALF], F32)[:]),
-            (sb("early_picks1", [P, HALF], F32)[:], sb("late_picks1", [P, HALF], F32)[:]),
-            halves(sb("low_picks2", [P, PH], F32)[:]),
-            halves(low[:, 6 * HALF : 8 * HALF]),
-        ]
-        low_late_bf = sb("low_late_bf", [P, GROUP * HALF], BF16)[:]
-        high_picks = [halves(sb("high_picks%d" % t, [P, PH], F32)[:]) for t in range(GROUP)]
+        def add_second(i, dst, m0):
+            nc.vector.tensor_tensor(
+                dst, h_sb[i][:].indirect(half_of(pos2_sb, m0)), picks[i][:, m0 : m0 + HALF], ALU.add)
+
+        def add_low(i, tag=None):
+            z_low[i] = sb("z_low%d" % i, [P, PH], F32, tag=tag)
+            for m0 in (0, HALF):
+                add_second(i, z_low[i][:, m0 : m0 + HALF], m0)
+
+        def turn_low(m0):
+            for m in range(m0, m0 + HALF, P):
+                for c in range(GROUP):
+                    nc.tensor.transpose(
+                        banks[turn_banks[m // P]][:, c * P : (c + 1) * P], z_low[c][:, m : m + P], identity[:])
+
+        nc.vector.tensor_copy(v_sc[:], tab_sc[:].indirect(offs_sb[:]))
+        nc.vector.tensor_copy(v_w[0][:], tab_w[0][:].indirect(offs_sb[:]))
+        bf01 = sb("bf01", [P, 2 * PASS_K], BF16)
+        weave(nc.scalar.copy, bf01[:], raw01[0][:])
+        codes, scales = quantize("w01", bf01[:], 2 * P)
+        for i in range(2):
+            weights[i, 0] = (codes, scales, i * P)
+
+        def gather_pass1(dst, t0, t1):
+            nc.vector.tensor_copy(dst, tab_w[1][:].indirect(offs_sb[:, t0 // LIST_ROWS : t1 // LIST_ROWS]))
+
+        def prepare_pass1(i):
+            rounded = sb("bf%d" % i, [P, PASS_K], BF16)
+            weave(nc.scalar.copy, rounded[:], raw01[1][:, :, i * P : (i + 1) * P])
+            weights[i, 1] = quantize("w%d" % i, rounded[:], P) + (0,)
+
+        v_w.append(sb("v_w1", [P, LAST_TOKENS], U32, tag="raw01_0"))
+        gather_pass1(v_w[1][:, 0:BANK], 0, BANK)
+        gather_pass1(v_w[1][:, BANK:LAST_TOKENS], BANK, LAST_TOKENS)
+        prepare_pass1(0)
+        v_last = sb("v_last", [P, S - LAST_TOKENS], U32, tag="bf0")
+        gather_pass1(v_last[:], LAST_TOKENS, S)
+        prepare_pass1(1)
+
+        stage1(0, [(0, 0, BANK, nc.scalar.copy), (1, BANK, BANK + HALF, nc.vector.tensor_copy),
+                   (2, BANK + HALF, S, nc.scalar.copy)])
+
+        def prepare_low(a, tag):
+            rounded = sb("bf23_%d" % a, [P, 2 * PASS_K], BF16, tag=tag)
+            weave(nc.scalar.copy, rounded[:], raw23[a][:])
+            codes, scales = quantize("w23_%d" % a, rounded[:], 2 * P)
+            for i in (2, 3):
+                weights[i, a] = (codes, scales, (i - 2) * P)
+
+        def prepare_high(name, u, a0, a1, tag):
+            rounded = sb(name + "_bf", [P, (a1 - a0) * 2 * PASS_K], BF16, tag=tag)
+            nc.scalar.copy(
+                rounded[:].rearrange("p (a t m j) -> p a m j t", a=a1 - a0, t=2, j=4),
+                high_raw[:].rearrange("p a j (m t) -> p a m j t", t=4)[:, a0:a1, :, :, 2 * u : 2 * u + 2],
+            )
+            codes, scales = quantize(name, rounded[:], (a1 - a0) * 2 * P)
+            for t in range(2):
+                for a in range(a0, a1):
+                    weights[GROUP + 2 * u + t, a] = (codes, scales, (2 * (a - a0) + t) * P)
+
+        turn_banks = (1, 2, 3, 4)
+        picks, z_low = {}, {}
+        picks[0] = pick_first(0)
+        prepare_low(0, "w0_q")
+        add_low(0, tag="raw23_0")
+        prepare_low(1, "w0_sc")
+        stage1(1, two_banks(3, 4))
+        picks[1] = pick_first(1)
+        add_low(1)
+        prepare_high("w45_0", 0, 0, 1, "w1_q")
+        stage1(2, two_banks(5, 6))
+        picks[2] = pick_first(2)
+        add_low(2)
+        h_sb[3] = sb("h3", [P, S], F32)
+        for b, t0 in ((7, 0), (0, BANK)):
+            for a in range(PASSES):
+                stage1_pass(3, a, banks[b], t0, t0 + BANK)
+        prepare_high("w45_1", 0, 1, 2, "w23_1_q")
+        for b, t0 in ((7, 0), (0, BANK)):
+            nc.scalar.copy(h_sb[3][:, t0 : t0 + BANK], banks[b][:])
+        picks[3] = pick_first(3, tag="w23_1_q")
+        add_low(3)
+        prepare_high("high1", 1, 0, 2, "w23_1_sc")
+        for i in range(GROUP, ROW_TILES):
+            stage1(i, two_banks(*((1, 2), (3, 4))[i % 2]))
+        turn_low(0)
+
+        z_high_early = sb("z_high_early", [P, GROUP, HALF], F32)
+        for t in range(GROUP):
+            picks[GROUP + t] = pick_first(GROUP + t)
+            add_second(GROUP + t, z_high_early[:, t, :], 0)
+
+        late_rows = sb("late_rows", [P, GROUP * HALF], F32, tag="high1_q")
+        z_high_late = late_rows[:].rearrange("p (t m) -> p t m", t=GROUP)
+
+        def round_turned(words, m0):
+            dst = words.bitcast(BF16).rearrange("m (b u p e) -> m b u p e", b=2, u=2, e=2)
+            for b in range(2):
+                src = banks[turn_banks[m0 // P + b]][:].rearrange("m (p u e) -> m u p e", u=2, e=2)
+                nc.scalar.copy(dst[:, b], src)
+
+        def turn_words(words, bank):
+            for w in range(0, BANK, P):
+                nc.tensor.transpose(bank[:, w : w + P], words[:, w : w + P], identity[:])
+
+        def fetch_words(name, bank):
+            rounded = sb(name, [P, GROUP * HALF], BF16)
+            nc.scalar.copy(
+                rounded[:].bitcast(F32).rearrange("p (b m u) -> p b m u", b=2, u=2),
+                bank[:].rearrange("p (b u m) -> p b m u", b=2, u=2),
+            )
+            return rounded
 
         z_q = [sb("z_q%d" % a, [P, PH], U32) for a in range(PASSES)]
         z_sc = [sb("z_sc%d" % a, [P, PH], U8) for a in range(PASSES)]
 
-        def round_z(copy, dst, src):
-            copy(dst.rearrange("p (c i t) -> p c t i", i=2, t=GROUP), src.rearrange("p t (c i) -> p c t i", i=2))
-
         def quant_z(a, m0, src):
-            quantize(z_q[a][:, m0 : m0 + HALF], z_sc[a][:, m0 : m0 + HALF], src)
+            nc.vector.quantize_mx(
+                out=z_q[a][:, m0 : m0 + HALF].bitcast(FP8X4), scales=z_sc[a][:, m0 : m0 + HALF], in_=src)
 
+        early_words = late_rows[:, 0:BANK]
+        round_turned(early_words, 0)
+        turn_words(early_words, banks[5])
+        low_early_bf = fetch_words("low_early_bf", banks[5])
+        turn_low(HALF)
+        late_words = late_rows[:, BANK : 2 * BANK]
+        round_turned(late_words, HALF)
+        turn_words(late_words, banks[6])
+        high_early_bf = late_rows[:, 0 : 2 * HALF].bitcast(BF16)
+        weave(nc.scalar.copy, high_early_bf, z_high_early[:])
+        low_late_bf = fetch_words("low_late_bf", banks[6])
+
+        quant_z(0, 0, low_early_bf[:])
+        for t in (2, 3):
+            add_second(GROUP + t, z_high_late[:, t, :], HALF)
+        quant_z(1, 0, high_early_bf)
+        for t in (0, 1):
+            add_second(GROUP + t, z_high_late[:, t, :], HALF)
+        quant_z(0, HALF, low_late_bf[:])
+
+        order = [banks[b] for b in (7, 0, 1, 2, 3, 4, 5, 6)]
         y01 = sb("y01", [P, 2 * PH], F32)
         y_sb = [y01[:, 0:PH], y01[:, PH : 2 * PH]] + [sb("y%d" % n, [P, PH], F32)[:] for n in range(2, OUT_TILES)]
 
-        def forget_mm(n0, m0, a, bank, opens):
+        def product_mm(content_side, n0, m0, a, bank, opens):
             for d in range(2):
                 n = n0 + d
+                if content_side:
+                    codes = wc_sb[:, a, 2 * n * P : 2 * (n + 1) * P].bitcast(FP4X4)
+                    scales = wcf_sc[:, a, n * P : (n + 1) * P]
+                else:
+                    codes = wf_sb[:, a, n * P : (n + 1) * P].bitcast(FP8X4)
+                    scales = wcf_sc[4:P, a, n * P : (n + 1) * P]
                 nc.tensor.matmul_mx(
                     out=bank[:, d * HALF : (d + 1) * HALF],
-                    lhsT=wf_sb[:, a, n * P : (n + 1) * P].bitcast(FP8X4),
-                    lhsT_scale=w2_sc[4:P, a, n * P : (n + 1) * P],
+                    lhsT=codes,
+                    lhsT_scale=scales,
                     rhs=z_q[a][:, m0 : m0 + HALF].bitcast(FP8X4),
                     rhs_scale=z_sc[a][:, m0 : m0 + HALF],
                     start=(opens and d == 0), stop=(not opens and d == 1),
                 )
 
-        def content_mm(n0, m0, a, bank, opens):
-            for c in range(4):
-                n, m = n0 + c // 2, m0 + (c % 2) * P
-                nc.tensor.matmul_mx(
-                    out=bank[:, c * P : (c + 1) * P],
-                    lhsT=wc_sb[:, a, 2 * n * P : 2 * (n + 1) * P].bitcast(FP4X4),
-                    lhsT_scale=w2_sc[:, a, n * P : (n + 1) * P],
-                    rhs=z_q[a][:, m : m + P].bitcast(FP8X4),
-                    rhs_scale=z_sc[a][:, m : m + P],
-                    start=(opens and c == 0), stop=(not opens and c == 3),
-                )
+        content = sb("content", [P, OUT_TILES, PH], F32, tag="tab_w1")
+        gate = sb("gate", [P, OUT_TILES, PH], F32, tag="tab_w0")
 
-        nc.vector.tensor_copy(v_w0[:], tab_w[0][:].indirect(offs_sb[:]))
-        nc.vector.tensor_copy(v_sc[:], tab_sc[:].indirect(offs_sb[:]))
-        low00 = sb("low00", [P, PAIR], BF16)[:]
-        round_low(nc.scalar.copy, low00, 0, 0)
-        quant_low(0, 0, low00)
-        low01 = sb("low01", [P, PAIR], BF16)[:]
-        round_low(nc.scalar.copy, low01, 0, 1)
-        v_w1 = sb("v_w1", [P, S], U32, tag="low00")
-        nc.vector.tensor_copy(v_w1[:], tab_w[1][:].indirect(offs_sb[:]))
-        low10 = placed.tile([P, PAIR], BF16, name="low10", align_bytes=64, offset=0)[:]
-        low11 = placed.tile([P, PAIR], BF16, name="low11", align_bytes=64, offset=2 * PAIR)[:]
-        round_low(nc.scalar.copy, low10, 1, 0, 0, SCALAR_WORDS)
-        round_low(nc.vector.tensor_copy, low10, 1, 0, SCALAR_WORDS, P)
-        low_q[1, 0] = sb("low_q10", [P, 2 * P], U32)
-        low_sc[1, 0] = sb("low_sc10", [P, 2 * P], U8)
-        for t in range(2):
-            cols = slice(t * P, (t + 1) * P)
-            quantize(low_q[1, 0][:, cols], low_sc[1, 0][:, cols], low10[:, t * PASS_K : (t + 1) * PASS_K])
-        quant_low(0, 1, low01, placed.tile([P, 2 * P], U32, name="low_q01", align_bytes=64, offset=0))
-        round_low(nc.scalar.copy, low11, 1, 1)
-        quant_low(1, 1, low11)
-
-        for i in range(2):
-            stage1(i)
-        for r in range(WARM_PASSES):
-            nc.tensor.matmul_mx(
-                out=banks[4][:],
-                lhsT=low_q[0, 0][:, 0:P].bitcast(FP8X4),
-                lhsT_scale=low_sc[0, 0][:, 0:P],
-                rhs=v_w0[:, 0:BANK].bitcast(FP8X4),
-                rhs_scale=v_sc[:, 0:BANK],
-                start=(r == 0),
-                stop=(r == WARM_PASSES - 1),
-            )
-        stage1(2)
-        pick_and_add_early(0, z_low_early[:, 0, :], low_picks[0])
-        pick_and_add_early(1, z_low_early[:, 1, :], low_picks[1])
-        prepare_high(0, low[:, 4 * HALF : 8 * HALF].bitcast(BF16))
-        stage1(3)
-        prepare_high(1, sb("high_bf1", [P, PASSES * PAIR], BF16, tag="early_picks1")[:])
-        pick_and_add_early(2, z_low_early[:, 2, :], low_picks[2])
-        add_second(2, z_low_late[:, 2, :], low_picks[2], HALF)
-        pick_and_add_early(3, z_low_early[:, 3, :], low_picks[3])
-        add_second(3, z_low_late[:, 3, :], low_picks[3], HALF)
-        for i in range(GROUP, ROW_TILES):
-            stage1(i)
-
-        content = sb("content", [P, OUT_TILES, PH], F32, tag="high_raw")
-        gate = sb("gate", [P, OUT_TILES, PH], F32)
+        def two(ap):
+            return ap.rearrange("p (d m) -> p d m", d=2)
 
         def gate_act(n0, m0, bank):
-            nc.scalar.activation(
-                gate[:, n0 : n0 + 2, m0 : m0 + HALF], bank[:].rearrange("p (d m) -> p d m", d=2), ACT.Sigmoid)
+            nc.scalar.activation(gate[:, n0 : n0 + 2, m0 : m0 + HALF], two(bank[:]), ACT.Sigmoid)
 
         def content_act(n0, m0, bank):
-            nc.scalar.activation(
-                content[:, n0 : n0 + 2, m0 : m0 + HALF], bank[:].rearrange("p (d m) -> p d m", d=2), ACT.Tanh)
+            nc.scalar.activation(content[:, n0 : n0 + 2, m0 : m0 + HALF], two(bank[:]), ACT.Tanh)
 
         def gated_mem(engine, dst, n0, m0):
             cols = slice(m0, m0 + HALF)
@@ -303,41 +342,23 @@ def tile_list_phrase_tree_forget_kernel(
         def state(engine, gated, n0, m0):
             cols = slice(m0, m0 + HALF)
             if n0 == 0:
-                pair = y01[:].rearrange("p (d m) -> p d m", d=2)
-                engine.tensor_tensor(pair[:, :, cols], gated, content[:, 0:2, cols], ALU.add)
+                engine.tensor_tensor(two(y01[:])[:, :, cols], gated, content[:, 0:2, cols], ALU.add)
             else:
                 for d in range(2):
                     engine.tensor_tensor(y_sb[n0 + d][:, cols], gated[:, d, :], content[:, n0 + d, cols], ALU.add)
 
-        for t in range(GROUP):
-            pick_and_add_early(GROUP + t, z_high_early[:, t, :], high_picks[t])
-        round_z(nc.scalar.copy, low_early_bf, z_low_early)
-        quant_z(0, 0, low_early_bf)
-
-        z_high_late = z_rows[:, HALF : 5 * HALF].rearrange("p (t m) -> p t m", t=GROUP)
-        high_early_bf = sb("high_early_bf", [P, GROUP * HALF], BF16)[:]
-        round_z(nc.scalar.copy, high_early_bf, z_high_early)
-        quant_z(1, 0, high_early_bf)
-
-        for i in range(2):
-            add_second(i, z_low_late[:, i, :], low_picks[i], HALF)
-        round_z(nc.scalar.copy, low_late_bf, z_low_late)
-        for t in (3, 0, 1, 2):
-            add_second(GROUP + t, z_high_late[:, t, :], high_picks[t], HALF)
-        quant_z(0, HALF, low_late_bf)
         for b in range(OUT_TILES):
-            product = content_mm if b % 2 else forget_mm
             opening = 0 if b < OPEN_EARLY else 1
-            product(b - b % 2, 0, opening, banks[b], True)
-            product(b - b % 2, 0, 1 - opening, banks[b], False)
-        forget_mm(0, HALF, 0, banks[6], True)
-        content_mm(0, HALF, 0, banks[7], True)
+            product_mm(b % 2, b - b % 2, 0, opening, order[b], True)
+            product_mm(b % 2, b - b % 2, 0, 1 - opening, order[b], False)
+        for side in range(2):
+            product_mm(side, 0, HALF, 0, order[6 + side], True)
 
         for j in range(3):
-            gate_act(2 * j, 0, banks[2 * j])
-            content_act(2 * j, 0, banks[2 * j + 1])
+            gate_act(2 * j, 0, order[2 * j])
+            content_act(2 * j, 0, order[2 * j + 1])
         high_late_bf = sb("high_late_bf", [P, GROUP * HALF], BF16)
-        round_z(nc.vector.tensor_copy, high_late_bf[:], z_high_late)
+        weave(nc.vector.tensor_copy, high_late_bf[:], z_high_late)
         quant_z(1, HALF, high_late_bf[:])
         early0 = gated_mem(nc.vector, z_high_late[:, 0:2, :], 0, 0)
         in_place(4, 0)
@@ -345,16 +366,16 @@ def tile_list_phrase_tree_forget_kernel(
         state(nc.vector, in_place(2, 0), 2, 0)
 
         late_banks = ((6, 7), (0, 1), (2, 3))
-        forget_mm(0, HALF, 1, banks[6], False)
+        product_mm(0, 0, HALF, 1, order[6], False)
         for a in range(PASSES):
-            forget_mm(2, HALF, a, banks[0], a == 0)
-        content_mm(0, HALF, 1, banks[7], False)
+            product_mm(0, 2, HALF, a, order[0], a == 0)
+        product_mm(1, 0, HALF, 1, order[7], False)
         for j in (1, 2):
             for a in range(PASSES):
-                content_mm(2 * j, HALF, a, banks[late_banks[j][1]], a == 0)
+                product_mm(1, 2 * j, HALF, a, order[late_banks[j][1]], a == 0)
             if j == 1:
                 for a in range(PASSES):
-                    forget_mm(4, HALF, a, banks[2], a == 0)
+                    product_mm(0, 4, HALF, a, order[2], a == 0)
 
         def turned_sum(n, bank, turned):
             for m in range(0, HALF, P):
@@ -371,17 +392,15 @@ def tile_list_phrase_tree_forget_kernel(
 
         for act, side in ((gate_act, 0), (content_act, 1)):
             for j in range(2):
-                act(2 * j, HALF, banks[late_banks[j][side]])
-        gate_act(4, HALF, banks[2])
-        content_act(4, HALF, banks[3])
+                act(2 * j, HALF, order[late_banks[j][side]])
+        gate_act(4, HALF, order[2])
+        content_act(4, HALF, order[3])
         last = sb("last", [P, 6 * HALF], F32)
         turned = {n: last[:, (n - 4) * HALF : (n - 3) * HALF] for n in (4, 5)}
         for n in (4, 5):
-            turned_sum(n, banks[n + 2], turned[n])
+            turned_sum(n, order[n + 2], turned[n])
         for n in (4, 5):
-            turn_back(n, turned[n], banks[n])
-        def two(ap):
-            return ap.rearrange("p (d m) -> p d m", d=2)
+            turn_back(n, turned[n], order[n])
 
         late0 = in_place(0, HALF)
         late2 = gated_mem(nc.vector, two(last[:, 15 * HALF // 4 : 23 * HALF // 4]), 2, HALF)

@@ -27,7 +27,8 @@ OUT_TILES = N // P
 HALF = PH // 2
 LIST_ROWS = 16
 LAST_TOKENS = 768
-OPEN_EARLY = 3
+HELD = 64
+OPEN_EARLY = 2
 
 
 def tile_list_phrase_tree_forget_kernel(
@@ -37,6 +38,7 @@ def tile_list_phrase_tree_forget_kernel(
     nc = tc.nc
     with ExitStack() as ctx:
         keep = ctx.enter_context(tc.tile_pool(name="keep", bufs=1))
+        placed = ctx.enter_context(tc.tile_pool(name="placed", bufs=1))
         psum = ctx.enter_context(tc.psum_pool(name="psum", bufs=1))
 
         def sb(name, shape, dtype, tag=None):
@@ -74,16 +76,20 @@ def tile_list_phrase_tree_forget_kernel(
                 tab_words[a].rearrange("p t i -> p (t i)").bitcast(I32),
             )
 
-        def load_w1(name, a, c0, c1):
-            tile = sb(name, [P, 4, c1 - c0], F32)
+        def at(name, shape, offset):
+            return placed.tile(shape, F32, name=name, align_bytes=64, offset=offset)
+
+        def load_w1(name, a, c0, c1, offset=None):
+            tile = sb(name, [P, 4, c1 - c0], F32) if offset is None else at(name, [P, 4, c1 - c0], offset)
             nc.sync.dma_start(tile[:], w1[PASS_K * a : PASS_K * (a + 1), c0:c1].rearrange("(p j) c -> p j c", j=4))
             return tile
 
         load_tab(0)
-        raw01 = [load_w1("raw01_0", 0, 0, 2 * P)]
+        raw0 = [load_w1("raw0_0", 0, 0, P)]
         load_tab(1)
-        raw01.append(load_w1("raw01_1", 1, 0, 2 * P))
-        raw23 = [load_w1("raw23_%d" % a, a, 2 * P, 4 * P) for a in range(PASSES)]
+        raw0.append(load_w1("raw0_1", 1, 0, P))
+        raw1 = [load_w1("raw1_%d" % a, a, P, 2 * P) for a in range(PASSES)]
+        raw23 = [load_w1("raw23_0", 0, 2 * P, 4 * P), load_w1("raw23_1", 1, 2 * P, 4 * P, offset=0)]
         high_raw = sb("high_raw", [P, PASSES, 4, PASS_K], F32)
         for a in range(PASSES):
             rows = slice(PASS_K * a, PASS_K * (a + 1))
@@ -125,21 +131,19 @@ def tile_list_phrase_tree_forget_kernel(
 
         def stage1_pass(i, a, bank, t0, t1):
             codes, scales, c0 = weights[i, a]
-            cuts = [t0, LAST_TOKENS, t1] if a == 1 and t0 < LAST_TOKENS < t1 else [t0, t1]
-            for u0, u1 in zip(cuts, cuts[1:]):
-                words = v_last[:] if a == 1 and u0 == LAST_TOKENS else v_w[a][:, u0:u1]
-                nc.tensor.matmul_mx(
-                    out=bank[:, u0 - t0 : u1 - t0],
-                    lhsT=codes[:, c0 : c0 + P].bitcast(FP8X4),
-                    lhsT_scale=scales[:, c0 : c0 + P],
-                    rhs=words.bitcast(FP8X4),
-                    rhs_scale=v_sc[4 * a : P, u0:u1],
-                    start=(a == 0),
-                    stop=(a == PASSES - 1 and u1 == t1),
-                )
+            words = v_last[:, t0 - BANK : t1 - BANK] if a == 1 and t0 >= BANK else v_w[a][:, t0:t1]
+            nc.tensor.matmul_mx(
+                out=bank[:, 0 : t1 - t0],
+                lhsT=codes[:, c0 : c0 + P].bitcast(FP8X4),
+                lhsT_scale=scales[:, c0 : c0 + P],
+                rhs=words.bitcast(FP8X4),
+                rhs_scale=v_sc[4 * a : P, t0:t1],
+                start=(a == 0),
+                stop=(a == PASSES - 1),
+            )
 
-        def stage1(i, pieces):
-            h_sb[i] = sb("h%d" % i, [P, S], F32)
+        def stage1(i, pieces, tile=None):
+            h_sb[i] = sb("h%d" % i, [P, S], F32) if tile is None else tile
             for b, t0, t1, copy in pieces:
                 for a in range(PASSES):
                     stage1_pass(i, a, banks[b], t0, t1)
@@ -151,8 +155,8 @@ def tile_list_phrase_tree_forget_kernel(
         def half_of(list_sb, m0):
             return list_sb[:, m0 // LIST_ROWS : (m0 + HALF) // LIST_ROWS]
 
-        def pick_first(i, tag=None):
-            tile = sb("picks%d" % i, [P, PH], F32, tag=tag)
+        def pick_first(i, tile=None):
+            tile = sb("picks%d" % i, [P, PH], F32)[:] if tile is None else tile
             for m0 in (0, HALF):
                 nc.vector.tensor_copy(tile[:, m0 : m0 + HALF], h_sb[i][:].indirect(half_of(pos1_sb, m0)))
             return tile
@@ -161,8 +165,8 @@ def tile_list_phrase_tree_forget_kernel(
             nc.vector.tensor_tensor(
                 dst, h_sb[i][:].indirect(half_of(pos2_sb, m0)), picks[i][:, m0 : m0 + HALF], ALU.add)
 
-        def add_low(i, tag=None):
-            z_low[i] = sb("z_low%d" % i, [P, PH], F32, tag=tag)
+        def add_low(i, tile=None):
+            z_low[i] = sb("z_low%d" % i, [P, PH], F32) if tile is None else tile
             for m0 in (0, HALF):
                 add_second(i, z_low[i][:, m0 : m0 + HALF], m0)
 
@@ -174,93 +178,109 @@ def tile_list_phrase_tree_forget_kernel(
 
         nc.vector.tensor_copy(v_sc[:], tab_sc[:].indirect(offs_sb[:]))
         nc.vector.tensor_copy(v_w[0][:], tab_w[0][:].indirect(offs_sb[:]))
-        bf01 = sb("bf01", [P, 2 * PASS_K], BF16)
-        weave(nc.scalar.copy, bf01[:], raw01[0][:])
-        codes, scales = quantize("w01", bf01[:], 2 * P)
-        for i in range(2):
-            weights[i, 0] = (codes, scales, i * P)
+        bf00 = sb("bf00", [P, PASS_K], BF16)
+        weave(nc.scalar.copy, bf00[:], raw0[0][:])
+        weights[0, 0] = quantize("w00", bf00[:], P) + (0,)
 
         def gather_pass1(dst, t0, t1):
             nc.vector.tensor_copy(dst, tab_w[1][:].indirect(offs_sb[:, t0 // LIST_ROWS : t1 // LIST_ROWS]))
 
-        def prepare_pass1(i):
-            rounded = sb("bf%d" % i, [P, PASS_K], BF16)
-            weave(nc.scalar.copy, rounded[:], raw01[1][:, :, i * P : (i + 1) * P])
-            weights[i, 1] = quantize("w%d" % i, rounded[:], P) + (0,)
+        v_w.append(sb("v_w1", [P, BANK], U32, tag="raw0_0"))
+        gather_pass1(v_w[1][:], 0, BANK)
+        bf0 = sb("bf0", [P, PASS_K], BF16)
+        weave(nc.scalar.copy, bf0[:], raw0[1][:])
+        weights[0, 1] = quantize("w0", bf0[:], P) + (0,)
+        v_last = sb("v_last", [P, BANK], U32, tag="raw0_1")
+        gather_pass1(v_last[:, 0 : LAST_TOKENS - BANK], BANK, LAST_TOKENS)
+        gather_pass1(v_last[:, LAST_TOKENS - BANK : BANK], LAST_TOKENS, S)
+        bf1 = sb("bf1", [P, PASSES, PASS_K], BF16)
+        for a in range(PASSES):
+            weave(nc.scalar.copy, bf1[:, a, :], raw1[a][:])
+        bf23 = [sb("bf23_0", [P, 2 * PASS_K], BF16, tag="bf0")]
+        weave(nc.vector.tensor_copy, bf23[0][:], raw23[0][:])
+        codes, scales = quantize("w1", bf1[:].rearrange("p a c -> p (a c)"), PASSES * P)
+        for a in range(PASSES):
+            weights[1, a] = (codes, scales, a * P)
 
-        v_w.append(sb("v_w1", [P, LAST_TOKENS], U32, tag="raw01_0"))
-        gather_pass1(v_w[1][:, 0:BANK], 0, BANK)
-        gather_pass1(v_w[1][:, BANK:LAST_TOKENS], BANK, LAST_TOKENS)
-        prepare_pass1(0)
-        v_last = sb("v_last", [P, S - LAST_TOKENS], U32, tag="bf0")
-        gather_pass1(v_last[:], LAST_TOKENS, S)
-        prepare_pass1(1)
+        stage1(0, [(0, 0, BANK, nc.scalar.copy), (1, BANK, LAST_TOKENS, nc.scalar.copy),
+                   (2, LAST_TOKENS, S, nc.scalar.copy)], sb("h0", [P, S], F32, tag="raw1_1"))
 
-        stage1(0, [(0, 0, BANK, nc.scalar.copy), (1, BANK, BANK + HALF, nc.vector.tensor_copy),
-                   (2, BANK + HALF, S, nc.scalar.copy)])
-
-        def prepare_low(a, tag):
-            rounded = sb("bf23_%d" % a, [P, 2 * PASS_K], BF16, tag=tag)
-            weave(nc.scalar.copy, rounded[:], raw23[a][:])
-            codes, scales = quantize("w23_%d" % a, rounded[:], 2 * P)
+        def quantize23(a):
+            codes, scales = quantize("w23_%d" % a, bf23[a][:], 2 * P)
             for i in (2, 3):
                 weights[i, a] = (codes, scales, (i - 2) * P)
 
-        def prepare_high(name, u, a0, a1, tag):
+        def prepare_high(name, u, a0, a1, tag, tiles=2):
             rounded = sb(name + "_bf", [P, (a1 - a0) * 2 * PASS_K], BF16, tag=tag)
             nc.scalar.copy(
                 rounded[:].rearrange("p (a t m j) -> p a m j t", a=a1 - a0, t=2, j=4),
                 high_raw[:].rearrange("p a j (m t) -> p a m j t", t=4)[:, a0:a1, :, :, 2 * u : 2 * u + 2],
             )
-            codes, scales = quantize(name, rounded[:], (a1 - a0) * 2 * P)
-            for t in range(2):
-                for a in range(a0, a1):
-                    weights[GROUP + 2 * u + t, a] = (codes, scales, (2 * (a - a0) + t) * P)
+            order = [(GROUP + 2 * u + t, a) for a in range(a0, a1) for t in range(2)]
+            for s0 in range(0, len(order), tiles):
+                piece = rounded[:, s0 * PASS_K : (s0 + tiles) * PASS_K]
+                codes, scales = quantize("%s_%d" % (name, s0), piece, tiles * P)
+                for s in range(tiles):
+                    weights[order[s0 + s]] = (codes, scales, s * P)
+            return rounded
 
         turn_banks = (1, 2, 3, 4)
         picks, z_low = {}, {}
+        quantize23(0)
         picks[0] = pick_first(0)
-        prepare_low(0, "w0_q")
-        add_low(0, tag="raw23_0")
-        prepare_low(1, "w0_sc")
-        stage1(1, two_banks(3, 4))
+        bf23.append(sb("bf23_1", [P, 2 * PASS_K], BF16, tag="w0_q"))
+        weave(nc.scalar.copy, bf23[1][:], raw23[1][:])
+        quantize23(1)
+        add_low(0, at("z_low0", [P, PH], 0))
+        stage1(1, two_banks(0, 1), at("h1", [P, S], 4 * PH))
         picks[1] = pick_first(1)
         add_low(1)
         prepare_high("w45_0", 0, 0, 1, "w1_q")
-        stage1(2, two_banks(5, 6))
+        stage1(2, two_banks(3, 4))
         picks[2] = pick_first(2)
         add_low(2)
-        h_sb[3] = sb("h3", [P, S], F32)
-        for b, t0 in ((7, 0), (0, BANK)):
-            for a in range(PASSES):
-                stage1_pass(3, a, banks[b], t0, t0 + BANK)
-        prepare_high("w45_1", 0, 1, 2, "w23_1_q")
-        for b, t0 in ((7, 0), (0, BANK)):
-            nc.scalar.copy(h_sb[3][:, t0 : t0 + BANK], banks[b][:])
-        picks[3] = pick_first(3, tag="w23_1_q")
-        add_low(3)
-        prepare_high("high1", 1, 0, 2, "w23_1_sc")
-        for i in range(GROUP, ROW_TILES):
-            stage1(i, two_banks(*((1, 2), (3, 4))[i % 2]))
+        stage1(3, two_banks(5, 6))
+        rounded45 = prepare_high("w45_1", 0, 1, 2, "w23_1_q", tiles=1)
+        picks[3] = pick_first(3, rounded45[:].bitcast(F32))
+        prepare_high("w67", 1, 0, 2, "w23_1_sc", tiles=4)
+        add_low(3, sb("z_low3", [P, PH], F32, tag="high_raw"))
+        for i, (b0, b1, b2, b3) in ((4, (1, 2, 3, 4)), (6, (7, 0, 5, 6))):
+            h_sb[i] = sb("h%d" % i, [P, S], F32)
+            for b, t0 in ((b0, 0), (b1, BANK)):
+                for a in range(PASSES):
+                    stage1_pass(i, a, banks[b], t0, t0 + BANK)
+            nc.scalar.copy(h_sb[i][:, 0:BANK], banks[b0][:])
+            nc.scalar.copy(h_sb[i][:, BANK : S - HELD], banks[b1][:, 0 : BANK - HELD])
+            stage1(i + 1, two_banks(b2, b3))
+            nc.scalar.copy(h_sb[i][:, S - HELD : S], banks[b1][:, BANK - HELD : BANK])
         turn_low(0)
 
-        z_high_early = sb("z_high_early", [P, GROUP, HALF], F32)
-        for t in range(GROUP):
-            picks[GROUP + t] = pick_first(GROUP + t)
-            add_second(GROUP + t, z_high_early[:, t, :], 0)
+        rows = sb("rows", [P, 8, HALF], F32)
+        z_high_early, z_high = rows[:, 0:4, :], rows[:, 2:6, :]
+        early_picks = sb("early_picks", [P, GROUP, HALF], F32)
+        late_picks = [rows[:, r, :] for r in (6, 7, 0, 1)]
 
-        late_rows = sb("late_rows", [P, GROUP * HALF], F32, tag="high1_q")
-        z_high_late = late_rows[:].rearrange("p (t m) -> p t m", t=GROUP)
+        def pick_high(t, dst, m0):
+            nc.vector.tensor_copy(dst, h_sb[GROUP + t][:].indirect(half_of(pos1_sb, m0)))
+
+        def add_high(t, dst, first, m0):
+            nc.vector.tensor_tensor(dst, h_sb[GROUP + t][:].indirect(half_of(pos2_sb, m0)), first, ALU.add)
+
+        for pair in ((1, 0), (3, 2)):
+            for t in pair:
+                pick_high(t, early_picks[:, t, :], 0)
+            for t in pair:
+                add_high(t, z_high_early[:, t, :], early_picks[:, t, :], 0)
 
         def round_turned(words, m0):
-            dst = words.bitcast(BF16).rearrange("m (b u p e) -> m b u p e", b=2, u=2, e=2)
             for b in range(2):
+                dst = words[:, 2 * b : 2 * b + 2, :].bitcast(BF16).rearrange("m u (p e) -> m u p e", e=2)
                 src = banks[turn_banks[m0 // P + b]][:].rearrange("m (p u e) -> m u p e", u=2, e=2)
-                nc.scalar.copy(dst[:, b], src)
+                nc.scalar.copy(dst, src)
 
         def turn_words(words, bank):
-            for w in range(0, BANK, P):
-                nc.tensor.transpose(bank[:, w : w + P], words[:, w : w + P], identity[:])
+            for w in range(4):
+                nc.tensor.transpose(bank[:, w * P : (w + 1) * P], words[:, w, :], identity[:])
 
         def fetch_words(name, bank):
             rounded = sb(name, [P, GROUP * HALF], BF16)
@@ -277,24 +297,26 @@ def tile_list_phrase_tree_forget_kernel(
             nc.vector.quantize_mx(
                 out=z_q[a][:, m0 : m0 + HALF].bitcast(FP8X4), scales=z_sc[a][:, m0 : m0 + HALF], in_=src)
 
-        early_words = late_rows[:, 0:BANK]
+        early_words = sb("early_words", [P, 4, P], F32)[:]
         round_turned(early_words, 0)
         turn_words(early_words, banks[5])
         low_early_bf = fetch_words("low_early_bf", banks[5])
         turn_low(HALF)
-        late_words = late_rows[:, BANK : 2 * BANK]
+        late_words = rows[:, 6:8, :].rearrange("p r (w m) -> p (r w) m", w=2)
         round_turned(late_words, HALF)
         turn_words(late_words, banks[6])
-        high_early_bf = late_rows[:, 0 : 2 * HALF].bitcast(BF16)
-        weave(nc.scalar.copy, high_early_bf, z_high_early[:])
+        high_early_bf = sb("high_early_bf", [P, GROUP * HALF], BF16, tag="early_words")[:]
+        weave(nc.scalar.copy, high_early_bf, z_high_early)
         low_late_bf = fetch_words("low_late_bf", banks[6])
 
         quant_z(0, 0, low_early_bf[:])
-        for t in (2, 3):
-            add_second(GROUP + t, z_high_late[:, t, :], HALF)
+        for t in range(2):
+            pick_high(t, late_picks[t], HALF)
         quant_z(1, 0, high_early_bf)
-        for t in (0, 1):
-            add_second(GROUP + t, z_high_late[:, t, :], HALF)
+        for t in range(2, GROUP):
+            pick_high(t, late_picks[t], HALF)
+        for t in range(GROUP):
+            add_high(t, z_high[:, t, :], late_picks[t], HALF)
         quant_z(0, HALF, low_late_bf[:])
 
         order = [banks[b] for b in (7, 0, 1, 2, 3, 4, 5, 6)]
@@ -358,9 +380,9 @@ def tile_list_phrase_tree_forget_kernel(
             gate_act(2 * j, 0, order[2 * j])
             content_act(2 * j, 0, order[2 * j + 1])
         high_late_bf = sb("high_late_bf", [P, GROUP * HALF], BF16)
-        weave(nc.vector.tensor_copy, high_late_bf[:], z_high_late)
+        weave(nc.vector.tensor_copy, high_late_bf[:], z_high)
         quant_z(1, HALF, high_late_bf[:])
-        early0 = gated_mem(nc.vector, z_high_late[:, 0:2, :], 0, 0)
+        early0 = gated_mem(nc.vector, z_high[:, 0:2, :], 0, 0)
         in_place(4, 0)
         state(nc.vector, early0, 0, 0)
         state(nc.vector, in_place(2, 0), 2, 0)

@@ -28,7 +28,10 @@ HALF = PH // 2
 LIST_ROWS = 16
 LAST_TOKENS = 768
 HELD = 64
-OPEN_EARLY = 2
+KIB = 1024
+TAIL = 6 * KIB
+WARM_PASSES = 3
+OPEN_EARLY = 6
 
 
 def tile_list_phrase_tree_forget_kernel(
@@ -155,20 +158,13 @@ def tile_list_phrase_tree_forget_kernel(
         def half_of(list_sb, m0):
             return list_sb[:, m0 // LIST_ROWS : (m0 + HALF) // LIST_ROWS]
 
-        def pick_first(i, tile=None):
-            tile = sb("picks%d" % i, [P, PH], F32)[:] if tile is None else tile
-            for m0 in (0, HALF):
-                nc.vector.tensor_copy(tile[:, m0 : m0 + HALF], h_sb[i][:].indirect(half_of(pos1_sb, m0)))
-            return tile
+        def pick_whole(i, dst):
+            nc.vector.tensor_copy(dst, h_sb[i][:].indirect(pos1_sb[:]))
+            return dst
 
-        def add_second(i, dst, m0):
-            nc.vector.tensor_tensor(
-                dst, h_sb[i][:].indirect(half_of(pos2_sb, m0)), picks[i][:, m0 : m0 + HALF], ALU.add)
-
-        def add_low(i, tile=None):
-            z_low[i] = sb("z_low%d" % i, [P, PH], F32) if tile is None else tile
-            for m0 in (0, HALF):
-                add_second(i, z_low[i][:, m0 : m0 + HALF], m0)
+        def add_whole(i, tile):
+            z_low[i] = tile
+            nc.vector.tensor_tensor(tile, h_sb[i][:].indirect(pos2_sb[:]), picks[i], ALU.add)
 
         def turn_low(m0):
             for m in range(m0, m0 + HALF, P):
@@ -210,10 +206,11 @@ def tile_list_phrase_tree_forget_kernel(
             for i in (2, 3):
                 weights[i, a] = (codes, scales, (i - 2) * P)
 
-        def prepare_high(name, u, a0, a1, tag, tiles=2):
-            rounded = sb(name + "_bf", [P, (a1 - a0) * 2 * PASS_K], BF16, tag=tag)
+        def prepare_high(name, u, a0, a1, tag, tiles=2, spare=0):
+            tile = sb(name + "_bf", [P, spare + (a1 - a0) * 2 * PASS_K], BF16, tag=tag)
+            rounded = tile[:, spare:]
             nc.scalar.copy(
-                rounded[:].rearrange("p (a t m j) -> p a m j t", a=a1 - a0, t=2, j=4),
+                rounded.rearrange("p (a t m j) -> p a m j t", a=a1 - a0, t=2, j=4),
                 high_raw[:].rearrange("p a j (m t) -> p a m j t", t=4)[:, a0:a1, :, :, 2 * u : 2 * u + 2],
             )
             order = [(GROUP + 2 * u + t, a) for a in range(a0, a1) for t in range(2)]
@@ -222,28 +219,34 @@ def tile_list_phrase_tree_forget_kernel(
                 codes, scales = quantize("%s_%d" % (name, s0), piece, tiles * P)
                 for s in range(tiles):
                     weights[order[s0 + s]] = (codes, scales, s * P)
-            return rounded
+            return tile
 
         turn_banks = (1, 2, 3, 4)
         picks, z_low = {}, {}
         quantize23(0)
-        picks[0] = pick_first(0)
+        picks[0] = pick_whole(0, sb("picks0", [P, PH], F32)[:])
         bf23.append(sb("bf23_1", [P, 2 * PASS_K], BF16, tag="w0_q"))
         weave(nc.scalar.copy, bf23[1][:], raw23[1][:])
         quantize23(1)
-        add_low(0, at("z_low0", [P, PH], 0))
+        add_whole(0, at("z_low0", [P, PH], 0)[:])
         stage1(1, two_banks(0, 1), at("h1", [P, S], 4 * PH))
-        picks[1] = pick_first(1)
-        add_low(1)
+        picks[1] = sb("picks1", [P, PH], F32)
+        z_low[1] = sb("z_low1", [P, PH], F32)
+        for m0 in (0, HALF):
+            nc.vector.tensor_copy(picks[1][:, m0 : m0 + HALF], h_sb[1][:].indirect(half_of(pos1_sb, m0)))
+        for m0 in (0, HALF):
+            cols = slice(m0, m0 + HALF)
+            nc.vector.tensor_tensor(
+                z_low[1][:, cols], h_sb[1][:].indirect(half_of(pos2_sb, m0)), picks[1][:, cols], ALU.add)
         prepare_high("w45_0", 0, 0, 1, "w1_q")
         stage1(2, two_banks(3, 4))
-        picks[2] = pick_first(2)
-        add_low(2)
+        picks[2] = pick_whole(2, sb("picks2", [P, PH], F32)[:])
         stage1(3, two_banks(5, 6))
-        rounded45 = prepare_high("w45_1", 0, 1, 2, "w23_1_q", tiles=1)
-        picks[3] = pick_first(3, rounded45[:].bitcast(F32))
+        picks[3] = pick_whole(3, sb("picks3", [P, PH], F32)[:])
+        rounded45 = prepare_high("w45_1", 0, 1, 2, "w23_1_q", tiles=1, spare=PASS_K)
+        add_whole(2, rounded45[:].bitcast(F32)[:, 0:PH])
         prepare_high("w67", 1, 0, 2, "w23_1_sc", tiles=4)
-        add_low(3, sb("z_low3", [P, PH], F32, tag="high_raw"))
+        add_whole(3, sb("z_low3", [P, PH], F32, tag="high_raw")[:])
         for i, (b0, b1, b2, b3) in ((4, (1, 2, 3, 4)), (6, (7, 0, 5, 6))):
             h_sb[i] = sb("h%d" % i, [P, S], F32)
             for b, t0 in ((b0, 0), (b1, BANK)):
@@ -255,10 +258,9 @@ def tile_list_phrase_tree_forget_kernel(
             nc.scalar.copy(h_sb[i][:, S - HELD : S], banks[b1][:, BANK - HELD : BANK])
         turn_low(0)
 
-        rows = sb("rows", [P, 8, HALF], F32)
-        z_high_early, z_high = rows[:, 0:4, :], rows[:, 2:6, :]
+        z_high_early = at("z_high_early", [P, GROUP, HALF], TAIL + 10 * KIB)[:]
         early_picks = sb("early_picks", [P, GROUP, HALF], F32)
-        late_picks = [rows[:, r, :] for r in (6, 7, 0, 1)]
+        rows = sb("rows", [P, 2, HALF], F32)
 
         def pick_high(t, dst, m0):
             nc.vector.tensor_copy(dst, h_sb[GROUP + t][:].indirect(half_of(pos1_sb, m0)))
@@ -274,13 +276,14 @@ def tile_list_phrase_tree_forget_kernel(
 
         def round_turned(words, m0):
             for b in range(2):
-                dst = words[:, 2 * b : 2 * b + 2, :].bitcast(BF16).rearrange("m u (p e) -> m u p e", e=2)
+                dst = words[b].bitcast(BF16).rearrange("m (u p e) -> m u p e", u=2, e=2)
                 src = banks[turn_banks[m0 // P + b]][:].rearrange("m (p u e) -> m u p e", u=2, e=2)
                 nc.scalar.copy(dst, src)
 
         def turn_words(words, bank):
             for w in range(4):
-                nc.tensor.transpose(bank[:, w * P : (w + 1) * P], words[:, w, :], identity[:])
+                nc.tensor.transpose(
+                    bank[:, w * P : (w + 1) * P], words[w // 2][:, (w % 2) * P : (w % 2 + 1) * P], identity[:])
 
         def fetch_words(name, bank):
             rounded = sb(name, [P, GROUP * HALF], BF16)
@@ -297,21 +300,31 @@ def tile_list_phrase_tree_forget_kernel(
             nc.vector.quantize_mx(
                 out=z_q[a][:, m0 : m0 + HALF].bitcast(FP8X4), scales=z_sc[a][:, m0 : m0 + HALF], in_=src)
 
-        early_words = sb("early_words", [P, 4, P], F32)[:]
+        early_words = [rows[:, 0, :], rows[:, 1, :]]
         round_turned(early_words, 0)
         turn_words(early_words, banks[5])
         low_early_bf = fetch_words("low_early_bf", banks[5])
+        for r in range(WARM_PASSES):
+            codes, scales, c0 = weights[0, 0]
+            nc.tensor.matmul_mx(
+                out=banks[2][:], lhsT=codes[:].bitcast(FP8X4), lhsT_scale=scales[:],
+                rhs=v_w[0][:, 0:BANK].bitcast(FP8X4), rhs_scale=v_sc[:, 0:BANK],
+                start=(r == 0), stop=(r == WARM_PASSES - 1),
+            )
         turn_low(HALF)
-        late_words = rows[:, 6:8, :].rearrange("p r (w m) -> p (r w) m", w=2)
+        late_words = [sb("late_words%d" % b, [P, HALF], F32)[:] for b in range(2)]
         round_turned(late_words, HALF)
         turn_words(late_words, banks[6])
-        high_early_bf = sb("high_early_bf", [P, GROUP * HALF], BF16, tag="early_words")[:]
+        high_early_bf = sb("high_early_bf", [P, GROUP * HALF], BF16, tag="high_raw")[:]
         weave(nc.scalar.copy, high_early_bf, z_high_early)
         low_late_bf = fetch_words("low_late_bf", banks[6])
 
-        quant_z(0, 0, low_early_bf[:])
+        late_picks67 = at("late_picks67", [P, 2, HALF], TAIL + 12 * KIB)
+        late_picks = early_words + [late_picks67[:, 0, :], late_picks67[:, 1, :]]
+        z_high = at("z_high_late", [P, 12, HALF], TAIL)[:, 0:GROUP, :]
         for t in range(2):
             pick_high(t, late_picks[t], HALF)
+        quant_z(0, 0, low_early_bf[:])
         quant_z(1, 0, high_early_bf)
         for t in range(2, GROUP):
             pick_high(t, late_picks[t], HALF)
@@ -320,8 +333,6 @@ def tile_list_phrase_tree_forget_kernel(
         quant_z(0, HALF, low_late_bf[:])
 
         order = [banks[b] for b in (7, 0, 1, 2, 3, 4, 5, 6)]
-        y01 = sb("y01", [P, 2 * PH], F32)
-        y_sb = [y01[:, 0:PH], y01[:, PH : 2 * PH]] + [sb("y%d" % n, [P, PH], F32)[:] for n in range(2, OUT_TILES)]
 
         def product_mm(content_side, n0, m0, a, bank, opens):
             for d in range(2):
@@ -347,11 +358,13 @@ def tile_list_phrase_tree_forget_kernel(
         def two(ap):
             return ap.rearrange("p (d m) -> p d m", d=2)
 
-        def gate_act(n0, m0, bank):
-            nc.scalar.activation(gate[:, n0 : n0 + 2, m0 : m0 + HALF], two(bank[:]), ACT.Sigmoid)
+        def gate_act(n0, m0, bank, dst=None):
+            dst = gate[:, n0 : n0 + 2, m0 : m0 + HALF] if dst is None else dst
+            nc.scalar.activation(dst, two(bank[:]), ACT.Sigmoid)
 
-        def content_act(n0, m0, bank):
-            nc.scalar.activation(content[:, n0 : n0 + 2, m0 : m0 + HALF], two(bank[:]), ACT.Tanh)
+        def content_act(n0, m0, bank, dst=None):
+            dst = content[:, n0 : n0 + 2, m0 : m0 + HALF] if dst is None else dst
+            nc.scalar.activation(dst, two(bank[:]), ACT.Tanh)
 
         def gated_mem(engine, dst, n0, m0):
             cols = slice(m0, m0 + HALF)
@@ -376,16 +389,24 @@ def tile_list_phrase_tree_forget_kernel(
         for side in range(2):
             product_mm(side, 0, HALF, 0, order[6 + side], True)
 
-        for j in range(3):
+        for j in range(2):
             gate_act(2 * j, 0, order[2 * j])
             content_act(2 * j, 0, order[2 * j + 1])
         high_late_bf = sb("high_late_bf", [P, GROUP * HALF], BF16)
-        weave(nc.vector.tensor_copy, high_late_bf[:], z_high)
+        weave(nc.scalar.copy, high_late_bf[:], z_high)
+        y01 = at("y01", [P, 2 * PH], TAIL)
+        y_sb = [y01[:, 0:PH], y01[:, PH : 2 * PH]]
+        y_sb.extend(at("y%d" % n, [P, PH], TAIL + 2 * n * KIB)[:] for n in (2, 3))
+        y_sb.extend(sb("y%d" % n, [P, PH], F32)[:] for n in (4, 5))
+        gate45 = at("gate45", [P, 2, HALF], TAIL + 8 * KIB)[:]
+        content45 = at("content45", [P, 2, HALF], TAIL + 10 * KIB)[:]
+        gate_act(4, 0, order[4], gate45)
+        content_act(4, 0, order[5], content45)
+        early = [in_place(n0, 0) for n0 in (0, 2)]
         quant_z(1, HALF, high_late_bf[:])
-        early0 = gated_mem(nc.vector, z_high[:, 0:2, :], 0, 0)
-        in_place(4, 0)
-        state(nc.vector, early0, 0, 0)
-        state(nc.vector, in_place(2, 0), 2, 0)
+        state(nc.vector, early[0], 0, 0)
+        state(nc.vector, early[1], 2, 0)
+        nc.vector.tensor_tensor(gate45, gate45, mem_sb[:, 4:6, 0:HALF], ALU.mult)
 
         late_banks = ((6, 7), (0, 1), (2, 3))
         product_mm(0, 0, HALF, 1, order[6], False)
@@ -401,9 +422,9 @@ def tile_list_phrase_tree_forget_kernel(
 
         def turned_sum(n, bank, turned):
             for m in range(0, HALF, P):
-                for first, src in ((True, content), (False, gate)):
+                for first, src in ((True, content45), (False, gate45)):
                     nc.tensor.matmul(
-                        bank[:, m : m + P], src[:, n, m : m + P], identity[:],
+                        bank[:, m : m + P], src[:, n - 4, m : m + P], identity[:],
                         start=first, stop=not first, is_transpose=True)
             nc.scalar.copy(turned, bank[:, 0:HALF])
 

@@ -30,7 +30,7 @@ LAST_TOKENS = 768
 HELD = 64
 KIB = 1024
 TAIL = 6 * KIB
-WARM_PASSES = 3
+WARM_PASSES = (3, 2)
 OPEN_EARLY = 6
 
 
@@ -304,17 +304,22 @@ def tile_list_phrase_tree_forget_kernel(
         round_turned(early_words, 0)
         turn_words(early_words, banks[5])
         low_early_bf = fetch_words("low_early_bf", banks[5])
-        for r in range(WARM_PASSES):
-            codes, scales, c0 = weights[0, 0]
-            nc.tensor.matmul_mx(
-                out=banks[2][:], lhsT=codes[:].bitcast(FP8X4), lhsT_scale=scales[:],
-                rhs=v_w[0][:, 0:BANK].bitcast(FP8X4), rhs_scale=v_sc[:, 0:BANK],
-                start=(r == 0), stop=(r == WARM_PASSES - 1),
-            )
+
+        def warm_up(bank, passes):
+            codes, scales = weights[0, 0][0:2]
+            for r in range(passes):
+                nc.tensor.matmul_mx(
+                    out=bank[:], lhsT=codes[:].bitcast(FP8X4), lhsT_scale=scales[:],
+                    rhs=v_w[0][:, 0:BANK].bitcast(FP8X4), rhs_scale=v_sc[:, 0:BANK],
+                    start=(r == 0), stop=(r == passes - 1),
+                )
+
+        warm_up(banks[2], WARM_PASSES[0])
         turn_low(HALF)
         late_words = [sb("late_words%d" % b, [P, HALF], F32)[:] for b in range(2)]
         round_turned(late_words, HALF)
         turn_words(late_words, banks[6])
+        warm_up(banks[4], WARM_PASSES[1])
         high_early_bf = sb("high_early_bf", [P, GROUP * HALF], BF16, tag="high_raw")[:]
         weave(nc.scalar.copy, high_early_bf, z_high_early)
         low_late_bf = fetch_words("low_late_bf", banks[6])
@@ -392,6 +397,9 @@ def tile_list_phrase_tree_forget_kernel(
         for j in range(2):
             gate_act(2 * j, 0, order[2 * j])
             content_act(2 * j, 0, order[2 * j + 1])
+        late_banks = ((6, 7), (0, 1), (2, 3))
+        for side in range(2):
+            product_mm(side, 2, HALF, 0, order[late_banks[1][side]], True)
         high_late_bf = sb("high_late_bf", [P, GROUP * HALF], BF16)
         weave(nc.scalar.copy, high_late_bf[:], z_high)
         y01 = at("y01", [P, 2 * PH], TAIL)
@@ -408,17 +416,12 @@ def tile_list_phrase_tree_forget_kernel(
         state(nc.vector, early[1], 2, 0)
         nc.vector.tensor_tensor(gate45, gate45, mem_sb[:, 4:6, 0:HALF], ALU.mult)
 
-        late_banks = ((6, 7), (0, 1), (2, 3))
-        product_mm(0, 0, HALF, 1, order[6], False)
-        for a in range(PASSES):
-            product_mm(0, 2, HALF, a, order[0], a == 0)
-        product_mm(1, 0, HALF, 1, order[7], False)
-        for j in (1, 2):
+        for side in range(2):
+            for j in range(2):
+                product_mm(side, 2 * j, HALF, 1, order[late_banks[j][side]], False)
+        for side in range(2):
             for a in range(PASSES):
-                product_mm(1, 2 * j, HALF, a, order[late_banks[j][1]], a == 0)
-            if j == 1:
-                for a in range(PASSES):
-                    product_mm(0, 4, HALF, a, order[2], a == 0)
+                product_mm(side, 4, HALF, a, order[late_banks[2][side]], a == 0)
 
         def turned_sum(n, bank, turned):
             for m in range(0, HALF, P):

@@ -64,13 +64,6 @@ def tile_list_phrase_tree_forget_kernel(
         nc.scalar.activation(warm[:, 1:2], warm[:, 0:1], ACT.Sigmoid)
 
         offs_sb = load_list("offs_sb", offs, S)
-        pos1_sb = load_list("pos1_sb", pos1, PH)
-        pos2_sb = load_list("pos2_sb", pos2, PH)
-        for q in range(4):
-            nc.sync.dma_start(
-                tab_sc[32 * q : 32 * q + 8, :].bitcast(I32),
-                tab_scales[:, 4 * q : 4 * q + 4, :].bitcast(I32),
-            )
         tab_w = [sb("tab_w%d" % a, [P, T], U32) for a in range(PASSES)]
 
         def load_tab(a):
@@ -87,9 +80,16 @@ def tile_list_phrase_tree_forget_kernel(
             nc.sync.dma_start(tile[:], w1[PASS_K * a : PASS_K * (a + 1), c0:c1].rearrange("(p j) c -> p j c", j=4))
             return tile
 
-        load_tab(0)
         raw0 = [load_w1("raw0_0", 0, 0, P)]
+        for q in range(4):
+            nc.sync.dma_start(
+                tab_sc[32 * q : 32 * q + 8, :].bitcast(I32),
+                tab_scales[:, 4 * q : 4 * q + 4, :].bitcast(I32),
+            )
+        load_tab(0)
         load_tab(1)
+        pos1_sb = load_list("pos1_sb", pos1, PH)
+        pos2_sb = load_list("pos2_sb", pos2, PH)
         raw0.append(load_w1("raw0_1", 1, 0, P))
         raw1 = [load_w1("raw1_%d" % a, a, P, 2 * P) for a in range(PASSES)]
         raw23 = [load_w1("raw23_0", 0, 2 * P, 4 * P), load_w1("raw23_1", 1, 2 * P, 4 * P, offset=0)]
@@ -172,16 +172,16 @@ def tile_list_phrase_tree_forget_kernel(
                     nc.tensor.transpose(
                         banks[turn_banks[m // P]][:, c * P : (c + 1) * P], z_low[c][:, m : m + P], identity[:])
 
-        nc.vector.tensor_copy(v_sc[:], tab_sc[:].indirect(offs_sb[:]))
-        nc.vector.tensor_copy(v_w[0][:], tab_w[0][:].indirect(offs_sb[:]))
         bf00 = sb("bf00", [P, PASS_K], BF16)
         weave(nc.scalar.copy, bf00[:], raw0[0][:])
         weights[0, 0] = quantize("w00", bf00[:], P) + (0,)
+        nc.vector.tensor_copy(v_sc[:], tab_sc[:].indirect(offs_sb[:]))
+        nc.vector.tensor_copy(v_w[0][:], tab_w[0][:].indirect(offs_sb[:]))
 
         def gather_pass1(dst, t0, t1):
             nc.vector.tensor_copy(dst, tab_w[1][:].indirect(offs_sb[:, t0 // LIST_ROWS : t1 // LIST_ROWS]))
 
-        v_w.append(sb("v_w1", [P, BANK], U32, tag="raw0_0"))
+        v_w.append(sb("v_w1", [P, BANK], U32))
         gather_pass1(v_w[1][:], 0, BANK)
         bf0 = sb("bf0", [P, PASS_K], BF16)
         weave(nc.scalar.copy, bf0[:], raw0[1][:])
@@ -474,5 +474,8 @@ def tile_list_phrase_tree_forget_kernel(
             pick_y(minus[n], n, pos4_sb)
         for n in range(2, OUT_TILES):
             result = (plus01, minus01)[n // 4][:, n % 2, :]
-            nc.vector.tensor_tensor(result, y_sb[n].indirect(pos3_sb[:]), minus[n], ALU.subtract)
-            nc.sync.dma_start(out[n * P : (n + 1) * P, :], result)
+            cuts = (0, CL) if n < OUT_TILES - 1 else (0, P, CL)
+            for c0, c1 in zip(cuts, cuts[1:]):
+                entries = pos3_sb[:, c0 // LIST_ROWS : c1 // LIST_ROWS]
+                nc.vector.tensor_tensor(result[:, c0:c1], y_sb[n].indirect(entries), minus[n][:, c0:c1], ALU.subtract)
+                nc.sync.dma_start(out[n * P : (n + 1) * P, c0:c1], result[:, c0:c1])

@@ -81,11 +81,17 @@ def tile_list_phrase_tree_forget_kernel(
             return tile
 
         raw0 = [load_w1("raw0_0", 0, 0, P)]
-        for q in range(4):
+        for q in range(2):
             nc.sync.dma_start(
                 tab_sc[32 * q : 32 * q + 8, :].bitcast(I32),
                 tab_scales[:, 4 * q : 4 * q + 4, :].bitcast(I32),
             )
+        for q in range(2, 4):
+            for a in range(PASSES):
+                nc.sync.dma_start(
+                    tab_sc[32 * q + 4 * a : 32 * q + 4 * a + 4, :].bitcast(I32),
+                    tab_scales[a, 4 * q : 4 * q + 4, :].bitcast(I32),
+                )
         load_tab(0)
         load_tab(1)
         pos1_sb = load_list("pos1_sb", pos1, PH)

@@ -124,8 +124,8 @@ def tile_list_phrase_tree_forget_kernel(
         pos3_sb = load_list("pos3_sb", pos3, CL)
         pos4_sb = load_list("pos4_sb", pos4, CL)
 
-        def quantize(name, rounded, words):
-            codes = sb(name + "_q", [P, words], U32)
+        def quantize(name, rounded, words, tag=None):
+            codes = sb(name + "_q", [P, words], U32, tag=tag)
             scales = sb(name + "_sc", [P, words], U8)
             nc.vector.quantize_mx(out=codes[:].bitcast(FP8X4), scales=scales[:], in_=rounded)
             return codes, scales
@@ -180,9 +180,9 @@ def tile_list_phrase_tree_forget_kernel(
 
         bf00 = sb("bf00", [P, PASS_K], BF16)
         weave(nc.scalar.copy, bf00[:], raw0[0][:])
-        weights[0, 0] = quantize("w00", bf00[:], P) + (0,)
         nc.vector.tensor_copy(v_sc[:], tab_sc[:].indirect(offs_sb[:]))
         nc.vector.tensor_copy(v_w[0][:], tab_w[0][:].indirect(offs_sb[:]))
+        weights[0, 0] = quantize("w00", bf00[:], P, tag="tab_sc") + (0,)
 
         def gather_pass1(dst, t0, t1):
             nc.vector.tensor_copy(dst, tab_w[1][:].indirect(offs_sb[:, t0 // LIST_ROWS : t1 // LIST_ROWS]))

from contextlib import ExitStack

import concourse.mybir as mybir
from concourse.masks import make_identity

K, T, S, H, PH, N, CL = 1024, 2048, 1024, 1024, 512, 768, 256
FLOPS = 2 * K * H * S + 2 * 2 * H * N * PH

F32 = mybir.dt.float32
BF16 = mybir.dt.bfloat16
I32 = mybir.dt.int32
U32 = mybir.dt.uint32
U16 = mybir.dt.uint16
U8 = mybir.dt.uint8
FP8X4 = mybir.dt.float8_e4m3fn_x4
FP4X4 = mybir.dt.float4_e2m1fn_x4
ACT = mybir.ActivationFunctionType
ALU = mybir.AluOpType

P = 128
BANK = 512
PASS_K = 512
PASSES = K // PASS_K
GROUP = 4
ROW_TILES = H // P
OUT_TILES = N // P
HALF = PH // 2
LIST_ROWS = 16
LAST_TOKENS = 768
HELD = 64
KIB = 1024
TAIL = 6 * KIB
WARM_PASSES = (3, 2)
OPEN_EARLY = 6


def tile_list_phrase_tree_forget_kernel(
    tc, tab_words, tab_scales, offs, w1, pos1, pos2, wc_words, wc_scales,
    wf_words, wf_scales, mem, pos3, pos4, out,
):
    nc = tc.nc
    with ExitStack() as ctx:
        keep = ctx.enter_context(tc.tile_pool(name="keep", bufs=1))
        placed = ctx.enter_context(tc.tile_pool(name="placed", bufs=1))
        psum = ctx.enter_context(tc.psum_pool(name="psum", bufs=1))

        def sb(name, shape, dtype, tag=None):
            return keep.tile(shape, dtype, name=name, tag=tag or name, align_bytes=64)

        banks = [psum.tile([P, BANK], F32, name="bank%d" % b) for b in range(8)]

        def load_list(name, src, entries):
            tile = sb(name, [P, entries // LIST_ROWS], U16)
            nc.sync.dma_start(tile[:], src)
            return tile

        tab_sc = sb("tab_sc", [P, T], U8)
        nc.gpsimd.memset(tab_sc[:].bitcast(I32), 0)
        identity = sb("identity", [P, P], F32)
        make_identity(nc, identity[:])

        warm = sb("warm", [P, 2], F32)
        nc.vector.memset(warm[:, 0:1], 0.0)
        nc.scalar.activation(warm[:, 1:2], warm[:, 0:1], ACT.Sigmoid)

        offs_sb = load_list("offs_sb", offs, S)
        tab_w = [sb("tab_w%d" % a, [P, T], U32) for a in range(PASSES)]

        def load_tab(a):
            nc.sync.dma_start(
                tab_w[a][:].bitcast(I32),
                tab_words[a].rearrange("p t i -> p (t i)").bitcast(I32),
            )

        def at(name, shape, offset):
            return placed.tile(shape, F32, name=name, align_bytes=64, offset=offset)

        def load_w1(name, a, c0, c1, offset=None):
            tile = sb(name, [P, 4, c1 - c0], F32) if offset is None else at(name, [P, 4, c1 - c0], offset)
            nc.sync.dma_start(tile[:], w1[PASS_K * a : PASS_K * (a + 1), c0:c1].rearrange("(p j) c -> p j c", j=4))
            return tile

        raw0 = [load_w1("raw0_0", 0, 0, P)]
        for q in range(2):
            nc.sync.dma_start(
                tab_sc[32 * q : 32 * q + 8, :].bitcast(I32),
                tab_scales[:, 4 * q : 4 * q + 4, :].bitcast(I32),
            )
        for q in range(2, 4):
            for a in range(PASSES):
                nc.sync.dma_start(
                    tab_sc[32 * q + 4 * a : 32 * q + 4 * a + 4, :].bitcast(I32),
                    tab_scales[a, 4 * q : 4 * q + 4, :].bitcast(I32),
                )
        load_tab(0)
        load_tab(1)
        pos1_sb = load_list("pos1_sb", pos1, PH)
        pos2_sb = load_list("pos2_sb", pos2, PH)
        raw0.append(load_w1("raw0_1", 1, 0, P))
        raw1 = [load_w1("raw1_%d" % a, a, P, 2 * P) for a in range(PASSES)]
        raw23 = [load_w1("raw23_0", 0, 2 * P, 4 * P), load_w1("raw23_1", 1, 2 * P, 4 * P, offset=0)]
        high_raw = sb("high_raw", [P, PASSES, 4, PASS_K], F32)
        for a in range(PASSES):
            rows = slice(PASS_K * a, PASS_K * (a + 1))
            nc.sync.dma_start(high_raw[:, a], w1[rows, PASS_K:H].rearrange("(p j) c -> p j c", j=4))

        wcf_sc = sb("wcf_sc", [P, PASSES, N], U8)
        nc.gpsimd.memset(wcf_sc[:].rearrange("p a c -> p (a c)").bitcast(I32), 0)
        for q in range(4):
            nc.sync.dma_start(
                wcf_sc[32 * q : 32 * q + 4, :, :].bitcast(I32),
                wc_scales[:, 4 * q : 4 * q + 4, :].rearrange("a r c -> r a c").bitcast(I32),
            )
            nc.sync.dma_start(
                wcf_sc[32 * q + 4 : 32 * q + 8, :, :].bitcast(I32),
                wf_scales[:, 4 * q : 4 * q + 4, :].rearrange("a r c -> r a c").bitcast(I32),
            )
        wc_sb = sb("wc_sb", [P, PASSES, 2 * N], U8)
        nc.sync.dma_start(wc_sb[:].bitcast(I32), wc_words.rearrange("a p c -> p a c").bitcast(I32))
        wf_sb = sb("wf_sb", [P, PASSES, N], U32)
        nc.sync.dma_start(wf_sb[:].bitcast(I32), wf_words.rearrange("a p c i -> p a (c i)").bitcast(I32))
        mem_sb = sb("mem_sb", [P, OUT_TILES, PH], F32)
        nc.sync.dma_start(mem_sb[:], mem.rearrange("(n p) m -> p n m", p=P))
        pos3_sb = load_list("pos3_sb", pos3, CL)
        pos4_sb = load_list("pos4_sb", pos4, CL)

        def quantize(name, rounded, words, tag=None):
            codes = sb(name + "_q", [P, words], U32, tag=tag)
            scales = sb(name + "_sc", [P, words], U8)
            nc.vector.quantize_mx(out=codes[:].bitcast(FP8X4), scales=scales[:], in_=rounded)
            return codes, scales

        def weave(copy, dst, src):
            copy(dst.rearrange("p (c i j) -> p c j i", i=2, j=4), src.rearrange("p j (c i) -> p c j i", i=2))

        v_sc = sb("v_sc", [P, S], U8)
        v_w = [sb("v_w0", [P, S], U32)]
        weights = {}
        h_sb = {}

        def stage1_pass(i, a, bank, t0, t1):
            codes, scales, c0 = weights[i, a]
            words = v_last[:, t0 - BANK : t1 - BANK] if a == 1 and t0 >= BANK else v_w[a][:, t0:t1]
            nc.tensor.matmul_mx(
                out=bank[:, 0 : t1 - t0],
                lhsT=codes[:, c0 : c0 + P].bitcast(FP8X4),
                lhsT_scale=scales[:, c0 : c0 + P],
                rhs=words.bitcast(FP8X4),
                rhs_scale=v_sc[4 * a : P, t0:t1],
                start=(a == 0),
                stop=(a == PASSES - 1),
            )

        def stage1(i, pieces, tile=None):
            h_sb[i] = sb("h%d" % i, [P, S], F32) if tile is None else tile
            for b, t0, t1, copy in pieces:
                for a in range(PASSES):
                    stage1_pass(i, a, banks[b], t0, t1)
                copy(h_sb[i][:, t0:t1], banks[b][:, 0 : t1 - t0])

        def two_banks(b0, b1):
            return [(b0, 0, BANK, nc.scalar.copy), (b1, BANK, S, nc.scalar.copy)]

        def half_of(list_sb, m0):
            return list_sb[:, m0 // LIST_ROWS : (m0 + HALF) // LIST_ROWS]

        def pick_whole(i, dst):
            nc.vector.tensor_copy(dst, h_sb[i][:].indirect(pos1_sb[:]))
            return dst

        def add_whole(i, tile):
            z_low[i] = tile
            nc.vector.tensor_tensor(tile, h_sb[i][:].indirect(pos2_sb[:]), picks[i], ALU.add)

        def turn_low(m0):
            for m in range(m0, m0 + HALF, P):
                for c in range(GROUP):
                    nc.tensor.transpose(
                        banks[turn_banks[m // P]][:, c * P : (c + 1) * P], z_low[c][:, m : m + P], identity[:])

        bf00 = sb("bf00", [P, PASS_K], BF16)
        weave(nc.scalar.copy, bf00[:], raw0[0][:])
        nc.vector.tensor_copy(v_sc[:], tab_sc[:].indirect(offs_sb[:]))
        nc.vector.tensor_copy(v_w[0][:], tab_w[0][:].indirect(offs_sb[:]))
        weights[0, 0] = quantize("w00", bf00[:], P, tag="tab_sc") + (0,)

        def gather_pass1(dst, t0, t1):
            nc.vector.tensor_copy(dst, tab_w[1][:].indirect(offs_sb[:, t0 // LIST_ROWS : t1 // LIST_ROWS]))

        v_w.append(sb("v_w1", [P, BANK], U32))
        gather_pass1(v_w[1][:], 0, BANK)
        bf0 = sb("bf0", [P, PASS_K], BF16)
        weave(nc.scalar.copy, bf0[:], raw0[1][:])
        weights[0, 1] = quantize("w0", bf0[:], P) + (0,)
        v_last = sb("v_last", [P, BANK], U32, tag="raw0_1")
        gather_pass1(v_last[:, 0 : LAST_TOKENS - BANK], BANK, LAST_TOKENS)
        gather_pass1(v_last[:, LAST_TOKENS - BANK : BANK], LAST_TOKENS, S)
        bf1 = sb("bf1", [P, PASSES, PASS_K], BF16)
        for a in range(PASSES):
            weave(nc.scalar.copy, bf1[:, a, :], raw1[a][:])
        bf23 = [sb("bf23_0", [P, 2 * PASS_K], BF16, tag="bf0")]
        weave(nc.vector.tensor_copy, bf23[0][:], raw23[0][:])
        codes, scales = quantize("w1", bf1[:].rearrange("p a c -> p (a c)"), PASSES * P)
        for a in range(PASSES):
            weights[1, a] = (codes, scales, a * P)

        stage1(0, [(0, 0, BANK, nc.scalar.copy), (1, BANK, LAST_TOKENS, nc.scalar.copy),
                   (2, LAST_TOKENS, S, nc.scalar.copy)], sb("h0", [P, S], F32, tag="raw1_1"))

        def quantize23(a):
            codes, scales = quantize("w23_%d" % a, bf23[a][:], 2 * P)
            for i in (2, 3):
                weights[i, a] = (codes, scales, (i - 2) * P)

        def prepare_high(name, u, a0, a1, tag, tiles=2, spare=0):
            tile = sb(name + "_bf", [P, spare + (a1 - a0) * 2 * PASS_K], BF16, tag=tag)
            rounded = tile[:, spare:]
            nc.scalar.copy(
                rounded.rearrange("p (a t m j) -> p a m j t", a=a1 - a0, t=2, j=4),
                high_raw[:].rearrange("p a j (m t) -> p a m j t", t=4)[:, a0:a1, :, :, 2 * u : 2 * u + 2],
            )
            order = [(GROUP + 2 * u + t, a) for a in range(a0, a1) for t in range(2)]
            for s0 in range(0, len(order), tiles):
                piece = rounded[:, s0 * PASS_K : (s0 + tiles) * PASS_K]
                codes, scales = quantize("%s_%d" % (name, s0), piece, tiles * P)
                for s in range(tiles):
                    weights[order[s0 + s]] = (codes, scales, s * P)
            return tile

        turn_banks = (1, 2, 3, 4)
        picks, z_low = {}, {}
        quantize23(0)
        picks[0] = pick_whole(0, sb("picks0", [P, PH], F32)[:])
        bf23.append(sb("bf23_1", [P, 2 * PASS_K], BF16, tag="w0_q"))
        weave(nc.scalar.copy, bf23[1][:], raw23[1][:])
        quantize23(1)
        add_whole(0, at("z_low0", [P, PH], 0)[:])
        stage1(1, two_banks(0, 1), at("h1", [P, S], 4 * PH))
        picks[1] = sb("picks1", [P, PH], F32)
        z_low[1] = sb("z_low1", [P, PH], F32)
        for m0 in (0, HALF):
            nc.vector.tensor_copy(picks[1][:, m0 : m0 + HALF], h_sb[1][:].indirect(half_of(pos1_sb, m0)))
        for m0 in (0, HALF):
            cols = slice(m0, m0 + HALF)
            nc.vector.tensor_tensor(
                z_low[1][:, cols], h_sb[1][:].indirect(half_of(pos2_sb, m0)), picks[1][:, cols], ALU.add)
        prepare_high("w45_0", 0, 0, 1, "w1_q")
        stage1(2, two_banks(3, 4))
        picks[2] = pick_whole(2, sb("picks2", [P, PH], F32)[:])
        stage1(3, two_banks(5, 6))
        picks[3] = pick_whole(3, sb("picks3", [P, PH], F32)[:])
        rounded45 = prepare_high("w45_1", 0, 1, 2, "w23_1_q", tiles=1, spare=PASS_K)
        add_whole(2, rounded45[:].bitcast(F32)[:, 0:PH])
        prepare_high("w67", 1, 0, 2, "w23_1_sc", tiles=4)
        add_whole(3, sb("z_low3", [P, PH], F32, tag="high_raw")[:])
        for i, (b0, b1, b2, b3) in ((4, (1, 2, 3, 4)), (6, (7, 0, 5, 6))):
            h_sb[i] = sb("h%d" % i, [P, S], F32)
            for b, t0 in ((b0, 0), (b1, BANK)):
                for a in range(PASSES):
                    stage1_pass(i, a, banks[b], t0, t0 + BANK)
            nc.scalar.copy(h_sb[i][:, 0:BANK], banks[b0][:])
            nc.scalar.copy(h_sb[i][:, BANK : S - HELD], banks[b1][:, 0 : BANK - HELD])
            stage1(i + 1, two_banks(b2, b3))
            nc.scalar.copy(h_sb[i][:, S - HELD : S], banks[b1][:, BANK - HELD : BANK])
        turn_low(0)

        z_high_early = at("z_high_early", [P, GROUP, HALF], TAIL + 10 * KIB)[:]
        early_picks = sb("early_picks", [P, GROUP, HALF], F32)
        rows = sb("rows", [P, 2, HALF], F32)

        def pick_high(t, dst, m0):
            nc.vector.tensor_copy(dst, h_sb[GROUP + t][:].indirect(half_of(pos1_sb, m0)))

        def add_high(t, dst, first, m0):
            nc.vector.tensor_tensor(dst, h_sb[GROUP + t][:].indirect(half_of(pos2_sb, m0)), first, ALU.add)

        for pair in ((1, 0), (3, 2)):
            for t in pair:
                pick_high(t, early_picks[:, t, :], 0)
            for t in pair:
                add_high(t, z_high_early[:, t, :], early_picks[:, t, :], 0)

        def round_turned(words, m0):
            for b in range(2):
                dst = words[b].bitcast(BF16).rearrange("m (u p e) -> m u p e", u=2, e=2)
                src = banks[turn_banks[m0 // P + b]][:].rearrange("m (p u e) -> m u p e", u=2, e=2)
                nc.scalar.copy(dst, src)

        def turn_words(words, bank):
            for w in range(4):
                nc.tensor.transpose(
                    bank[:, w * P : (w + 1) * P], words[w // 2][:, (w % 2) * P : (w % 2 + 1) * P], identity[:])

        def fetch_words(name, bank):
            rounded = sb(name, [P, GROUP * HALF], BF16)
            nc.scalar.copy(
                rounded[:].bitcast(F32).rearrange("p (b m u) -> p b m u", b=2, u=2),
                bank[:].rearrange("p (b u m) -> p b m u", b=2, u=2),
            )
            return rounded

        z_q = [sb("z_q%d" % a, [P, PH], U32) for a in range(PASSES)]
        z_sc = [sb("z_sc%d" % a, [P, PH], U8) for a in range(PASSES)]

        def quant_z(a, m0, src):
            nc.vector.quantize_mx(
                out=z_q[a][:, m0 : m0 + HALF].bitcast(FP8X4), scales=z_sc[a][:, m0 : m0 + HALF], in_=src)

        early_words = [rows[:, 0, :], rows[:, 1, :]]
        round_turned(early_words, 0)
        turn_words(early_words, banks[5])
        low_early_bf = fetch_words("low_early_bf", banks[5])

        def warm_up(bank, passes):
            codes, scales = weights[0, 0][0:2]
            for r in range(passes):
                nc.tensor.matmul_mx(
                    out=bank[:], lhsT=codes[:].bitcast(FP8X4), lhsT_scale=scales[:],
                    rhs=v_w[0][:, 0:BANK].bitcast(FP8X4), rhs_scale=v_sc[:, 0:BANK],
                    start=(r == 0), stop=(r == passes - 1),
                )

        warm_up(banks[2], WARM_PASSES[0])
        turn_low(HALF)
        late_words = [sb("late_words%d" % b, [P, HALF], F32)[:] for b in range(2)]
        round_turned(late_words, HALF)
        turn_words(late_words, banks[6])
        warm_up(banks[4], WARM_PASSES[1])
        high_early_bf = sb("high_early_bf", [P, GROUP * HALF], BF16, tag="high_raw")[:]
        weave(nc.scalar.copy, high_early_bf, z_high_early)
        low_late_bf = fetch_words("low_late_bf", banks[6])

        late_picks67 = at("late_picks67", [P, 2, HALF], TAIL + 12 * KIB)
        late_picks = early_words + [late_picks67[:, 0, :], late_picks67[:, 1, :]]
        z_high = at("z_high_late", [P, 12, HALF], TAIL)[:, 0:GROUP, :]
        for t in range(2):
            pick_high(t, late_picks[t], HALF)
        quant_z(0, 0, low_early_bf[:])
        quant_z(1, 0, high_early_bf)
        for t in range(2, GROUP):
            pick_high(t, late_picks[t], HALF)
        for t in range(GROUP):
            add_high(t, z_high[:, t, :], late_picks[t], HALF)
        quant_z(0, HALF, low_late_bf[:])

        order = [banks[b] for b in (7, 0, 1, 2, 3, 4, 5, 6)]

        def product_mm(content_side, n0, m0, a, bank, opens):
            for d in range(2):
                n = n0 + d
                if content_side:
                    codes = wc_sb[:, a, 2 * n * P : 2 * (n + 1) * P].bitcast(FP4X4)
                    scales = wcf_sc[:, a, n * P : (n + 1) * P]
                else:
                    codes = wf_sb[:, a, n * P : (n + 1) * P].bitcast(FP8X4)
                    scales = wcf_sc[4:P, a, n * P : (n + 1) * P]
                nc.tensor.matmul_mx(
                    out=bank[:, d * HALF : (d + 1) * HALF],
                    lhsT=codes,
                    lhsT_scale=scales,
                    rhs=z_q[a][:, m0 : m0 + HALF].bitcast(FP8X4),
                    rhs_scale=z_sc[a][:, m0 : m0 + HALF],
                    start=(opens and d == 0), stop=(not opens and d == 1),
                )

        content = sb("content", [P, OUT_TILES, PH], F32, tag="tab_w1")
        gate = sb("gate", [P, OUT_TILES, PH], F32, tag="tab_w0")

        def two(ap):
            return ap.rearrange("p (d m) -> p d m", d=2)

        def gate_act(n0, m0, bank, dst=None):
            dst = gate[:, n0 : n0 + 2, m0 : m0 + HALF] if dst is None else dst
            nc.scalar.activation(dst, two(bank[:]), ACT.Sigmoid)

        def content_act(n0, m0, bank, dst=None):
            dst = content[:, n0 : n0 + 2, m0 : m0 + HALF] if dst is None else dst
            nc.scalar.activation(dst, two(bank[:]), ACT.Tanh)

        def gated_mem(engine, dst, n0, m0):
            cols = slice(m0, m0 + HALF)
            engine.tensor_tensor(dst, gate[:, n0 : n0 + 2, cols], mem_sb[:, n0 : n0 + 2, cols], ALU.mult)
            return dst

        def in_place(n0, m0):
            return gated_mem(nc.vector, gate[:, n0 : n0 + 2, m0 : m0 + HALF], n0, m0)

        def state(engine, gated, n0, m0):
            cols = slice(m0, m0 + HALF)
            if n0 == 0:
                engine.tensor_tensor(two(y01[:])[:, :, cols], gated, content[:, 0:2, cols], ALU.add)
            else:
                for d in range(2):
                    engine.tensor_tensor(y_sb[n0 + d][:, cols], gated[:, d, :], content[:, n0 + d, cols], ALU.add)

        for b in range(OUT_TILES):
            opening = 0 if b < OPEN_EARLY else 1
            product_mm(b % 2, b - b % 2, 0, opening, order[b], True)
            product_mm(b % 2, b - b % 2, 0, 1 - opening, order[b], False)
        for side in range(2):
            product_mm(side, 0, HALF, 0, order[6 + side], True)

        for j in range(2):
            gate_act(2 * j, 0, order[2 * j])
            content_act(2 * j, 0, order[2 * j + 1])
        late_banks = ((6, 7), (0, 1), (2, 3))
        for side in range(2):
            product_mm(side, 2, HALF, 0, order[late_banks[1][side]], True)
        high_late_bf = sb("high_late_bf", [P, GROUP * HALF], BF16)
        weave(nc.scalar.copy, high_late_bf[:], z_high)
        y01 = at("y01", [P, 2 * PH], TAIL)
        y_sb = [y01[:, 0:PH], y01[:, PH : 2 * PH]]
        y_sb.extend(at("y%d" % n, [P, PH], TAIL + 2 * n * KIB)[:] for n in (2, 3))
        y_sb.extend(sb("y%d" % n, [P, PH], F32)[:] for n in (4, 5))
        gate45 = at("gate45", [P, 2, HALF], TAIL + 8 * KIB)[:]
        content45 = at("content45", [P, 2, HALF], TAIL + 10 * KIB)[:]
        gate_act(4, 0, order[4], gate45)
        content_act(4, 0, order[5], content45)
        early = [in_place(n0, 0) for n0 in (0, 2)]
        quant_z(1, HALF, high_late_bf[:])
        state(nc.vector, early[0], 0, 0)
        state(nc.vector, early[1], 2, 0)
        nc.vector.tensor_tensor(gate45, gate45, mem_sb[:, 4:6, 0:HALF], ALU.mult)

        for side in range(2):
            for j in range(2):
                product_mm(side, 2 * j, HALF, 1, order[late_banks[j][side]], False)
        for side in range(2):
            for a in range(PASSES):
                product_mm(side, 4, HALF, a, order[late_banks[2][side]], a == 0)

        def turned_sum(n, bank, turned):
            for m in range(0, HALF, P):
                for first, src in ((True, content45), (False, gate45)):
                    nc.tensor.matmul(
                        bank[:, m : m + P], src[:, n - 4, m : m + P], identity[:],
                        start=first, stop=not first, is_transpose=True)
            nc.scalar.copy(turned, bank[:, 0:HALF])

        def turn_back(n, turned, bank):
            for m in range(0, HALF, P):
                nc.tensor.transpose(bank[:, m : m + P], turned[:, m : m + P], identity[:])
            nc.scalar.copy(y_sb[n][:, 0:HALF], bank[:, 0:HALF])

        for act, side in ((gate_act, 0), (content_act, 1)):
            for j in range(2):
                act(2 * j, HALF, order[late_banks[j][side]])
        gate_act(4, HALF, order[2])
        content_act(4, HALF, order[3])
        last = sb("last", [P, 6 * HALF], F32)
        turned = {n: last[:, (n - 4) * HALF : (n - 3) * HALF] for n in (4, 5)}
        for n in (4, 5):
            turned_sum(n, order[n + 2], turned[n])
        for n in (4, 5):
            turn_back(n, turned[n], order[n])

        late0 = in_place(0, HALF)
        late2 = gated_mem(nc.vector, two(last[:, 15 * HALF // 4 : 23 * HALF // 4]), 2, HALF)
        state(nc.vector, late0, 0, HALF)
        state(nc.vector, late2, 2, HALF)
        late4 = gated_mem(nc.gpsimd, two(last[:, 2 * HALF : 4 * HALF]), 4, HALF)
        state(nc.gpsimd, late4, 4, HALF)
        plus01, minus01 = mem_sb[:, 2:4, HALF:PH], content[:, 2:4, HALF:PH]
        minus = {n: last[:, (n + 2) * CL : (n + 3) * CL] for n in (2, 3)}
        for n in (4, 5):
            minus[n] = sb("minus%d" % n, [P, CL], F32)[:]

        def pick_y(dst, n, list_sb):
            nc.vector.tensor_copy(dst, y_sb[n].indirect(list_sb[:]))

        for n in range(2):
            pick_y(plus01[:, n, :], n, pos3_sb)
        for n in range(2):
            pick_y(minus01[:, n, :], n, pos4_sb)
        result01 = two(last[:, 0 : 4 * HALF])[:, :, HALF : 2 * HALF]
        nc.gpsimd.tensor_tensor(result01, plus01, minus01, ALU.subtract)
        for n in range(2):
            nc.sync.dma_start(out[n * P : (n + 1) * P, :], result01[:, n, :])
        for n in range(2, OUT_TILES):
            pick_y(minus[n], n, pos4_sb)
        for n in range(2, OUT_TILES):
            result = (plus01, minus01)[n // 4][:, n % 2, :]
            cuts = (0, CL) if n < OUT_TILES - 1 else (0, P, CL)
            for c0, c1 in zip(cuts, cuts[1:]):
                entries = pos3_sb[:, c0 // LIST_ROWS : c1 // LIST_ROWS]
                nc.vector.tensor_tensor(result[:, c0:c1], y_sb[n].indirect(entries), minus[n][:, c0:c1], ALU.subtract)
                nc.sync.dma_start(out[n * P : (n + 1) * P, c0:c1], result[:, c0:c1])
